import numpy as np, ml_dtypes
CORES = [2,3,42,43,82,83,122,123]
N = 8
BF = ml_dtypes.bfloat16
def gentries(a):
    return np.ascontiguousarray(a.reshape(8, 16, -1).transpose(0, 2, 1)).reshape(8, -1)
def gtable(e):
    e = np.asarray(e); return np.ascontiguousarray(e.reshape(8, -1, 16).transpose(0, 2, 1)).reshape(128, -1).astype(np.int32)
C, F, P, CAP, L, T, RO = 3072, 2048, 256, 16, 4, 5, 2
def parts(rng):
    return dict(su=rng.integers(0, F, (N, 8, 16, C)), se=rng.integers(0, 2, (N, 8, 16, C)), pw=rng.integers(-7, 8, (N, 8, 16, F)), ot=rng.integers(0, C, (N, 8, L, F)),
                x=rng.integers(0, 16, (N, 8, 16, P)), dr=rng.integers(0, 16, (N, 8, 16, P)), c=rng.integers(0, C, (N, 8, P)),
                th=rng.choice(np.array([8, 9, 10, 10, 11, 11, 12, 17]), (N, 8, P)), hw=rng.integers(-7, 8, (N, 8, 16, 2)))
def pack(s):
    def b(a): return np.ascontiguousarray(a.reshape(N, 128, -1)).astype(np.float32).astype(BF)
    return {"sf": np.ascontiguousarray((2 * s["su"] + s["se"]).reshape(N, 128, C)).astype(np.int32), "pw": b(s["pw"]), "ot": np.ascontiguousarray(s["ot"].reshape(N, 8 * L, F)).astype(np.int32),
            "x0": b(s["x"]), "dr": b(s["dr"]), "c0": np.stack([gtable(a) for a in s["c"]]), "th": np.stack([gtable(a) for a in s["th"]]), "hw": b(s["hw"])}
def setup_inputs(rng):
    return pack(parts(rng))
def behind(rng, s, g):
    n = 2 * CAP; q = C // 4; e = np.arange(C)
    s["pw"][:, g] = rng.integers(1, 8, (N, 16, F)); s["x"][:, g] = rng.integers(1, 16, (N, 16, P))
    half = np.argsort(rng.random((N, 16, C)), axis=1) % 2
    s["se"][:, g] = np.where(e < q, 0, np.where(e < 2 * q, half, np.where(e < C - n, 1, 0)))
    s["ot"][:, g] = rng.integers(2 * q, C - n, (N, L, F)); s["c"][:, g] = rng.integers(0, q, (N, P)); s["th"][:, g] = rng.integers(0, 17, (N, P))
    o = np.stack([rng.permutation(P) for r in range(N)]); ask, late = o[:, :n], o[:, n:2 * n]
    for k in range(N):
        r = (k - 1) % N; y = s["x"][r, g][:, ask[r]]
        u = np.add.reduce(s["hw"][k, g][:, :, None] * y[:, None, :], axis=0); h = ((u[0] * u[1]) >> 5) & (F - 1)
        s["pw"][k, g][:, h] = np.array([1, -2] + [0] * 14)[:, None]
        s["ot"][k, g, 0, h] = rng.integers(q, 2 * q, n); s["ot"][k, g, 1, h] = rng.integers(0, q, n)
        free = np.setdiff1d(np.arange(F), h); mine = free[free % N == (k + 1) % N]
        s["su"][k, g] = rng.choice(free, (16, C)); b = rng.permutation(np.arange(2 * q, C - n))[:n]
        s["su"][k, g][:, b] = rng.choice(mine, (16, n))
        s["su"][k, g][:, C - n:] = h[rng.integers(0, n, (16, n))]; s["su"][k, g, 0, C - n:] = h
        s["c"][k, g, ask[k]] = b; s["th"][k, g, ask[k]] = rng.integers(1, 9, n)
        s["c"][k, g, late[k]] = C - n + np.arange(n); s["th"][k, g, late[k]] = rng.integers(9, 17, n)
    for k in range(N):
        s["x"][k, g, 0, late[k]] = 2 * T - 3; s["x"][k, g, 1, late[k]] = 0; s["dr"][k, g, 0, late[k]] = 0; s["dr"][k, g, 1, late[k]] = 1
def setup_inputs_room(rng):
    s = parts(rng); s["su"] = s["su"] - s["su"] % N + np.arange(C) % N
    for r in range(N):
        for g in range(0, 8, 2):
            n = rng.choice(np.array([0, 1, CAP - 1, CAP, CAP + 1, 2 * CAP]), N)
            if g == 0: n[(r + 1) % N] = CAP
            if g == 2: n[(r + 1) % N] = CAP + 1
            if g == 4: n[(r + 2) % N] = 2 * CAP
            k = np.full(P, -1); w = np.repeat(np.arange(N), n); k[:len(w)] = w; k = rng.permutation(k)
            s["c"][r, g] = rng.integers(0, C // N, P) * N + np.where(k < 0, rng.integers(0, N, P), k)
            s["th"][r, g] = np.where(k < 0, 0, 17)
    s["th"][:, 1] = 0
    s["th"][:, 3] = 17; s["pw"][:, 3] = rng.integers(1, 8, (N, 16, F)); s["se"][:, 3] = 0; s["x"][:, 3] = rng.integers(1, 16, (N, 16, P))
    for r in range(0, N, 2): s["c"][r, 3] = rng.integers(0, C // N, P) * N + (r + 1) % N
    s["pw"][:, 5] = rng.integers(5, 8, (N, 16, F)); s["se"][:, 5] = 1; s["x"][:, 5] = rng.integers(13, 16, (N, 16, P))
    s["th"][:, 5] = np.where(s["c"][:, 5] % N == N - 1, 0, rng.integers(1, 18, (N, P)))
    for p, e, k in ((0, 0, 0), (P - 1, C - 1, F - 1)):
        s["c"][:, 5, p] = e; s["th"][:, 5, p] = 17; s["su"][:, 5, :, e] = k
    behind(rng, s, 7)
    return pack(s)
def setup_inputs_ties(rng):
    s = parts(rng); five = rng.integers(0, F, (N, 8, 5, C))
    s["su"] = np.take_along_axis(five, rng.integers(0, 5, (N, 8, 16, C)), 2)
    s["pw"] = rng.integers(-1, 2, s["pw"].shape) * (rng.random(s["pw"].shape) < 0.4)
    s["x"] = rng.integers(0, 2, s["x"].shape); s["dr"] = rng.choice(np.array([0, 0, 1, 15]), s["dr"].shape)
    s["th"] = rng.integers(8, 18, (N, 8, P))
    for p, t in ((3, 17), (5, 16), (P - 1, 17)): s["x"][..., p] = 0; s["dr"][..., p] = 0; s["th"][..., p] = t
    return pack(s)
def turn(rng, s, g):
    h = C // 2
    s["pw"][:, g] = rng.integers(1, 8, (N, 16, F)); s["se"][:, g] = np.where(np.arange(C) < h, 1, 0)
    s["x"][:, g] = rng.integers(1, 16, (N, 16, P)); s["th"][:, g] = rng.integers(1, 17, (N, P))
    s["ot"][:, g, 0] = rng.integers(0, h, (N, F)); s["ot"][:, g, 1] = rng.integers(h, C, (N, F))
def setup_inputs_alike(rng):
    s = parts(rng); pool = rng.integers(0, F, (N, 8, 1, 12)); pool[..., 0] = 0; pool[..., 1] = F - 1
    s["su"] = np.take_along_axis(pool, rng.integers(0, 12, (N, 8, 16 * C))[:, :, None, :], 3).reshape(N, 8, 16, C)
    t = rng.integers(0, 8, P)
    for k in ("x", "dr", "c"): s[k][:, ::2] = s[k][:, ::2][..., t]
    h = C // 2; turn(rng, s, 1); turn(rng, s, 3)
    for r in range(N):
        k = np.full(P, 1); k[1 + rng.permutation(P - 2)[:int(rng.integers(65, 125))]] = 0; k[0] = 0; k[P - 1] = 2
        s["su"][r, 1, :, :h] = np.array([0, int(rng.integers(1, F - 1)), F - 1])[np.arange(h) % 3]
        s["c"][r, 1] = k + 3 * rng.integers(0, h // 3, P)
        o = rng.permutation(F)[:F // P * P].reshape(P, F // P); e = rng.permutation(h)[:P]
        s["su"][r, 3][:, e] = o[np.arange(P)[None, :], rng.integers(0, F // P, (16, P))]
        s["c"][r, 3] = e
    return pack(s)
def setup_inputs_ends(rng):
    s = parts(rng)
    s["su"] = np.where(rng.random(s["su"].shape) < 0.3, rng.choice(np.array([0, F - 1]), s["su"].shape), s["su"])
    s["ot"] = np.where(rng.random(s["ot"].shape) < 0.4, rng.choice(np.array([0, C - 1]), s["ot"].shape), s["ot"])
    s["c"] = np.where(rng.random(s["c"].shape) < 0.4, rng.choice(np.array([0, C - 1]), s["c"].shape), s["c"])
    s["pw"] = rng.choice(np.array([-7, 7]), s["pw"].shape)
    s["x"] = rng.choice(np.array([0, 15]), s["x"].shape); s["dr"] = rng.choice(np.array([0, 1, 15]), s["dr"].shape)
    s["th"] = rng.choice(np.array([0, 1, 8, 9, 10, 11, 16, 17]), s["th"].shape)
    s["hw"] = rng.choice(np.array([-7, 7]), s["hw"].shape); s["hw"][:, 0] = 7; s["hw"][:, 1, :, 0] = 7; s["hw"][:, 1, :, 1] = -7
    for p in (0, 7, P - 1): s["x"][..., p] = 15; s["dr"][..., p] = 0; s["th"][..., p] = 17
    return pack(s)
def setup_inputs_spread(rng):
    s = parts(rng)
    s["pw"] = np.rint(s["pw"] * rng.random((N, 8, 1, F))).astype(np.int64)
    s["x"] = (16 * rng.random((N, 8, 1, P)) * rng.random((N, 8, 16, P))).astype(np.int64)
    s["dr"] = (16 * rng.random((N, 8, 1, P)) * rng.random((N, 8, 16, P))).astype(np.int64)
    s["su"] = np.minimum((F * rng.random((N, 8, 16, C)) ** 3).astype(np.int64), F - 1)
    s["ot"] = np.minimum((C * rng.random((N, 8, L, F)) ** 2).astype(np.int64), C - 1)
    s["c"] = np.minimum((C * rng.random((N, 8, P)) ** 4).astype(np.int64), C - 1)
    s["th"] = rng.integers(0, 18, (N, 8, P))
    return pack(s)
def check_inputs(d):
    bad = []
    for k, lo, hi in (("sf", 0, 2 * F - 1), ("pw", -7, 7), ("ot", 0, C - 1), ("x0", 0, 15), ("dr", 0, 15), ("c0", 0, C - 1), ("th", 0, 17), ("hw", -7, 7)):
        a = np.asarray(d[k]).astype(np.float64)
        if not np.all((a >= lo) & (a <= hi) & (a == np.rint(a))): bad.append("range of " + k)
    return bad
def lowest(m, f):
    lane = np.broadcast_to(np.arange(P), m.shape); key = np.arange(N * 8).reshape(N, 8, 1) * F + f
    first = np.full(N * 8 * F, P); np.minimum.at(first, key[m], lane[m])
    return m & (first[key] == lane)
def reference(sf, pw, ot, x0, dr, c0, th, hw):
    cells = sf.astype(np.int64).reshape(N, 8, 16, C); w = pw.astype(np.float32).astype(np.int32).reshape(N, 8, 16, F); o = ot.astype(np.int64).reshape(N, 8, L, F)
    x = x0.astype(np.float32).astype(np.int32).reshape(N, 8, 16, P); step = dr.astype(np.float32).astype(np.int32).reshape(N, 8, 16, P); hv = hw.astype(np.float32).astype(np.int64).reshape(N, 8, 16, 2)
    c = np.stack([gentries(a) for a in c0]).astype(np.int64); t = np.stack([gentries(a) for a in th]).astype(np.int64)
    d = c.copy(); j = np.full((N, 8, P), -1); f = np.zeros((N, 8, P), np.int64)
    rk = np.arange(N)[:, None, None]; gr = np.arange(8)[None, :, None]
    for rnd in range(RO):
        for sub in range(T):
            live = j < L
            code = np.take_along_axis(cells, d[:, :, None, :], 3); su = code >> 1
            v = np.stack([np.add.reduce(np.take_along_axis(w, su[:, :, i:i + 1], 3) * x, axis=2) for i in range(16)], axis=2)
            v = np.where((code & 1) == 1, -v, v)
            inside = live & (np.add.reduce((v >= 0).astype(np.int64), axis=2) >= t); miss = live & ~inside
            a, b, p = np.nonzero(lowest(inside & (j > 0), f)); ff, jj = f[a, b, p], j[a, b, p]
            up, lo = o[a, b, jj - 1, ff], o[a, b, jj, ff]
            o[a, b, jj - 1, ff] = lo; o[a, b, jj, ff] = up
            c = np.where(inside, d, c); x = np.where(inside[:, :, None, :], (x + step) & 15, x)
            least = np.take_along_axis(su, np.argmin(v, axis=2)[:, :, None, :], 2)[:, :, 0]
            f = np.where(miss & (j == -1), least, f)
            j = np.where(inside, -1, np.where(miss, j + 1, j))
            d = np.where(miss & (j < L), o[rk, gr, np.clip(j, 0, L - 1), f], d)
        wait = j == L; q = f % N; served = np.zeros((N, 8, P), bool)
        for k in range(N):
            m = wait & (q == k); n = m.astype(np.int64)
            served = served | (m & (np.add.accumulate(n, axis=2) - n < CAP))
        wq = hv[q, gr]; xt = x.transpose(0, 1, 3, 2).astype(np.int64)
        h = ((np.add.reduce(xt * wq[..., 0], axis=3) * np.add.reduce(xt * wq[..., 1], axis=3)) >> 5) & (F - 1)
        ans = o[q, gr, 0, h]
        a, b, p = np.nonzero(lowest(served, f)); o[a, b, L - 1, f[a, b, p]] = ans[a, b, p]
        d = np.where(served, ans, d); j = np.where(served, L - 1, j)
    return {"yt": o.reshape(N, 8 * L, F).astype(np.float32), "yc": np.stack([gtable(a) for a in c]).astype(np.float32), "yx": x.reshape(N, 128, P).astype(np.float32)}

@@ -1,0 +1,647 @@
+from concourse.bass import DstId, RemoteDMATransfer
+from concourse.mybir import AluOpType as A, ActivationFunctionType as AF
+
+F32, B16, I32, U16, F16 = "float32", "bfloat16", "int32", "uint16", "float16"
+N, NSUB, TW, ZC = 8, 10, 2080, 2064
+NA = 2
+NPOOL = 5
+GA, SC, MU, PE = 1.62, 4.0, 1.04, 0.6
+
+
+def _s(shape, d):
+    return ("sbuf", shape, d)
+
+
+SCRATCH = {
+    "sfs": _s([128, 3072], I32), "pws": _s([128, 2048], B16), "pw2": _s([128, 4096], B16), "otq": _s([128, 512], I32),
+    "oth": _s([128, 512], B16), "otl": _s([128, 512], B16), "tab": _s([128, TW], B16), "xt": _s([128, 11 * 256], B16),
+    "stp": _s([128, 256], B16), "xa": _s([128, 256], B16), "xb": _s([128, 256], B16), "xc": _s([128, 256], B16),
+    "c0s": _s([128, 16], I32), "ths": _s([128, 16], I32), "hws": _s([128, 2], B16), "hwa": _s([128, 16], B16),
+    "xe": _s([128, 4096], B16), "gg": _s([128, 4096], B16), "p2": _s([128, 4096], B16), "pp": _s([128, 16, 16, 16], B16),
+    "cod": _s([128, 256], U16), "sr": _s([128, 256], I32), "ind": _s([128, 256], B16), "mns": _s([128, 256], F32),
+    "cnt": _s([128, 256], B16), "sg": _s([128, 256], F16), "ee": _s([128, 256], B16), "lg": _s([128, 256], B16),
+    "lm": _s([128, 256], B16), "col": _s([128, 256], B16), "mm": _s([128, 256], B16), "ncl": _s([128, 256], B16),
+    "frm": _s([128, 256], F32), "uu": _s([128, 512], B16), "hg": _s([128, 2048], B16), "dg": _s([128, 512], B16),
+    "ag": _s([128, 256], F32), "msk": _s([128, 256], F32), "ya": _s([128, 2048], F32), "y3": _s([128, TW], F32),
+    "yxs": _s([128, 256], F32), "anr": _s([128, 256], F32), "oh": _s([128, 256], B16), "cum": _s([128, 256], B16),
+    "le": _s([128, 256], B16), "svr": _s([128, 256], B16), "asc": _s([128, 256], F32),
+    "req0": _s([128, 128], U16), "req1": _s([128, 128], U16), "xb0": _s([128, 272], F32), "xb1": _s([128, 272], F32),
+    "inh": _s([128, 176], B16), "idh": _s([128, 176], F32), "nih": _s([128, 176], F32), "csc": _s([128, 176], F32),
+    "sm": _s([128, 20, 16], F32), "si": _s([128, 6, 16], I32), "nf": _s([128, 16], F32), "fc": _s([128, 16], F32),
+    "qs": _s([128, 16], F32), "hl": _s([128, 32], B16),
+    "du": _s([128, 16], U16), "fz": _s([128, 16], U16), "iu": _s([128, 16], U16), "nu": _s([128, 16], U16),
+    "ju": _s([128, 16], U16), "ou": _s([128, 32], U16), "qo": _s([128, 32], U16), "wu": _s([128, 16], U16),
+    "pu": _s([128, 16], U16), "bc": _s([128, 32], U16),
+    "pi": _s([128, 8], I32), "ci": _s([128, 8], I32), "cf": _s([128, 32], F32), "ro": _s([128, 144], F32),
+    "rx": _s([128, 4, 128], F32), "ii": _s([128, 256], B16), "kp": _s([128, 256], B16), "bg": _s([128, 256], B16),
+    "one": _s([128, 256], B16), "tri": _s([128, 256], B16), "dia": _s([128, 256], B16), "fh": _s([128, 512], B16),
+    "fl": _s([128, 512], B16), "zz": _s([128, 6, 144], B16), "zh": _s([128, 144], F16), "mb": _s([128, 14, 128], B16),
+    "mf": _s([128, 3, 128], F32), "hq": _s([128, 7, 144], B16), "w32": _s([128, 32], B16), "lt": _s([128, 16], B16),
+    "st": _s([128, 16], B16), "r3": _s([128, 16], B16),
+}
+for _b in range(8):
+    SCRATCH["ps%d" % _b] = ("psum", [128, 512], F32)
+SEMAPHORES = ["pool", "pe", "dve", "act", "l_c0", "l_sf", "l_ot", "l_x0", "l_pw", "l_dr", "l_th", "l_hw", "l_hs", "hwarr",
+              "rq0", "rq1", "an0", "an1", "sent", "o_ya", "o_y3", "o_yc", "o_yx"]
+
+
+def slots(T, topo, h):
+    ch = topo.chip(T.cores[h])
+
+    def far(s):
+        cs = topo.chip(T.cores[s])
+        return (3 if s == h else 2 if cs == ch else 1 if topo.same_plane(cs, ch) else 0, s)
+    return sorted(range(N), key=far)
+
+
+def off_engines(T, topo, src):
+    return topo.engines(src, [c for c in T.cores if topo.chip(c) != topo.chip(src)][0])
+
+
+def share(T, topo, src, dsts):
+    off = off_engines(T, topo, src)
+    far = [d for d in dsts if topo.chip(d) != topo.chip(src)]
+    per = 1
+    while far and 2 * per * len(far) <= len(off):
+        per *= 2
+    out = {d: off[k * per:(k + 1) * per] for k, d in enumerate(far)}
+    for d in dsts:
+        if d not in out:
+            out[d] = [e for e in topo.engines(src, d) if e not in off]
+    return out
+
+
+def bits(engines):
+    return sum(1 << e for e in engines)
+
+
+def schedule(ops):
+    n = len(ops)
+    succ = [[] for _ in range(n)]
+    left = [0] * n
+    for i, o in enumerate(ops):
+        pre = {}
+        for d in o["deps"]:
+            if isinstance(d, tuple):
+                for a in d[2]:
+                    pre[a] = max(pre.get(a, 0), d[3])
+            else:
+                pre[d] = max(pre.get(d, 0), ops[d]["lat"] + (60 if ops[d]["eng"] == o["eng"] else 110))
+        for d in o["ord"]:
+            pre.setdefault(d, 0)
+        for d, l in pre.items():
+            succ[d].append((i, l))
+        left[i] = len(pre)
+    prio = [0.0] * n
+    for i in range(n - 1, -1, -1):
+        prio[i] = ops[i]["cost"] + max([l + prio[j] for j, l in succ[i]] + [ops[i]["lat"]])
+    ready = [0.0] * n
+    cand = {}
+    for i in range(n):
+        if left[i] == 0:
+            cand.setdefault(ops[i]["eng"], []).append(i)
+    free, order = {}, []
+    while len(order) < n:
+        best = None
+        for e, l in cand.items():
+            if not l:
+                continue
+            t0 = max(free.get(e, 0.0), min(ready[i] for i in l))
+            pick = max((i for i in l if ready[i] <= t0), key=lambda i: (prio[i], -i))
+            soon = [i for i in l if t0 < ready[i] < t0 + 0.4 * ops[pick]["cost"] and prio[i] > prio[pick] + 300]
+            if soon:
+                pick = max(soon, key=lambda i: (prio[i], -i))
+            st = max(t0, ready[pick])
+            if best is None or st < best[0]:
+                best = (st, e, pick)
+        st, e, i = best
+        cand[e].remove(i)
+        free[e] = st + ops[i]["cost"]
+        order.append(i)
+        for j, l in succ[i]:
+            ready[j] = max(ready[j], free[e] + l)
+            left[j] -= 1
+            if left[j] == 0:
+                cand.setdefault(ops[j]["eng"], []).append(j)
+    return order
+
+
+def rank_program(g, core, T, topo):
+    rank = T.rank_of(core)
+    if rank is None:
+        return
+    Q = {"pool": g, "pe": g.tensor, "dve": g.vector, "act": g.scalar, "sync": g.sync}
+    ops, lastw, readers = [], {}, {}
+
+    def op(eng, fn, r, w, cost, dma=None, lat=0.0):
+        deps, order = [], []
+        for k in r:
+            if k in lastw:
+                deps.append(lastw[k])
+            if k.startswith("ps"):
+                deps += [x for x in readers.get(k, []) if ops[x]["eng"] != eng]
+        for k in w:
+            for x in readers.get(k, []) + ([lastw[k]] if k in lastw else []):
+                (order if eng == "pe" and ops[x]["eng"] == "pe" else deps).append(x)
+        ops.append({"eng": eng, "fn": fn, "deps": deps, "ord": order, "dma": dma, "sig": False, "cost": cost, "lat": lat})
+        me_ = len(ops) - 1
+        for k in r:
+            readers.setdefault(k, []).append(me_)
+        for k in w:
+            lastw[k] = me_
+            readers[k] = []
+        return me_
+
+    v = g.vector
+
+    def vc(n, k):
+        return 60 + (max(67.0, n * k) if k < GA else n * k)
+
+    def ts(out, in0, s1, o0, s2=None, o1=None, r=(), w=(), n=16, k=1.04):
+        if o1 is None:
+            op("dve", lambda: v.tensor_scalar(out, in0, s1, None, o0), r, w, vc(n, k))
+        else:
+            op("dve", lambda: v.tensor_scalar(out, in0, s1, s2, o0, o1), r, w, vc(n, k))
+
+    def tt(out, a, b, o, r, w, n=16, k=MU):
+        op("dve", lambda: v.tensor_tensor(out, a, b, o), r, w, vc(n, k))
+
+    def cp(out, a, r, w, n=16, k=1.04):
+        op("dve", lambda: v.tensor_copy(out, a), r, w, vc(n, k))
+
+    def ms(out, c, w, n=16):
+        op("dve", lambda: v.memset(out, c), (), w, vc(n, 0.52))
+
+    def scan(out, d0, d1, o0, o1, r, w, k=1.04):
+        op("dve", lambda: v.tensor_tensor_scan(out, d0, d1, 0.0, o0, o1), r, w, vc(256, k))
+
+    def ac(out, a, r, w, n=256, k=1.04, bias=None):
+        if bias is None:
+            op("act", lambda: g.scalar.activation(out, a, AF.Copy), r, w, 15 + vc(n, k))
+        else:
+            op("act", lambda: g.scalar.activation(out, a, AF.Identity, bias=bias), r, w, 15 + vc(n, k))
+
+    def mm(out, l, rh, st, sp, r, w, n=64):
+        op("pe", lambda: g.tensor.matmul(out, l, rh, st, sp), r, w, max(64, n) * PE)
+
+    def iota(out, pat, base, cm, w, n, flag=True):
+        if flag:
+            op("pool", lambda: g.iota(out, pat, base, cm, allow_small_or_imprecise_dtypes=True), (), w, 130 + 2.1 * n)
+        else:
+            op("pool", lambda: g.iota(out, pat, base, cm), (), w, 130 + 2.1 * n)
+
+    def dma(eng, out, in_, sem, r, w, lat):
+        op(eng, lambda: Q[eng].dma_start(out, in_), r, w + ["q" + eng + sem], 60, dma=sem, lat=lat)
+
+    PS = [T["ps%d" % b] for b in range(8)]
+
+    def to_l(bank, n, z, src, first, rk, lo=0, hi=None):
+        for r_ in range(16):
+            mm(PS[bank][:, 0:n], z(r_), src[:, lo + r_:hi:16], first and r_ == 0, r_ == 15, rk, ["ps%d" % bank])
+
+    def zw(k):
+        return lambda r_: T.zz[:, k, 15 - r_:143 - r_]
+    Z32, Z1, Z4K, ZA, ZQ, Z37 = [zw(k) for k in range(6)]
+
+    def ZH(r_):
+        return T.zh[:, 15 - r_:143 - r_]
+
+    peers = [s for s in range(N) if s != rank]
+    far = [s for s in peers if topo.chip(T.cores[s]) != topo.chip(core)]
+    near = [s for s in peers if s not in far]
+    sent = [0]
+
+    def dst(s):
+        a = topo.addr(T.cores[s])
+        return DstId(rid=a[0], pnc=a[1])
+
+    def to_all(src, land, sem, r, key, cost):
+        off = off_engines(T, topo, core)
+        trs = [RemoteDMATransfer(dst_ids=[dst(s) for s in far], dma_engine_mask=bits(off), remote_sem=T.sem[sem], srcs=[src], dsts=[land(s) for s in far])]
+        sent[0] += len(off)
+        for s in near:
+            en = share(T, topo, core, [T.cores[s]])[T.cores[s]]
+            trs.append(RemoteDMATransfer(dst_ids=[dst(s)], dma_engine_mask=bits(en), remote_sem=T.sem[sem], src=src, dst=land(s)))
+            sent[0] += len(en)
+        me_ = op("pool", lambda: g.remote_dma_fused(trs, local_sem=T.sem.sent), r, (), cost)
+        come = sum(len(off_engines(T, topo, T.cores[s])) for s in far) + sum(len(share(T, topo, T.cores[s], [core])[core]) for s in near)
+        lastw[key] = (sem, come, [me_], 6000)
+
+    def halves(h):
+        sl = slots(T, topo, h)
+        return [sl[0:4], [s for s in sl[4:8] if s != h]]
+
+    def answer_engines(h, half):
+        return share(T, topo, T.cores[h], [T.cores[s] for s in halves(h)[half]])
+
+    ans_in = sum(len(answer_engines(h, hf)[core]) for h in peers for hf in range(2) if rank in halves(h)[hf])
+    myslots = slots(T, topo, rank)
+
+    dma("sync", T.c0s[:], T.c0[:], "l_c0", [], ["c0s", "sq"], 2000)
+    dma("act", T.xt[:, 0:256], T.x0[:], "l_x0", [], ["x0"], 2200)
+    dma("act", T.pws[:], T.pw[:], "l_pw", [], ["pws"], 4000)
+    dma("sync", T.sfs[:], T.sf[:], "l_sf", [], ["sfs"], 9000)
+    dma("sync", T.otq[:], T.ot[:], "l_ot", [], ["otq"], 10000)
+    dma("act", T.stp[:], T.dr[:], "l_dr", [], ["stp"], 4500)
+    dma("act", T.ths[:], T.th[:], "l_th", [], ["ths"], 4500)
+    dma("sync", T.hws[:], T.hw[:], "l_hs", [], ["hws"], 10000)
+    dma("sync", T.hwa[:, 2 * rank:2 * rank + 2], T.hw[:], "l_hw", [], ["hwown"], 10000)
+    for a_, b_ in ((0, 3), (3, 4), (4, 7), (7, 8), (1, 2), (2, 5), (5, 6)):
+        ops[b_]["ord"].append(a_)
+
+    iota(T.pi[:, 0:1], [[0, 1]], 0, 1, ["pi"], 1, False)
+    iota(T.ro[:], [[1, 144]], 0, 0, ["ro"], 144)
+    iota(T.ii[:], [[0, 16], [1, 16]], 0, 0, ["ii"], 256)
+    iota(T.fh[:], [[64, 8], [0, 64]], 0, 512, ["fh"], 512)
+    iota(T.fl[:], [[0, 8], [1, 64]], 0, 0, ["fl"], 512)
+    iota(T.rx[:, 0], [[2, 64], [-1, 2]], 1, 0, ["rx0"], 128)
+    iota(T.rx[:, 1], [[4, 32], [-1, 4]], 3, 0, ["rx1"], 128)
+    iota(T.rx[:, 2], [[16, 8], [-8, 2], [1, 8]], 8, 0, ["rx2"], 128)
+    iota(T.rx[:, 3], [[16, 8], [0, 16]], 0, 0, ["rx3"], 128)
+    C = {}
+
+    def colf(name, k):
+        C[name] = T.cf[:, k:k + 1]
+        return C[name]
+    for k, (m, sh) in enumerate(((15, 0), (112, 0), (3, 0), (15, 2), (2, 0), (127, 0))):
+        ts(T.ci[:, k:k + 1], T.pi[:, 0:1], m, A.bitwise_and, sh, A.logical_shift_right, r=["pi"], w=["ci%d" % k])
+    cp(T.cf[:, 0:6], T.ci[:, 0:6], ["ci%d" % k for k in range(6)], ["cf"])
+    for k, n_ in enumerate(("r", "g16", "r3", "rq", "b2", "p")):
+        colf(n_, k)
+    S = {n_: T.sm[:, k] for k, n_ in enumerate(("th", "thp", "nq", "df", "jj", "jm", "e5", "fd", "j2", "cfd", "nfd", "nin", "ub", "sv", "nw", "yc", "t1"))}
+    SI = {n_: T.si[:, k] for k, n_ in enumerate(("mk", "mk2", "fi", "q", "pr", "h"))}
+    IB, I4K, BM, BOF, IKP, SELY = T.mb[:, 0], T.mb[:, 6], T.mb[:, 7], T.mb[:, 8], T.mb[:, 9], T.mb[:, 10, 0:32]
+    IF, IF16, DD = T.mf[:, 0], T.mf[:, 1], T.mf[:, 2]
+    R128 = T.ro[:, 0:128]
+    for name, k, a, s1, o0, s2, o1 in (
+            ("a", 6, "g16", 15.0, A.add, None, None), ("k", 7, "g16", "rq", A.add, 4.0, A.add), ("k8", 8, "g16", "rq", A.add, 12.0, A.add),
+            ("ge4", 9, "r", 4.0, A.is_ge, None, None), ("mid", 10, "r", 12.0, A.is_lt, "ge4", A.mult), ("r256", 11, "r", 1.0 / 256, A.mult, None, None),
+            ("dum", 12, "r", 2048.0, A.add, None, None), ("lt8", 13, "r", 8.0, A.is_lt, None, None), ("d16", 14, "dum", 1.0 / 16, A.mult, None, None),
+            ("ge8", 15, "r", 8.0, A.is_ge, None, None), ("s1", 17, "b2", 2.0, A.add, "lt8", A.mult), ("rm8", 23, "r", -8.0, A.add, None, None),
+            ("p1", 24, "r", 16.0, A.mult, 128.0, A.min), ("p2", 25, "r", float(rank), A.is_equal, float(256 - 16 * rank), A.mult),
+            ("y", 26, "g16", 0.25, A.mult, "r3", A.add), ("ndum", 28, "r", -1.0, A.mult, -2048.0, A.add)):
+        ts(colf(name, k), C[a], C.get(s1, s1), o0, C.get(s2, s2), o1, r=["cf"] + ["c_" + x for x in (a, s1, s2) if isinstance(x, str)], w=["c_" + name])
+
+    def eq(out, row, rk, a, s2, w, n):
+        ts(out, row, C.get(a, a), A.is_equal, C.get(s2, s2), None if s2 is None else A.mult,
+           r=["cf", rk] + ["c_" + x for x in (a, s2) if isinstance(x, str)], w=[w], n=n)
+    eq(T.r3[:], T.ro[:, 0:16], "ro", "r3", None, "r3", 16)
+    eq(IB, R128, "ro", "p", None, "ib", 128)
+    eq(T.hq[:, 4], T.ro[:], "ro", "k", None, "hq4", 144)
+    eq(T.hq[:, 5], T.ro[:], "ro", "k8", "mid", "hq5", 144)
+    eq(T.zz[:, 0], T.ro[:], "ro", "a", 32.0, "z32", 144)
+    eq(T.zz[:, 1], T.ro[:], "ro", "a", None, "z1", 144)
+    eq(T.zz[:, 2], T.ro[:], "ro", "a", 4096.0, "z4k", 144)
+    eq(T.zh[:], T.ro[:], "ro", "a", None, "zh", 144)
+    eq(T.w32[:], T.ro[:, 0:32], "ro", "r", None, "w32", 32)
+    eq(I4K, R128, "ro", "p", 4096.0, "i4k", 128)
+    eq(IF, R128, "ro", "p", None, "if", 128)
+    eq(IF16, R128, "ro", "p", 1.0 / 16, "if16", 128)
+    eq(DD, R128, "ro", "p", "d16", "dd", 128)
+    tt(T.hq[:, 6], T.hq[:, 4], T.hq[:, 5], A.add, ["hq4", "hq5"], ["hq6"], 144)
+    for q in range(4):
+        ts(T.mb[:, 1 + q], T.ii[:, 0:128], 8.0, A.is_equal, T.mb[:, 0, q:q + 1], A.mult, r=["ii", "ib"], w=["s8%d" % q])
+        ts(T.hq[:, q], T.hq[:, 6], T.r3[:, q:q + 1], A.mult, r=["hq6", "r3"], w=["hq%d" % q])
+    ts(T.mb[:, 5], T.ii[:, 0:128], 11.0, A.is_equal, T.mb[:, 0, 0:1], A.mult, r=["ii", "ib"], w=["s11"])
+    tt(colf("m12", 16), T.r3[:, 1:2], T.r3[:, 2:3], A.add, ["r3"], ["c_m12"])
+    ts(colf("s2", 18), C["m12"], 4.0, A.mult, -1.0, A.add, r=["c_m12"], w=["c_s2"])
+    ts(colf("s3", 19), C["s2"], C["ge8"], A.mult, C["s1"], A.add, r=["c_s2", "c_ge8", "c_s1"], w=["c_s3"])
+    eq(T.mb[:, 11], T.rx[:, 0], "rx0", "p", "lt8", "m11", 128)
+    eq(T.mb[:, 12], T.rx[:, 1], "rx1", "p", "ge8", "m12", 128)
+    eq(T.mb[:, 13], T.rx[:, 2], "rx2", "p", "m12", "m13", 128)
+    eq(T.st[:], T.ro[:, 0:16], "ro", "s3", None, "st", 16)
+    tt(T.mb[:, 11], T.mb[:, 11], T.mb[:, 12], A.add, ["m11", "m12"], ["m11"], 128)
+    tt(T.mb[:, 13], T.mb[:, 13], IB, A.add, ["m13", "ib"], ["m13"], 128)
+    tt(T.mb[:, 11], T.mb[:, 11], IB, A.subtract, ["m11", "ib"], ["m11"], 128)
+    for name, k, a, b in (("f2", 20, 8, 11), ("a04", 21, 0, 4), ("a37", 22, 3, 7)):
+        tt(colf(name, k), T.w32[:, a:a + 1], T.w32[:, b:b + 1], A.add, ["w32"], ["c_" + name])
+    ts(colf("n37", 27), C["a37"], 0.0, A.is_equal, r=["c_a37"], w=["c_n37"])
+    eq(BOF, T.rx[:, 3], "rx3", "g16", "f2", "bof", 128)
+    eq(T.zz[:, 3], T.ro[:], "ro", "a", "a04", "za", 144)
+    eq(T.zz[:, 4], T.ro[:], "ro", "a", "rm8", "zq", 144)
+    eq(T.zz[:, 5], T.ro[:], "ro", "a", "a37", "z37", 144)
+    eq(SELY, T.ro[:, 0:32], "ro", "y", "lt8", "sely", 32)
+    eq(IKP, R128, "ro", "p", "n37", "ikp", 128)
+    ts(T.dia[:], T.ii[:], C["r"], A.is_equal, r=["ii", "cf"], w=["dia"], n=128)
+    ts(T.tri[:], T.ii[:], C["r"], A.is_le, -8192.0, A.mult, r=["ii", "cf"], w=["tri"], n=128)
+    ts(T.kp[:], T.ii[:], 0.0, A.is_gt, r=["ii"], w=["kp"], n=128)
+    ts(T.bg[:], T.ii[:], 0.0, A.is_equal, 1.0e6, A.mult, r=["ii"], w=["bg"], n=128)
+    ts(T.pu[:], T.ro[:, 0:16], C["p1"], A.add, C["p2"], A.add, r=["ro", "c_p1", "c_p2"], w=["pu"])
+    ts(T.lt[:], T.r3[:], C["lt8"], A.mult, r=["r3", "c_lt8"], w=["lt"])
+    ts(S["nq"], T.ro[:, 0:16], 1.0 / 16, A.mult, C["r256"], A.add, r=["ro", "c_r256"], w=["nq"])
+    cp(T.bc[:], T.ro[:, 0:32], ["ro"], ["bc"])
+    cp(T.du[:], T.c0s[:], ["c0s"], ["du"])
+    cp(S["th"], T.ths[:], ["ths"], ["th"])
+    cp(S["df"], T.c0s[:], ["c0s"], ["df"])
+    cp(T.idh[:, 0:176:11], T.c0s[:], ["c0s"], ["id_0"])
+    ms(T.one[:], 1.0, ["one"], 256)
+    ms(T.ju[:], 0, ["ju"])
+    ms(S["jm"], 1.0, ["jm"])
+    ms(T.xt[:, 512:2816], 0.0, ["x%d" % n_ for n_ in range(2, 11)], 2304)
+    ms(T.inh[:, 0:176:11], 1.0, ["in_0"])
+    ms(T.ou[:], 0, ["ou"])
+    ms(T.tab[:, 2048:TW], 0.0, ["tabz"])
+    ms(T.y3[:, 2048:TW], 0.0, ["y3z"])
+    ms(T.xb1[:, 128:144], 0.0, ["dfxb1"])
+    for e in range(2):
+        ms(T["xb%d" % e][:, 16 * rank:16 * rank + 16], 0.0, ["ownxb%d" % e])
+    to_all(T.hws[:], lambda s: T.hwa[:, 2 * rank:2 * rank + 2], "hwarr", ["hws"], "hwa", 3000)
+
+    for h_ in range(2):
+        cp(T.pw2[:, 2048 * h_:2048 * h_ + 2048:2], T.pws[:, 1024 * h_:1024 * h_ + 1024], ["pws"], ["pw2a%d" % h_], 512)
+        ts(T.pw2[:, 2048 * h_ + 1:2048 * h_ + 2048:2], T.pws[:, 1024 * h_:1024 * h_ + 1024], -1.0, A.mult, r=["pws"], w=["pw2b%d" % h_], n=512)
+    PW2 = ["pw2a0", "pw2a1", "pw2b0", "pw2b1"]
+    cp(T.oth[:], T.otq[:], ["otq"], ["oth"], 512)
+    tt(T.otl[:], T.otq[:], T.oth[:], A.subtract, ["otq", "oth"], ["otl"], 1024)
+    for q in range(4):
+        k = ["ps%d" % (4 + q)]
+        mm(PS[4 + q][:], T.mb[:, 1 + q], T.fh[:], True, False, ["s8%d" % q, "fh"], k, 512)
+        mm(PS[4 + q][:], T.mb[:, 5], T.fl[:], False, False, ["s11", "fl"], k, 512)
+        mm(PS[4 + q][:], T.hq[:, q, 4:132], T.oth[:], False, False, ["hq%d" % q, "oth"], k, 512)
+        mm(PS[4 + q][:], T.hq[:, q, 0:128], T.otl[:], False, True, ["hq%d" % q, "otl"], k, 512)
+        if q % 2:
+            ac(T.tab[:, 512 * q:512 * q + 512], PS[4 + q][:], k, ["tab%d" % q], 512)
+        else:
+            cp(T.tab[:, 512 * q:512 * q + 512], PS[4 + q][:], k, ["tab%d" % q], 512)
+    mm(PS[6][:, 0:128], T.mb[:, 11], T.mb[:, 13], True, True, ["m11", "m13"], ["ps6"], 128)
+    cp(BM, PS[6][:, 0:128], ["ps6"], ["bm"], 128)
+    TAB = ["tab%d" % q for q in range(4)] + ["tabz"]
+    XE = ["xe%d" % i for i in range(16)]
+
+    def expand(src, key, nd):
+        for i in range(16):
+            o = T.xe[:, i:4096:16]
+            if i < NPOOL:
+                op("pool", lambda o=o: g.affine_select(o, src, [[0, 256]], A.is_ge, 0.0, 0, 0), [key], ["xe%d" % i], 700)
+            elif i < 16 - nd:
+                ac(o, src, [key], ["xe%d" % i])
+            else:
+                cp(o, src, [key], ["xe%d" % i], 128)
+
+    def next_x(n):
+        a, b = T.xt[:, 256 * (n - 1):256 * n], T.xt[:, 256 * n:256 * n + 256]
+        tt(T.xa[:], a, T.stp[:], A.add, ["x%d" % (n - 1), "stp"], ["xa"], 256)
+        ts(T.xb[:], T.xa[:], 16.0, A.is_ge, -16.0, A.mult, r=["xa"], w=["xb"], n=128)
+        tt(b, T.xa[:], T.xb[:], A.add, ["xa", "xb", "xread"], ["x%d" % n], 256)
+
+    def place(out, n, w):
+        ac(out, T.xt[:, 0:256 * n + 256].indirect(T.nu[:]), ["x%d" % k for k in range(n + 1)] + ["nu"], w, k=GA)
+
+    def scatters(win, src, rk, wk):
+        for c in range(15, -1, -1):
+            cp(win[:].indirect(T.ou[:, 2 * c:2 * c + 1]), src[:, 16 * c:16 * c + 16], ["ou"] + rk, wk, 16, SC)
+
+    def lowest(flag, fk, base, bk):
+        tt(T.fc[:], flag, base, A.mult, [fk, bk], ["fc"])
+        tt(T.ee[:], T.fc[:].indirect(T.bc[:, 0:16]), T.frm[:], A.is_equal, ["fc", "bc", "frm"], ["ee"], 256, GA)
+        mm(PS[2][:, 0:16], IF, T.fc[:], True, False, ["if", "fc"], ["ps2"], 256)
+        to_l(2, 16, Z4K, T.ee, False, ["z4k", "ee"])
+        ts(T.ou[:, 0:32:2], PS[2][:, 0:16], 0.0, A.min, C["dum"], A.add, r=["ps2", "c_dum"], w=["ou"])
+
+    def columns():
+        ac(T.col[:], T.tab[:].indirect(T.fz[:]), TAB + ["fz"], ["col"], k=GA)
+        mm(PS[5][:, 0:256], IB, T.tri[:], True, False, ["ib", "tri"], ["ps5"], 256)
+        mm(PS[5][:, 0:256], BOF, T.col[:], False, True, ["bof", "col"], ["ps5"], 256)
+        ac(T.frm[:], PS[5][:, 0:256], ["ps5", "c_ndum"], ["frm"], bias=C["ndum"])
+
+    def swapped():
+        tt(T.mm[:], T.st[:].indirect(T.ju[:]), T.col[:], A.mult, ["st", "ju", "col"], ["mm"], 256, GA)
+        mm(PS[4][:, 0:256], IB, T.col[:], True, False, ["ib", "col"], ["ps4"], 256)
+        mm(PS[4][:, 0:256], BM, T.mm[:], False, True, ["bm", "mm"], ["ps4"], 256)
+        ac(T.ncl[:], PS[4][:, 0:256], ["ps4"], ["ncl"])
+
+    def statics(t):
+        cp(T.ju[:], S["jj"], ["jj"], ["ju"])
+        ts(S["jm"], S["jj"], 1.0, A.add, 5.0, A.min, r=["jj"], w=["jm"])
+        if t < NSUB - 1:
+            ac(T.lm[:], T.lt[:].indirect(T.ju[:]), ["lt", "ju"], ["lm"], k=GA)
+            ts(T.nf[:], S["jj"], 1.0, A.is_ge, 16.0, A.mult, r=["jj"], w=["nf"])
+            tt(S["nfd"], T.nf[:], S["fd"], A.mult, ["nf", "fd"], ["nfd"])
+        if t >= 2:
+            ts(S["j2"], S["jj"], 2.0, A.is_ge, r=["jj"], w=["j2"])
+            tt(S["cfd"], S["j2"], S["fd"], A.mult, ["j2", "fd"], ["cfd"])
+        if t >= 5:
+            ts(S["e5"], S["jj"], 5.0, A.is_equal, 99.0, A.mult, r=["jj"], w=["e5"])
+            tt(S["thp"], S["e5"], S["th"], A.add, ["e5", "th"], ["thp"])
+
+    def request(e):
+        rq = T["req%d" % e]
+        own = rq[:, 112:128]
+        cp(SI["fi"], T.fz[:], ["fz"], ["fi"])
+        ts(SI["q"], SI["fi"], 7, A.bitwise_and, r=["fi"], w=["q"])
+        for h_ in range(2):
+            ts(T.qo[:, 16 * h_:16 * h_ + 16], SI["q"], 2.0, A.mult, float(h_), A.add, r=["q"], w=["qo%d" % h_])
+            tt(T.uu[:, 256 * h_:256 * h_ + 256], T.hwa[:].indirect(T.qo[:, 16 * h_:16 * h_ + 16]), T.xc[:], A.mult, ["hwa", "hwown", "qo%d" % h_, "xc"], ["uu%d" % h_], 256, GA)
+        to_l(6, 32, Z1, T.uu, True, ["z1", "uu0", "uu1"])
+        cp(S["ub"], PS[6][:, 16:32], ["ps6"], ["ub"])
+        tt(SI["pr"], PS[6][:, 0:16], S["ub"], A.mult, ["ps6", "ub"], ["pr"])
+        ts(SI["h"], SI["pr"], 5, A.arith_shift_right, 2047, A.bitwise_and, r=["pr"], w=["h"])
+        cp(own, SI["h"], ["h"], ["rqown%d" % e])
+        to_all(own, lambda s: rq[:, 16 * slots(T, topo, s).index(rank):16 * slots(T, topo, s).index(rank) + 16], "rq%d" % e,
+               ["rqown%d" % e, "ownxb%d" % e], "rqarr%d" % e, 600)
+
+    def codes():
+        cp(T.cod[:], T.sfs[:].indirect(T.du[:]), ["sfs", "du"], ["cod"], 256, GA)
+
+    def test():
+        mm(PS[0][:, 0:256], IB, T.ii[:], True, False, ["ib", "ii"], ["ps0"], 256)
+        for a in range(0, NA, 2):
+            b = min(a + 2, NA)
+            tt(T.p2[:, 256 * a:256 * b], T.pw2[:].indirect(T.cod[:, 16 * a:16 * b]), T.xe[:, 256 * a:256 * b], A.mult, PW2 + ["cod"] + XE, ["pp%d" % a], 256 * (b - a), GA)
+            for c in range(a, b):
+                for r_ in range(16):
+                    mm(PS[0][:, 16 * c:16 * c + 16], Z32(r_), T.p2[:, 256 * c + 16 * r_:256 * c + 16 * r_ + 16], False, False, ["z32", "pp%d" % a], ["ps0"])
+        cuts = list(range(NA, 14, 2)) + [14, 15, 16]
+        start, keys = NA, []
+        for a, b in zip(cuts[:-1], cuts[1:]):
+            ac(T.gg[:, 256 * a:256 * b], T.pw2[:].indirect(T.cod[:, 16 * a:16 * b]), PW2 + ["cod"], ["gg%d" % a], 256 * (b - a), GA)
+            tt(T.pp[:, a:b], T.gg[:, 256 * a:256 * b], T.xe[:, 256 * a:256 * b], A.mult, ["gg%d" % a] + XE, ["pp%d" % a], 256 * (b - a))
+            keys.append("pp%d" % a)
+            if (16 - b) % 4 == 0:
+                for r_ in range(16):
+                    mm(PS[0][:, 16 * start:16 * b], Z32(r_), T.pp[:, start:b, r_, :], False, b == 16 and r_ == 15, ["z32"] + keys, ["ps0"])
+                start, keys = b, []
+
+    expand(T.xt[:, 0:256], "x0", 0)
+    ac(T.lm[:], T.lt[:].indirect(T.ju[:]), ["lt", "ju"], ["lm"], k=GA)
+    codes()
+    for t in range(NSUB):
+        last, re_, ex, e = t == NSUB - 1, t >= 2, t % 5 == 4, t // 5
+        next_x(t + 1)
+        if ex:
+            request(e)
+        test()
+        if not last:
+            ts(T.sr[:], T.cod[:], 0.5, A.mult, -0.25, A.add, r=["cod"], w=["sr"], n=256)
+        if re_:
+            swapped()
+        ins, ik = T.inh[:, t + 1:176:11], "in_%d" % (t + 1)
+        thp, tk = (S["thp"], "thp") if t >= 5 else (S["th"], "th")
+        ts(T.ind[:], PS[0][:, 0:256], 0.0, A.is_ge, r=["ps0"], w=["ind"], n=256)
+        scan(T.cnt[:], T.kp[:], T.ind[:], A.mult, A.add, ["kp", "ind"], ["cnt"], 0.52)
+        tt(ins, T.cnt[:, 15:256:16], thp, A.is_ge, ["cnt", tk], [ik])
+        tt(S["nq"], S["nq"], ins, A.add, ["nq", ik], ["nq"])
+        ts(T.nu[:], S["nq"], 256.0, A.mult, r=["nq"], w=["nu"])
+        idd, idk = T.idh[:, t + 1:176:11], "id_%d" % (t + 1)
+        tt(idd, ins, S["df"], A.mult, [ik, "df"], [idk])
+        tt(S["nin"], T.cnt[:, 15:256:16], thp, A.is_lt, ["cnt", tk], ["nin"])
+        tt(S["jj"], S["nin"], S["jm"], A.mult, ["nin", "jm"], ["jj"])
+        if last:
+            place(T.yxs[:], t + 1, ["yxs"])
+            dma("sync", T.yx[:], T.yxs[:], "o_yx", ["yxs"], ["yx"], 2500)
+        else:
+            place(T.xc[:], t + 1, ["xc"])
+            expand(T.xc[:], "xc", 0 if re_ else 4)
+            scan(T.mns[:], T.bg[:], PS[0][:, 0:256], A.add, A.min, ["bg", "ps0"], ["mns"])
+            if t == 0:
+                cp(SI["mk"], T.mns[:, 15:256:16], ["mns"], ["mk"])
+            else:
+                tt(SI["mk"], T.mns[:, 15:256:16], T.nf[:], A.add, ["mns", "nf"], ["mk"])
+            ts(SI["mk2"], SI["mk"], 31, A.bitwise_and, r=["mk"], w=["mk2"])
+            cp(T.iu[:], SI["mk2"], ["mk2"], ["iu"])
+            tt(T.sg[:], T.w32[:].indirect(T.iu[:]), T.sr[:], A.mult, ["w32", "iu", "sr"], ["sg"], 256, GA)
+            mm(PS[1][:, 0:16], I4K, ins, True, False, ["i4k", ik], ["ps1"])
+            if t > 0:
+                mm(PS[1][:, 0:16], IF16, S["nfd"], False, False, ["if16", "nfd"], ["ps1"], 256)
+                mm(PS[1][:, 0:16], DD, T.nf[:], False, False, ["dd", "nf"], ["ps1"], 256)
+            to_l(1, 16, ZH, T.sg, False, ["zh", "sg"])
+        if re_:
+            lowest(ins, ik, S["cfd"], "cfd")
+            scatters(T.tab, T.ncl, ["ncl"], TAB)
+        if ex:
+            xb, rq = T["xb%d" % e], T["req%d" % e]
+            rk = TAB + ["rqarr%d" % e, "rqown%d" % e]
+            for hf in range(2):
+                cp(T.hg[:, 1024 * hf:1024 * hf + 512], T.tab[:].indirect(rq[:, 64 * hf:64 * hf + 32]), rk, ["hga%d" % hf], 512, GA)
+                ac(T.hg[:, 1024 * hf + 512:1024 * hf + 1024], T.tab[:].indirect(rq[:, 64 * hf + 32:64 * hf + 64]), rk, ["hgb%d" % hf], 512, GA)
+            sends = []
+            for hf in range(2):
+                to_l(6 + hf, 64, ZA, T.hg, True, ["za", "hga%d" % hf, "hgb%d" % hf], 1024 * hf, 1024 * hf + 1024)
+                cp(xb[:, 144 + 64 * hf:208 + 64 * hf], PS[6 + hf][:, 0:64], ["ps%d" % (6 + hf)], ["ans%d%d" % (e, hf)], 64)
+                en = answer_engines(rank, hf)
+                trs = []
+                for s in halves(rank)[hf]:
+                    k = 144 + 16 * myslots.index(s)
+                    trs.append(RemoteDMATransfer(dst_ids=[dst(s)], dma_engine_mask=bits(en[T.cores[s]]), remote_sem=T.sem["an%d" % e],
+                                                 src=xb[:, k:k + 16], dst=xb[:, 16 * rank:16 * rank + 16]))
+                    sent[0] += len(en[T.cores[s]])
+                sends.append(op("pool", lambda trs=trs: g.remote_dma_fused(trs, local_sem=T.sem.sent), ["ans%d%d" % (e, hf)], (), 600))
+            lastw["anarr%d" % e] = ("an%d" % e, ans_in, sends, 5000)
+        if not last:
+            ts(T.fz[:], PS[1][:, 0:16], float(ZC), A.min, r=["ps1"], w=["fz"])
+            ts(S["fd"], T.fz[:], C["dum"], A.subtract, r=["fz", "c_dum"], w=["fd"])
+            tt(T.lg[:], T.tab[:].indirect(T.fz[:]), T.lm[:], A.mult, TAB + ["fz", "lm"], ["lg"], 256, GA)
+            mm(PS[3][:, 0:16], IF, idd, True, False, ["if", idk], ["ps3"], 256)
+            to_l(3, 16, Z1, T.lg, False, ["z1", "lg"])
+        if not ex:
+            cp(T.du[:], PS[3][:, 0:16], ["ps3"], ["du"])
+            codes()
+            cp(S["df"], T.du[:], ["du"], ["df"])
+            statics(t + 1)
+            if t >= 1:
+                columns()
+            continue
+        if not last:
+            cp(xb[:, 128:144], PS[3][:, 0:16], ["ps3"], ["dfxb0"])
+        columns()
+        ts(S["nw"], S["jj"], 5.0, A.is_lt, 16.0, A.mult, r=["jj"], w=["nw"])
+        tt(S["t1"], S["nw"], SI["q"], A.add, ["nw", "q"], ["t1"])
+        cp(T.wu[:], S["t1"], ["t1"], ["wu"])
+        ac(T.oh[:], T.w32[:].indirect(T.wu[:]), ["w32", "wu"], ["oh"], k=GA)
+        scan(T.cum[:], T.one[:], T.oh[:], A.mult, A.add, ["one", "oh"], ["cum"], 0.52)
+        ts(T.le[:], T.cum[:], 16.0, A.is_le, r=["cum"], w=["le"], n=128)
+        tt(T.svr[:], T.le[:], T.oh[:], A.mult, ["le", "oh"], ["svr"], 256)
+        to_l(1, 16, ZQ, T.svr, True, ["zq", "svr"])
+        ts(T.qs[:], PS[1][:, 0:16], 8.0, A.add, r=["ps1"], w=["qs"])
+        ts(S["sv"], PS[1][:, 0:16], 0.0, A.is_lt, r=["ps1"], w=["sv"])
+        tt(T.msk[:], T.qs[:].indirect(T.bc[:, 0:16]), T.ii[:], A.is_equal, ["qs", "bc", "ii"], ["msk"], 256, GA)
+        lowest(S["sv"], "sv", S["fd"], "fd")
+        tt(T.ag[:], xb[:].indirect(T.pu[:]), T.msk[:], A.mult,
+           ["anarr%d" % e, "ans%d0" % e, "ans%d1" % e, "ownxb%d" % e, "dfxb%d" % e, "pu", "msk"], ["ag"], 256, GA)
+        scan(T.asc[:], T.kp[:], T.ag[:], A.mult, A.add, ["kp", "ag"], ["asc"])
+        an = T.asc[:, 15:256:16]
+        if not last:
+            cp(T.du[:], an, ["asc"], ["du"])
+            codes()
+            cp(S["df"], T.du[:], ["du"], ["df"])
+            tt(S["jj"], S["jj"], S["sv"], A.subtract, ["jj", "sv"], ["jj"])
+            statics(t + 1)
+        cp(T.hl[:, 0:16], an, ["asc"], ["hl0"])
+        tt(T.hl[:, 16:32], an, T.hl[:, 0:16], A.subtract, ["asc", "hl0"], ["hl1"])
+        for hf in range(2):
+            tt(T.dg[:, 256 * hf:256 * hf + 256], T.hl[:].indirect(T.bc[:, 16 * hf:16 * hf + 16]), T.dia[:], A.mult, ["hl0", "hl1", "bc", "dia"], ["dg%d" % hf], 256, GA)
+        if not last:
+            mm(PS[4][:, 0:256], IKP, T.col[:], True, False, ["ikp", "col"], ["ps4"], 256)
+            mm(PS[4][:, 0:256], Z1(3), T.dg[:, 0:256], False, False, ["z1", "dg0"], ["ps4"], 256)
+            mm(PS[4][:, 0:256], Z1(7), T.dg[:, 256:512], False, True, ["z1", "dg1"], ["ps4"], 256)
+            ac(T.ncl[:], PS[4][:, 0:256], ["ps4"], ["ncl"])
+            scatters(T.tab, T.ncl, ["ncl"], TAB)
+            ac(T.col[:], T.tab[:].indirect(T.fz[:]), TAB + ["fz"], ["col"], k=GA)
+            continue
+        ts(T.nih[:], T.inh[:], -1.0, A.mult, 1.0, A.add, r=["in_%d" % k for k in range(11)], w=["nih"], n=176)
+        scan(T.csc[:], T.nih[:], T.idh[:], A.mult, A.add, ["nih"] + ["id_%d" % k for k in range(11)], ["csc"])
+        cp(S["yc"], T.csc[:, 10:176:11], ["csc"], ["ycs"])
+        dma("sync", T.yc[:], S["yc"], "o_yc", ["ycs"], ["yc"], 2500)
+        for q in range(4):
+            cs = slice(512 * q, 512 * q + 512)
+            b3, ba = (0, 3)[q % 2], (5, 7)[q % 2]
+            mm(PS[ba][0:32, :], SELY, T.tab[:, cs], True, True, ["sely"] + TAB, ["ps%d" % ba], 512)
+            mm(PS[b3][:], Z37(0), T.tab[:, cs], True, True, ["z37"] + TAB, ["ps%d" % b3], 512)
+            ac(T.y3[:, cs], PS[b3][:], ["ps%d" % b3], ["y3%d" % q], 512)
+            cp(T.ya[0:32, cs], PS[ba][0:32, :], ["ps%d" % ba], ["ya%d" % q], 512)
+        dma("sync", T.yt[:], T.ya[0:32, :], "o_ya", ["ya%d" % q for q in range(4)], ["yt"], 3000)
+        mm(PS[4][:, 0:256], Z1(0), T.dg[:, 0:256], True, False, ["z1", "dg0"], ["ps4"], 256)
+        mm(PS[4][:, 0:256], Z1(0), T.dg[:, 256:512], False, True, ["z1", "dg1"], ["ps4"], 256)
+        cp(T.anr[:], PS[4][:, 0:256], ["ps4"], ["anr"], 256)
+        Y3 = ["y3%d" % q for q in range(4)] + ["y3z"]
+        scatters(T.y3, T.anr, ["anr"], Y3)
+        dma("sync", T.yt[3:32:4, :], T.y3[0:128:16, 0:2048], "o_y3", Y3, ["yt"], 2500)
+
+    order = schedule(ops)
+    pos = {i: k for k, i in enumerate(order)}
+    known, plan = {e_: {} for e_ in Q}, []
+    for i in order:
+        o = ops[i]
+        kn = known[o["eng"]]
+        need = {}
+        for d in o["deps"]:
+            if isinstance(d, tuple):
+                need[d[0]] = d
+            else:
+                s = ops[d]["dma"] or ops[d]["eng"]
+                if s not in need or pos[d] > pos[need[s]]:
+                    need[s] = d
+        waits = []
+        for s, d in sorted(need.items(), key=lambda x: -(n_ops(x[1], pos))):
+            p_ = 0 if isinstance(d, tuple) else pos[d]
+            if kn.get(s, -1) < p_:
+                waits.append((s, d))
+                kn[s] = p_
+                if not isinstance(d, tuple):
+                    ops[d]["sig"] = True
+                    for s2, p2 in ops[d]["clock"].items():
+                        kn[s2] = max(kn.get(s2, -1), p2)
+        o["clock"] = dict(kn)
+        plan.append(waits)
+    cnt = {}
+    for i in order:
+        o = ops[i]
+        if o["sig"] and not o["dma"]:
+            cnt[o["eng"]] = cnt.get(o["eng"], 0) + 1
+            o["n"] = cnt[o["eng"]]
+    for i, waits in zip(order, plan):
+        o = ops[i]
+        for s, d in waits:
+            Q[o["eng"]].wait_ge(T.sem[s], d[1] if isinstance(d, tuple) else 16 if ops[d]["dma"] else ops[d]["n"])
+        call = o["fn"]()
+        if o["dma"]:
+            call.then_inc(T.sem[o["dma"]], 16)
+        elif o["sig"]:
+            call.then_inc(T.sem[o["eng"]], 1)
+    g.wait_ge(T.sem.sent, sent[0])
+    for s in ("o_y3", "o_yc", "o_yx"):
+        g.sync.wait_ge(T.sem[s], 16)
+
+
+def n_ops(d, pos):
+    return 0 if isinstance(d, tuple) else pos[d]

@@ -2,10 +2,11 @@ from concourse.bass import DstId, RemoteDMATransfer
 from concourse.mybir import AluOpType as A, ActivationFunctionType as AF
 
 F32, B16, I32, U16, F16 = "float32", "bfloat16", "int32", "uint16", "float16"
-N, NSUB, TW, ZC = 8, 10, 2080, 2064
-NA = 2
-NPOOL = 5
-GA, SC, MU, PE = 1.62, 4.0, 1.04, 0.6
+N, NSUB, TW, ZC = 8, 10, 2112, 2080
+NA = 4
+NPOOL = 7
+GA, SC, MU, PE = 1.3, 3.2, 0.83, 0.65
+RULE, SAME, CROSS, FIX = 0.5, 100, 200, 100
 
 
 def _s(shape, d):
@@ -15,29 +16,30 @@ def _s(shape, d):
 SCRATCH = {
     "sfs": _s([128, 3072], I32), "pws": _s([128, 2048], B16), "pw2": _s([128, 4096], B16), "otq": _s([128, 512], I32),
     "oth": _s([128, 512], B16), "otl": _s([128, 512], B16), "tab": _s([128, TW], B16), "xt": _s([128, 11 * 256], B16),
-    "stp": _s([128, 256], B16), "xa": _s([128, 256], B16), "xb": _s([128, 256], B16), "xc": _s([128, 256], B16),
+    "stp": _s([128, 256], B16), "xa": _s([128, 256], B16), "xc": _s([128, 256], B16),
     "c0s": _s([128, 16], I32), "ths": _s([128, 16], I32), "hws": _s([128, 2], B16), "hwa": _s([128, 16], B16),
     "xe": _s([128, 4096], B16), "gg": _s([128, 4096], B16), "p2": _s([128, 4096], B16), "pp": _s([128, 16, 16, 16], B16),
     "cod": _s([128, 256], U16), "sr": _s([128, 256], I32), "ind": _s([128, 256], B16), "mns": _s([128, 256], F32),
-    "cnt": _s([128, 256], B16), "sg": _s([128, 256], F16), "ee": _s([128, 256], B16), "lg": _s([128, 256], B16),
+    "cnt": _s([128, 256], B16), "sg": _s([128, 256], F16), "ee": _s([128, 512], B16), "lg": _s([128, 256], B16),
     "lm": _s([128, 256], B16), "col": _s([128, 256], B16), "mm": _s([128, 256], B16), "ncl": _s([128, 256], B16),
-    "frm": _s([128, 256], F32), "uu": _s([128, 512], B16), "hg": _s([128, 2048], B16), "dg": _s([128, 512], B16),
+    "frm": _s([128, 512], F32), "od": _s([128, 256], B16), "t0": _s([128, 256], B16), "bf": _s([128, 16], F32), "be": _s([128, 16], U16),
+    "uu": _s([128, 512], B16), "hg": _s([128, 2048], B16), "dg": _s([128, 512], B16),
     "ag": _s([128, 256], F32), "msk": _s([128, 256], F32), "ya": _s([128, 2048], F32), "y3": _s([128, TW], F32),
     "yxs": _s([128, 256], F32), "anr": _s([128, 256], F32), "oh": _s([128, 256], B16), "cum": _s([128, 256], B16),
-    "le": _s([128, 256], B16), "svr": _s([128, 256], B16), "asc": _s([128, 256], F32),
+    "le": _s([128, 256], B16), "svr": _s([128, 256], B16), "asc": _s([128, 256], F32), "dgf": _s([128, 256], F32),
     "req0": _s([128, 128], U16), "req1": _s([128, 128], U16), "xb0": _s([128, 272], F32), "xb1": _s([128, 272], F32),
     "inh": _s([128, 176], B16), "idh": _s([128, 176], F32), "nih": _s([128, 176], F32), "csc": _s([128, 176], F32),
-    "sm": _s([128, 20, 16], F32), "si": _s([128, 6, 16], I32), "nf": _s([128, 16], F32), "fc": _s([128, 16], F32),
+    "sm": _s([128, 20, 16], F32), "si": _s([128, 6, 16], I32), "fd": _s([128, 16], F32), "nf": _s([128, 16], F32), "fc": _s([128, 16], F32),
     "qs": _s([128, 16], F32), "hl": _s([128, 32], B16),
     "du": _s([128, 16], U16), "fz": _s([128, 16], U16), "iu": _s([128, 16], U16), "nu": _s([128, 16], U16),
-    "ju": _s([128, 16], U16), "ou": _s([128, 32], U16), "qo": _s([128, 32], U16), "wu": _s([128, 16], U16),
-    "pu": _s([128, 16], U16), "bc": _s([128, 32], U16),
+    "ju": _s([128, 16], U16), "ou": _s([128, 16], U16), "qo": _s([128, 32], U16), "wu": _s([128, 16], U16),
+    "pu": _s([128, 16], U16), "bc": _s([128, 32], U16), "b15": _s([128, 16], U16),
     "pi": _s([128, 8], I32), "ci": _s([128, 8], I32), "cf": _s([128, 32], F32), "ro": _s([128, 144], F32),
     "rx": _s([128, 4, 128], F32), "ii": _s([128, 256], B16), "kp": _s([128, 256], B16), "bg": _s([128, 256], B16),
-    "one": _s([128, 256], B16), "tri": _s([128, 256], B16), "dia": _s([128, 256], B16), "fh": _s([128, 512], B16),
-    "fl": _s([128, 512], B16), "zz": _s([128, 6, 144], B16), "zh": _s([128, 144], F16), "mb": _s([128, 14, 128], B16),
-    "mf": _s([128, 3, 128], F32), "hq": _s([128, 7, 144], B16), "w32": _s([128, 32], B16), "lt": _s([128, 16], B16),
-    "st": _s([128, 16], B16), "r3": _s([128, 16], B16),
+    "one": _s([128, 256], B16), "tri": _s([128, 512], B16), "dia": _s([128, 256], B16), "fh": _s([128, 512], B16),
+    "fl": _s([128, 512], B16), "zz": _s([128, 6, 144], B16), "zh": _s([128, 144], F16), "mb": _s([128, 16, 128], B16),
+    "mf": _s([128, 2, 128], F32), "hq": _s([128, 7, 144], B16), "w2": _s([128, 32], B16), "w32": _s([128, 32], B16), "lt": _s([128, 16], B16),
+    "st": _s([128, 16], B16), "r3": _s([128, 16], F32),
 }
 for _b in range(8):
     SCRATCH["ps%d" % _b] = ("psum", [128, 512], F32)
@@ -86,7 +88,7 @@ def schedule(ops):
                 for a in d[2]:
                     pre[a] = max(pre.get(a, 0), d[3])
             else:
-                pre[d] = max(pre.get(d, 0), ops[d]["lat"] + (60 if ops[d]["eng"] == o["eng"] else 110))
+                pre[d] = max(pre.get(d, 0), ops[d]["lat"] + (SAME if ops[d]["eng"] == o["eng"] else CROSS))
         for d in o["ord"]:
             pre.setdefault(d, 0)
         for d, l in pre.items():
@@ -107,10 +109,15 @@ def schedule(ops):
             if not l:
                 continue
             t0 = max(free.get(e, 0.0), min(ready[i] for i in l))
-            pick = max((i for i in l if ready[i] <= t0), key=lambda i: (prio[i], -i))
-            soon = [i for i in l if t0 < ready[i] < t0 + 0.4 * ops[pick]["cost"] and prio[i] > prio[pick] + 300]
-            if soon:
-                pick = max(soon, key=lambda i: (prio[i], -i))
+            pick = None
+            for p_ in sorted((i for i in l if ready[i] <= t0), key=lambda i: (-prio[i], i)):
+                soon = [i for i in l if t0 < ready[i] < t0 + RULE * ops[p_]["cost"] and prio[i] > prio[p_] + 300]
+                if not soon:
+                    pick = p_
+                    break
+                later = max(soon, key=lambda i: (prio[i], -i))
+            if pick is None:
+                pick = later
             st = max(t0, ready[pick])
             if best is None or st < best[0]:
                 best = (st, e, pick)
@@ -142,7 +149,7 @@ def rank_program(g, core, T, topo):
                 deps += [x for x in readers.get(k, []) if ops[x]["eng"] != eng]
         for k in w:
             for x in readers.get(k, []) + ([lastw[k]] if k in lastw else []):
-                (order if eng == "pe" and ops[x]["eng"] == "pe" else deps).append(x)
+                (order if k.startswith("ch") or (eng == "pe" and ops[x]["eng"] == "pe") else deps).append(x)
         ops.append({"eng": eng, "fn": fn, "deps": deps, "ord": order, "dma": dma, "sig": False, "cost": cost, "lat": lat})
         me_ = len(ops) - 1
         for k in r:
@@ -155,7 +162,7 @@ def rank_program(g, core, T, topo):
     v = g.vector
 
     def vc(n, k):
-        return 60 + (max(67.0, n * k) if k < GA else n * k)
+        return FIX + (max(67.0, n * k) if k < GA else n * k)
 
     def ts(out, in0, s1, o0, s2=None, o1=None, r=(), w=(), n=16, k=1.04):
         if o1 is None:
@@ -175,11 +182,11 @@ def rank_program(g, core, T, topo):
     def scan(out, d0, d1, o0, o1, r, w, k=1.04):
         op("dve", lambda: v.tensor_tensor_scan(out, d0, d1, 0.0, o0, o1), r, w, vc(256, k))
 
-    def ac(out, a, r, w, n=256, k=1.04, bias=None):
+    def ac(out, a, r, w, n=256, k=1.04, bias=None, f=AF.Identity, scale=1.0):
         if bias is None:
-            op("act", lambda: g.scalar.activation(out, a, AF.Copy), r, w, 15 + vc(n, k))
+            op("act", lambda: g.scalar.activation(out, a, AF.Copy, scale=scale), r, w, 15 + vc(n, k))
         else:
-            op("act", lambda: g.scalar.activation(out, a, AF.Identity, bias=bias), r, w, 15 + vc(n, k))
+            op("act", lambda: g.scalar.activation(out, a, f, bias=bias, scale=scale), r, w, 15 + vc(n, k))
 
     def mm(out, l, rh, st, sp, r, w, n=64):
         op("pe", lambda: g.tensor.matmul(out, l, rh, st, sp), r, w, max(64, n) * PE)
@@ -225,7 +232,7 @@ def rank_program(g, core, T, topo):
             sent[0] += len(en)
         me_ = op("pool", lambda: g.remote_dma_fused(trs, local_sem=T.sem.sent), r, (), cost)
         come = sum(len(off_engines(T, topo, T.cores[s])) for s in far) + sum(len(share(T, topo, T.cores[s], [core])[core]) for s in near)
-        lastw[key] = (sem, come, [me_], 6000)
+        lastw[key] = (sem, come, [me_], 10000)
 
     def halves(h):
         sl = slots(T, topo, h)
@@ -237,17 +244,15 @@ def rank_program(g, core, T, topo):
     ans_in = sum(len(answer_engines(h, hf)[core]) for h in peers for hf in range(2) if rank in halves(h)[hf])
     myslots = slots(T, topo, rank)
 
-    dma("sync", T.c0s[:], T.c0[:], "l_c0", [], ["c0s", "sq"], 2000)
-    dma("act", T.xt[:, 0:256], T.x0[:], "l_x0", [], ["x0"], 2200)
-    dma("act", T.pws[:], T.pw[:], "l_pw", [], ["pws"], 4000)
-    dma("sync", T.sfs[:], T.sf[:], "l_sf", [], ["sfs"], 9000)
-    dma("sync", T.otq[:], T.ot[:], "l_ot", [], ["otq"], 10000)
-    dma("act", T.stp[:], T.dr[:], "l_dr", [], ["stp"], 4500)
-    dma("act", T.ths[:], T.th[:], "l_th", [], ["ths"], 4500)
-    dma("sync", T.hws[:], T.hw[:], "l_hs", [], ["hws"], 10000)
-    dma("sync", T.hwa[:, 2 * rank:2 * rank + 2], T.hw[:], "l_hw", [], ["hwown"], 10000)
-    for a_, b_ in ((0, 3), (3, 4), (4, 7), (7, 8), (1, 2), (2, 5), (5, 6)):
-        ops[b_]["ord"].append(a_)
+    dma("sync", T.c0s[:], T.c0[:], "l_c0", [], ["c0s", "chs"], 2000)
+    dma("act", T.xt[:, 0:256], T.x0[:], "l_x0", [], ["x0", "chq"], 2200)
+    dma("act", T.pws[:], T.pw[:], "l_pw", [], ["pws", "chq"], 4000)
+    dma("sync", T.sfs[:], T.sf[:], "l_sf", [], ["sfs", "chs"], 9000)
+    dma("sync", T.otq[:], T.ot[:], "l_ot", [], ["otq", "chs"], 10000)
+    dma("act", T.stp[:], T.dr[:], "l_dr", [], ["stp", "chq"], 4500)
+    dma("act", T.ths[:], T.th[:], "l_th", [], ["ths", "chq"], 4500)
+    dma("sync", T.hws[:], T.hw[:], "l_hs", [], ["hws", "chs"], 10000)
+    dma("sync", T.hwa[:, 2 * rank:2 * rank + 2], T.hw[:], "l_hw", [], ["hwown", "chs"], 10000)
 
     iota(T.pi[:, 0:1], [[0, 1]], 0, 1, ["pi"], 1, False)
     iota(T.ro[:], [[1, 144]], 0, 0, ["ro"], 144)
@@ -268,40 +273,45 @@ def rank_program(g, core, T, topo):
     cp(T.cf[:, 0:6], T.ci[:, 0:6], ["ci%d" % k for k in range(6)], ["cf"])
     for k, n_ in enumerate(("r", "g16", "r3", "rq", "b2", "p")):
         colf(n_, k)
-    S = {n_: T.sm[:, k] for k, n_ in enumerate(("th", "thp", "nq", "df", "jj", "jm", "e5", "fd", "j2", "cfd", "nfd", "nin", "ub", "sv", "nw", "yc", "t1"))}
+    S = {n_: T.sm[:, k] for k, n_ in enumerate(("th", "thp", "nq", "df", "jj", "jm", "e5", "fr", "j2", "cfd", "nfd", "nin", "ub", "sv", "nw", "yc", "t1"))}
+    S["fd"] = T.fd[:]
     SI = {n_: T.si[:, k] for k, n_ in enumerate(("mk", "mk2", "fi", "q", "pr", "h"))}
-    IB, I4K, BM, BOF, IKP, SELY = T.mb[:, 0], T.mb[:, 6], T.mb[:, 7], T.mb[:, 8], T.mb[:, 9], T.mb[:, 10, 0:32]
-    IF, IF16, DD = T.mf[:, 0], T.mf[:, 1], T.mf[:, 2]
+    IB, I4K, BM, BOF, IKP, SELY, IM8 = T.mb[:, 0], T.mb[:, 6], T.mb[:, 7], T.mb[:, 8], T.mb[:, 9], T.mb[:, 10, 0:32], T.mb[:, 14]
+    I2, IF, ZF = T.mb[:, 15], T.mf[:, 0], T.mf[:, 1]
     R128 = T.ro[:, 0:128]
     for name, k, a, s1, o0, s2, o1 in (
             ("a", 6, "g16", 15.0, A.add, None, None), ("k", 7, "g16", "rq", A.add, 4.0, A.add), ("k8", 8, "g16", "rq", A.add, 12.0, A.add),
             ("ge4", 9, "r", 4.0, A.is_ge, None, None), ("mid", 10, "r", 12.0, A.is_lt, "ge4", A.mult), ("r256", 11, "r", 1.0 / 256, A.mult, None, None),
-            ("dum", 12, "r", 2048.0, A.add, None, None), ("lt8", 13, "r", 8.0, A.is_lt, None, None), ("d16", 14, "dum", 1.0 / 16, A.mult, None, None),
+            ("dum", 12, "r", 2048.0, A.add, None, None), ("lt8", 13, "r", 8.0, A.is_lt, None, None), ("r2", 14, "r", 2.0, A.mult, None, None),
             ("ge8", 15, "r", 8.0, A.is_ge, None, None), ("s1", 17, "b2", 2.0, A.add, "lt8", A.mult), ("rm8", 23, "r", -8.0, A.add, None, None),
             ("p1", 24, "r", 16.0, A.mult, 128.0, A.min), ("p2", 25, "r", float(rank), A.is_equal, float(256 - 16 * rank), A.mult),
-            ("y", 26, "g16", 0.25, A.mult, "r3", A.add), ("ndum", 28, "r", -1.0, A.mult, -2048.0, A.add)):
+            ("y", 26, "g16", 0.25, A.mult, "r3", A.add), ("dum16", 29, "r", 2064.0, A.add, None, None),
+            ("ndum16", 30, "r", -1.0, A.mult, -2064.0, A.add), ("ndum", 28, "r", -1.0, A.mult, -2048.0, A.add)):
         ts(colf(name, k), C[a], C.get(s1, s1), o0, C.get(s2, s2), o1, r=["cf"] + ["c_" + x for x in (a, s1, s2) if isinstance(x, str)], w=["c_" + name])
 
     def eq(out, row, rk, a, s2, w, n):
         ts(out, row, C.get(a, a), A.is_equal, C.get(s2, s2), None if s2 is None else A.mult,
            r=["cf", rk] + ["c_" + x for x in (a, s2) if isinstance(x, str)], w=[w], n=n)
+
+    def scaled(out, a, ak, s, w, n):
+        ac(out, a, [ak] + (["c_" + s] if isinstance(s, str) else []), [w], n, scale=C.get(s, s))
     eq(T.r3[:], T.ro[:, 0:16], "ro", "r3", None, "r3", 16)
     eq(IB, R128, "ro", "p", None, "ib", 128)
     eq(T.hq[:, 4], T.ro[:], "ro", "k", None, "hq4", 144)
     eq(T.hq[:, 5], T.ro[:], "ro", "k8", "mid", "hq5", 144)
     eq(T.zz[:, 0], T.ro[:], "ro", "a", 32.0, "z32", 144)
     eq(T.zz[:, 1], T.ro[:], "ro", "a", None, "z1", 144)
-    eq(T.zz[:, 2], T.ro[:], "ro", "a", 4096.0, "z4k", 144)
     eq(T.zh[:], T.ro[:], "ro", "a", None, "zh", 144)
+    eq(T.w2[:], T.ro[:, 0:32], "ro", "r2", None, "w2", 32)
     eq(T.w32[:], T.ro[:, 0:32], "ro", "r", None, "w32", 32)
-    eq(I4K, R128, "ro", "p", 4096.0, "i4k", 128)
-    eq(IF, R128, "ro", "p", None, "if", 128)
-    eq(IF16, R128, "ro", "p", 1.0 / 16, "if16", 128)
-    eq(DD, R128, "ro", "p", "d16", "dd", 128)
+    for out, s, w in ((I4K, 4096.0, "i4k"), (IF, 1.0, "if"), (I2, 2.0, "i2"), (IM8, -8.0, "im8")):
+        scaled(out, IB, "ib", s, w, 128)
+    scaled(T.zz[:, 2], T.zz[:, 1], "z1", 4096.0, "z4k", 144)
+    scaled(ZF, Z1(0), "z1", 1.0, "zf", 128)
     tt(T.hq[:, 6], T.hq[:, 4], T.hq[:, 5], A.add, ["hq4", "hq5"], ["hq6"], 144)
     for q in range(4):
         ts(T.mb[:, 1 + q], T.ii[:, 0:128], 8.0, A.is_equal, T.mb[:, 0, q:q + 1], A.mult, r=["ii", "ib"], w=["s8%d" % q])
-        ts(T.hq[:, q], T.hq[:, 6], T.r3[:, q:q + 1], A.mult, r=["hq6", "r3"], w=["hq%d" % q])
+        ac(T.hq[:, q], T.hq[:, 6], ["hq6", "r3"], ["hq%d" % q], 144, scale=T.r3[:, q:q + 1])
     ts(T.mb[:, 5], T.ii[:, 0:128], 11.0, A.is_equal, T.mb[:, 0, 0:1], A.mult, r=["ii", "ib"], w=["s11"])
     tt(colf("m12", 16), T.r3[:, 1:2], T.r3[:, 2:3], A.add, ["r3"], ["c_m12"])
     ts(colf("s2", 18), C["m12"], 4.0, A.mult, -1.0, A.add, r=["c_m12"], w=["c_s2"])
@@ -317,16 +327,21 @@ def rank_program(g, core, T, topo):
         tt(colf(name, k), T.w32[:, a:a + 1], T.w32[:, b:b + 1], A.add, ["w32"], ["c_" + name])
     ts(colf("n37", 27), C["a37"], 0.0, A.is_equal, r=["c_a37"], w=["c_n37"])
     eq(BOF, T.rx[:, 3], "rx3", "g16", "f2", "bof", 128)
-    eq(T.zz[:, 3], T.ro[:], "ro", "a", "a04", "za", 144)
-    eq(T.zz[:, 4], T.ro[:], "ro", "a", "rm8", "zq", 144)
-    eq(T.zz[:, 5], T.ro[:], "ro", "a", "a37", "z37", 144)
+    for k, s, w in ((3, "a04", "za"), (4, "rm8", "zq"), (5, "a37", "z37")):
+        scaled(T.zz[:, k], T.zz[:, 1], "z1", s, w, 144)
     eq(SELY, T.ro[:, 0:32], "ro", "y", "lt8", "sely", 32)
-    eq(IKP, R128, "ro", "p", "n37", "ikp", 128)
+    scaled(IKP, IB, "ib", "n37", "ikp", 128)
     ts(T.dia[:], T.ii[:], C["r"], A.is_equal, r=["ii", "cf"], w=["dia"], n=128)
-    ts(T.tri[:], T.ii[:], C["r"], A.is_le, -8192.0, A.mult, r=["ii", "cf"], w=["tri"], n=128)
+    iota(T.od[:], [[0, 8], [-16, 2], [0, 16]], 0, 0, ["od"], 256)
+    iota(T.bf[:], [[2, 8], [0, 2]], 0, 0, ["bf"], 16)
+    cp(T.be[:], T.bf[:], ["bf"], ["be"])
+    ts(T.t0[:], T.ii[:], C["r"], A.is_le, -8192.0, A.mult, r=["ii", "cf"], w=["t0"], n=128)
+    tt(T.tri[:, 0:256], T.t0[:], T.od[:], A.add, ["t0", "od"], ["tri"], 256)
+    ts(T.tri[:, 256:512], T.od[:], 0.0, A.is_equal, -8192.0, A.mult, r=["od"], w=["tri2"], n=128)
     ts(T.kp[:], T.ii[:], 0.0, A.is_gt, r=["ii"], w=["kp"], n=128)
     ts(T.bg[:], T.ii[:], 0.0, A.is_equal, 1.0e6, A.mult, r=["ii"], w=["bg"], n=128)
     ts(T.pu[:], T.ro[:, 0:16], C["p1"], A.add, C["p2"], A.add, r=["ro", "c_p1", "c_p2"], w=["pu"])
+    ts(T.b15[:], T.ro[:, 0:16], 16.0, A.mult, 15.0, A.add, r=["ro"], w=["b15"])
     ts(T.lt[:], T.r3[:], C["lt8"], A.mult, r=["r3", "c_lt8"], w=["lt"])
     ts(S["nq"], T.ro[:, 0:16], 1.0 / 16, A.mult, C["r256"], A.add, r=["ro", "c_r256"], w=["nq"])
     cp(T.bc[:], T.ro[:, 0:32], ["ro"], ["bc"])
@@ -337,9 +352,7 @@ def rank_program(g, core, T, topo):
     ms(T.one[:], 1.0, ["one"], 256)
     ms(T.ju[:], 0, ["ju"])
     ms(S["jm"], 1.0, ["jm"])
-    ms(T.xt[:, 512:2816], 0.0, ["x%d" % n_ for n_ in range(2, 11)], 2304)
     ms(T.inh[:, 0:176:11], 1.0, ["in_0"])
-    ms(T.ou[:], 0, ["ou"])
     ms(T.tab[:, 2048:TW], 0.0, ["tabz"])
     ms(T.y3[:, 2048:TW], 0.0, ["y3z"])
     ms(T.xb1[:, 128:144], 0.0, ["dfxb1"])
@@ -354,15 +367,15 @@ def rank_program(g, core, T, topo):
     cp(T.oth[:], T.otq[:], ["otq"], ["oth"], 512)
     tt(T.otl[:], T.otq[:], T.oth[:], A.subtract, ["otq", "oth"], ["otl"], 1024)
     for q in range(4):
-        k = ["ps%d" % (4 + q)]
-        mm(PS[4 + q][:], T.mb[:, 1 + q], T.fh[:], True, False, ["s8%d" % q, "fh"], k, 512)
-        mm(PS[4 + q][:], T.mb[:, 5], T.fl[:], False, False, ["s11", "fl"], k, 512)
-        mm(PS[4 + q][:], T.hq[:, q, 4:132], T.oth[:], False, False, ["hq%d" % q, "oth"], k, 512)
-        mm(PS[4 + q][:], T.hq[:, q, 0:128], T.otl[:], False, True, ["hq%d" % q, "otl"], k, 512)
+        k = ["ps%d" % (3 + q)]
+        mm(PS[3 + q][:], T.mb[:, 1 + q], T.fh[:], True, False, ["s8%d" % q, "fh"], k, 512)
+        mm(PS[3 + q][:], T.mb[:, 5], T.fl[:], False, False, ["s11", "fl"], k, 512)
+        mm(PS[3 + q][:], T.hq[:, q, 4:132], T.oth[:], False, False, ["hq%d" % q, "oth"], k, 512)
+        mm(PS[3 + q][:], T.hq[:, q, 0:128], T.otl[:], False, True, ["hq%d" % q, "otl"], k, 512)
         if q % 2:
-            ac(T.tab[:, 512 * q:512 * q + 512], PS[4 + q][:], k, ["tab%d" % q], 512)
+            ac(T.tab[:, 512 * q:512 * q + 512], PS[3 + q][:], k, ["tab%d" % q], 512)
         else:
-            cp(T.tab[:, 512 * q:512 * q + 512], PS[4 + q][:], k, ["tab%d" % q], 512)
+            cp(T.tab[:, 512 * q:512 * q + 512], PS[3 + q][:], k, ["tab%d" % q], 512)
     mm(PS[6][:, 0:128], T.mb[:, 11], T.mb[:, 13], True, True, ["m11", "m13"], ["ps6"], 128)
     cp(BM, PS[6][:, 0:128], ["ps6"], ["bm"], 128)
     TAB = ["tab%d" % q for q in range(4)] + ["tabz"]
@@ -372,37 +385,47 @@ def rank_program(g, core, T, topo):
         for i in range(16):
             o = T.xe[:, i:4096:16]
             if i < NPOOL:
-                op("pool", lambda o=o: g.affine_select(o, src, [[0, 256]], A.is_ge, 0.0, 0, 0), [key], ["xe%d" % i], 700)
+                op("pool", lambda o=o: g.affine_select(o, src, [[0, 256]], A.is_ge, 0.0, 0, 0), [key], ["xe%d" % i, "chp"], 700)
             elif i < 16 - nd:
-                ac(o, src, [key], ["xe%d" % i])
+                ac(o, src, [key], ["xe%d" % i, "cha"])
             else:
                 cp(o, src, [key], ["xe%d" % i], 128)
 
     def next_x(n):
         a, b = T.xt[:, 256 * (n - 1):256 * n], T.xt[:, 256 * n:256 * n + 256]
-        tt(T.xa[:], a, T.stp[:], A.add, ["x%d" % (n - 1), "stp"], ["xa"], 256)
-        ts(T.xb[:], T.xa[:], 16.0, A.is_ge, -16.0, A.mult, r=["xa"], w=["xb"], n=128)
-        tt(b, T.xa[:], T.xb[:], A.add, ["xa", "xb", "xread"], ["x%d" % n], 256)
+        o, k = PS[7][:, 0:256], ["ps7"]
+        mm(o, IB, a, True, False, ["ib", "x%d" % (n - 1)], k, 256)
+        mm(o, IB, T.stp[:], False, True, ["ib", "stp"], k, 256)
+        ac(T.xa[:], o, k, ["xa"], bias=-15.5, f=AF.Sign)
+        mm(o, IB, a, True, False, ["ib", "x%d" % (n - 1)], k, 256)
+        mm(o, IB, T.stp[:], False, False, ["ib", "stp"], k, 256)
+        mm(o, IM8, T.xa[:], False, True, ["im8", "xa"], k, 256)
+        ac(b, o, k, ["x%d" % n], bias=-8.0)
 
     def place(out, n, w):
         ac(out, T.xt[:, 0:256 * n + 256].indirect(T.nu[:]), ["x%d" % k for k in range(n + 1)] + ["nu"], w, k=GA)
 
     def scatters(win, src, rk, wk):
-        for c in range(15, -1, -1):
-            cp(win[:].indirect(T.ou[:, 2 * c:2 * c + 1]), src[:, 16 * c:16 * c + 16], ["ou"] + rk, wk, 16, SC)
+        for c in range(7, -1, -1):
+            cp(win[:].indirect(T.ou[:, 2 * c:2 * c + 2]), src[:, 32 * c:32 * c + 32], ["ou0", "ou1"] + rk, wk, 32, SC)
 
     def lowest(flag, fk, base, bk):
         tt(T.fc[:], flag, base, A.mult, [fk, bk], ["fc"])
-        tt(T.ee[:], T.fc[:].indirect(T.bc[:, 0:16]), T.frm[:], A.is_equal, ["fc", "bc", "frm"], ["ee"], 256, GA)
         mm(PS[2][:, 0:16], IF, T.fc[:], True, False, ["if", "fc"], ["ps2"], 256)
-        to_l(2, 16, Z4K, T.ee, False, ["z4k", "ee"])
-        ts(T.ou[:, 0:32:2], PS[2][:, 0:16], 0.0, A.min, C["dum"], A.add, r=["ps2", "c_dum"], w=["ou"])
+        for h_, off in enumerate((T.bc[:, 0:16], T.be[:])):
+            cs = slice(256 * h_, 256 * h_ + 256)
+            tt(T.ee[:, cs], T.fc[:].indirect(off), T.frm[:, cs], A.is_equal, ["fc", "bc", "be", "frm"], ["ee%d" % h_], 256, GA)
+            for r_ in range(16):
+                mm(PS[2][:, 0:16], Z4K(r_), T.ee[:, 256 * h_ + r_:256 * h_ + 256:16], False, h_ == 1 and r_ == 15, ["z4k", "ee%d" % h_], ["ps2"])
+        for h_, n_ in enumerate(("dum", "dum16")):
+            ts(T.ou[:, h_:16:2], PS[2][:, h_:16:2], 0.0, A.min, C[n_], A.add, r=["ps2", "c_" + n_], w=["ou%d" % h_])
 
     def columns():
         ac(T.col[:], T.tab[:].indirect(T.fz[:]), TAB + ["fz"], ["col"], k=GA)
-        mm(PS[5][:, 0:256], IB, T.tri[:], True, False, ["ib", "tri"], ["ps5"], 256)
-        mm(PS[5][:, 0:256], BOF, T.col[:], False, True, ["bof", "col"], ["ps5"], 256)
-        ac(T.frm[:], PS[5][:, 0:256], ["ps5", "c_ndum"], ["frm"], bias=C["ndum"])
+        mm(PS[5][:], IB, T.tri[:], True, False, ["ib", "tri", "tri2"], ["ps5"], 512)
+        mm(PS[5][:, 0:256], BOF, T.col[:], False, False, ["bof", "col"], ["ps5"], 256)
+        mm(PS[5][:, 256:512], BOF, T.col[:], False, True, ["bof", "col"], ["ps5"], 256)
+        ac(T.frm[:], PS[5][:], ["ps5", "c_ndum"], ["frm"], 512, bias=C["ndum"])
 
     def swapped():
         tt(T.mm[:], T.st[:].indirect(T.ju[:]), T.col[:], A.mult, ["st", "ju", "col"], ["mm"], 256, GA)
@@ -415,13 +438,13 @@ def rank_program(g, core, T, topo):
         ts(S["jm"], S["jj"], 1.0, A.add, 5.0, A.min, r=["jj"], w=["jm"])
         if t < NSUB - 1:
             ac(T.lm[:], T.lt[:].indirect(T.ju[:]), ["lt", "ju"], ["lm"], k=GA)
-            ts(T.nf[:], S["jj"], 1.0, A.is_ge, 16.0, A.mult, r=["jj"], w=["nf"])
-            tt(S["nfd"], T.nf[:], S["fd"], A.mult, ["nf", "fd"], ["nfd"])
+            ac(T.nf[:], S["jj"], ["jj"], ["nf"], 16, bias=0.0, f=AF.Sign)
+            tt(S["nfd"], T.nf[:], S["fr"], A.mult, ["nf", "fr"], ["nfd"])
         if t >= 2:
             ts(S["j2"], S["jj"], 2.0, A.is_ge, r=["jj"], w=["j2"])
             tt(S["cfd"], S["j2"], S["fd"], A.mult, ["j2", "fd"], ["cfd"])
         if t >= 5:
-            ts(S["e5"], S["jj"], 5.0, A.is_equal, 99.0, A.mult, r=["jj"], w=["e5"])
+            ac(S["e5"], S["jj"], ["jj"], ["e5"], 16, bias=-396.0, f=AF.Relu, scale=99.0)
             tt(S["thp"], S["e5"], S["th"], A.add, ["e5", "th"], ["thp"])
 
     def request(e):
@@ -444,7 +467,7 @@ def rank_program(g, core, T, topo):
         cp(T.cod[:], T.sfs[:].indirect(T.du[:]), ["sfs", "du"], ["cod"], 256, GA)
 
     def test():
-        mm(PS[0][:, 0:256], IB, T.ii[:], True, False, ["ib", "ii"], ["ps0"], 256)
+        mm(PS[0][:, 0:256], I2, T.ii[:], True, False, ["i2", "ii"], ["ps0"], 256)
         for a in range(0, NA, 2):
             b = min(a + 2, NA)
             tt(T.p2[:, 256 * a:256 * b], T.pw2[:].indirect(T.cod[:, 16 * a:16 * b]), T.xe[:, 256 * a:256 * b], A.mult, PW2 + ["cod"] + XE, ["pp%d" % a], 256 * (b - a), GA)
@@ -454,12 +477,18 @@ def rank_program(g, core, T, topo):
         cuts = list(range(NA, 14, 2)) + [14, 15, 16]
         start, keys = NA, []
         for a, b in zip(cuts[:-1], cuts[1:]):
-            ac(T.gg[:, 256 * a:256 * b], T.pw2[:].indirect(T.cod[:, 16 * a:16 * b]), PW2 + ["cod"], ["gg%d" % a], 256 * (b - a), GA)
-            tt(T.pp[:, a:b], T.gg[:, 256 * a:256 * b], T.xe[:, 256 * a:256 * b], A.mult, ["gg%d" % a] + XE, ["pp%d" % a], 256 * (b - a))
-            keys.append("pp%d" % a)
+            ac(T.gg[:, 256 * a:256 * b], T.pw2[:].indirect(T.cod[:, 16 * a:16 * b]), PW2 + ["cod"], ["gg%d" % a, "cha"], 256 * (b - a), GA)
+            if b == 16:
+                for h_ in range(2):
+                    cs = slice(256 * a + 128 * h_, 256 * a + 128 * h_ + 128)
+                    tt(T.pp[:, a, 8 * h_:8 * h_ + 8], T.gg[:, cs], T.xe[:, cs], A.mult, ["gg%d" % a] + XE, ["pl%d" % h_], 128)
+            else:
+                tt(T.pp[:, a:b], T.gg[:, 256 * a:256 * b], T.xe[:, 256 * a:256 * b], A.mult, ["gg%d" % a] + XE, ["pp%d" % a], 256 * (b - a))
+                keys.append("pp%d" % a)
             if (16 - b) % 4 == 0:
                 for r_ in range(16):
-                    mm(PS[0][:, 16 * start:16 * b], Z32(r_), T.pp[:, start:b, r_, :], False, b == 16 and r_ == 15, ["z32"] + keys, ["ps0"])
+                    mm(PS[0][:, 16 * start:16 * b], Z32(r_), T.pp[:, start:b, r_, :], False, b == 16 and r_ == 15,
+                       ["z32"] + keys + (["pl%d" % (r_ // 8)] if b == 16 else []), ["ps0"])
                 start, keys = b, []
 
     expand(T.xt[:, 0:256], "x0", 0)
@@ -491,7 +520,7 @@ def rank_program(g, core, T, topo):
             dma("sync", T.yx[:], T.yxs[:], "o_yx", ["yxs"], ["yx"], 2500)
         else:
             place(T.xc[:], t + 1, ["xc"])
-            expand(T.xc[:], "xc", 0 if re_ else 4)
+            expand(T.xc[:], "xc", 0 if re_ else 2)
             scan(T.mns[:], T.bg[:], PS[0][:, 0:256], A.add, A.min, ["bg", "ps0"], ["mns"])
             if t == 0:
                 cp(SI["mk"], T.mns[:, 15:256:16], ["mns"], ["mk"])
@@ -499,11 +528,10 @@ def rank_program(g, core, T, topo):
                 tt(SI["mk"], T.mns[:, 15:256:16], T.nf[:], A.add, ["mns", "nf"], ["mk"])
             ts(SI["mk2"], SI["mk"], 31, A.bitwise_and, r=["mk"], w=["mk2"])
             cp(T.iu[:], SI["mk2"], ["mk2"], ["iu"])
-            tt(T.sg[:], T.w32[:].indirect(T.iu[:]), T.sr[:], A.mult, ["w32", "iu", "sr"], ["sg"], 256, GA)
+            tt(T.sg[:], T.w2[:].indirect(T.iu[:]), T.sr[:], A.mult, ["w2", "iu", "sr"], ["sg"], 256, GA)
             mm(PS[1][:, 0:16], I4K, ins, True, False, ["i4k", ik], ["ps1"])
             if t > 0:
-                mm(PS[1][:, 0:16], IF16, S["nfd"], False, False, ["if16", "nfd"], ["ps1"], 256)
-                mm(PS[1][:, 0:16], DD, T.nf[:], False, False, ["dd", "nf"], ["ps1"], 256)
+                mm(PS[1][:, 0:16], IF, S["nfd"], False, False, ["if", "nfd"], ["ps1"], 256)
             to_l(1, 16, ZH, T.sg, False, ["zh", "sg"])
         if re_:
             lowest(ins, ik, S["cfd"], "cfd")
@@ -529,14 +557,16 @@ def rank_program(g, core, T, topo):
             lastw["anarr%d" % e] = ("an%d" % e, ans_in, sends, 5000)
         if not last:
             ts(T.fz[:], PS[1][:, 0:16], float(ZC), A.min, r=["ps1"], w=["fz"])
-            ts(S["fd"], T.fz[:], C["dum"], A.subtract, r=["fz", "c_dum"], w=["fd"])
+            for h_, n_ in enumerate(("ndum", "ndum16")):
+                ac(T.fd[:, h_:16:2], PS[1][:, h_:16:2], ["ps1", "c_" + n_], ["fd"], 16, bias=C[n_])
+            ac(S["fr"], PS[1][:, 0:16], ["ps1"], ["fr"], 16)
             tt(T.lg[:], T.tab[:].indirect(T.fz[:]), T.lm[:], A.mult, TAB + ["fz", "lm"], ["lg"], 256, GA)
             mm(PS[3][:, 0:16], IF, idd, True, False, ["if", idk], ["ps3"], 256)
             to_l(3, 16, Z1, T.lg, False, ["z1", "lg"])
         if not ex:
             cp(T.du[:], PS[3][:, 0:16], ["ps3"], ["du"])
             codes()
-            cp(S["df"], T.du[:], ["du"], ["df"])
+            ac(S["df"], PS[3][:, 0:16], ["ps3"], ["df"], 16)
             statics(t + 1)
             if t >= 1:
                 columns()
@@ -563,14 +593,13 @@ def rank_program(g, core, T, topo):
         if not last:
             cp(T.du[:], an, ["asc"], ["du"])
             codes()
-            cp(S["df"], T.du[:], ["du"], ["df"])
+            ac(S["df"], an, ["asc"], ["df"], 16)
             tt(S["jj"], S["jj"], S["sv"], A.subtract, ["jj", "sv"], ["jj"])
             statics(t + 1)
-        cp(T.hl[:, 0:16], an, ["asc"], ["hl0"])
-        tt(T.hl[:, 16:32], an, T.hl[:, 0:16], A.subtract, ["asc", "hl0"], ["hl1"])
-        for hf in range(2):
-            tt(T.dg[:, 256 * hf:256 * hf + 256], T.hl[:].indirect(T.bc[:, 16 * hf:16 * hf + 16]), T.dia[:], A.mult, ["hl0", "hl1", "bc", "dia"], ["dg%d" % hf], 256, GA)
-        if not last:
+            cp(T.hl[:, 0:16], an, ["asc"], ["hl0"])
+            tt(T.hl[:, 16:32], an, T.hl[:, 0:16], A.subtract, ["asc", "hl0"], ["hl1"])
+            for hf in range(2):
+                tt(T.dg[:, 256 * hf:256 * hf + 256], T.hl[:].indirect(T.bc[:, 16 * hf:16 * hf + 16]), T.dia[:], A.mult, ["hl0", "hl1", "bc", "dia"], ["dg%d" % hf], 256, GA)
             mm(PS[4][:, 0:256], IKP, T.col[:], True, False, ["ikp", "col"], ["ps4"], 256)
             mm(PS[4][:, 0:256], Z1(3), T.dg[:, 0:256], False, False, ["z1", "dg0"], ["ps4"], 256)
             mm(PS[4][:, 0:256], Z1(7), T.dg[:, 256:512], False, True, ["z1", "dg1"], ["ps4"], 256)
@@ -588,13 +617,19 @@ def rank_program(g, core, T, topo):
             mm(PS[ba][0:32, :], SELY, T.tab[:, cs], True, True, ["sely"] + TAB, ["ps%d" % ba], 512)
             mm(PS[b3][:], Z37(0), T.tab[:, cs], True, True, ["z37"] + TAB, ["ps%d" % b3], 512)
             ac(T.y3[:, cs], PS[b3][:], ["ps%d" % b3], ["y3%d" % q], 512)
-            cp(T.ya[0:32, cs], PS[ba][0:32, :], ["ps%d" % ba], ["ya%d" % q], 512)
+            if q % 2:
+                ac(T.ya[0:32, cs], PS[ba][0:32, :], ["ps%d" % ba], ["ya%d" % q], 512)
+            else:
+                cp(T.ya[0:32, cs], PS[ba][0:32, :], ["ps%d" % ba], ["ya%d" % q], 512)
         dma("sync", T.yt[:], T.ya[0:32, :], "o_ya", ["ya%d" % q for q in range(4)], ["yt"], 3000)
-        mm(PS[4][:, 0:256], Z1(0), T.dg[:, 0:256], True, False, ["z1", "dg0"], ["ps4"], 256)
-        mm(PS[4][:, 0:256], Z1(0), T.dg[:, 256:512], False, True, ["z1", "dg1"], ["ps4"], 256)
-        cp(T.anr[:], PS[4][:, 0:256], ["ps4"], ["anr"], 256)
+        tt(T.dgf[:], T.asc[:].indirect(T.b15[:]), T.dia[:], A.mult, ["asc", "b15", "dia"], ["dgf"], 256, GA)
+        for hf in (1, 0):
+            cs = slice(128 * hf, 128 * hf + 128)
+            mm(PS[(4, 6)[hf]][:, 0:128], ZF, T.dgf[:, cs], True, True, ["zf", "dgf"], ["ps%d" % (4, 6)[hf]], 512)
+            cp(T.anr[:, cs], PS[(4, 6)[hf]][:, 0:128], ["ps%d" % (4, 6)[hf]], ["anr%d" % hf], 128)
         Y3 = ["y3%d" % q for q in range(4)] + ["y3z"]
-        scatters(T.y3, T.anr, ["anr"], Y3)
+        for c in range(7, -1, -1):
+            cp(T.y3[:].indirect(T.ou[:, 2 * c:2 * c + 2]), T.anr[:, 32 * c:32 * c + 32], ["ou0", "ou1", "anr%d" % (c // 4)], Y3, 32, SC)
         dma("sync", T.yt[3:32:4, :], T.y3[0:128:16, 0:2048], "o_y3", Y3, ["yt"], 2500)
 
     order = schedule(ops)
@@ -612,8 +647,8 @@ def rank_program(g, core, T, topo):
                 if s not in need or pos[d] > pos[need[s]]:
                     need[s] = d
         waits = []
-        for s, d in sorted(need.items(), key=lambda x: -(n_ops(x[1], pos))):
-            p_ = 0 if isinstance(d, tuple) else pos[d]
+        for s, d in sorted(need.items(), key=lambda x: -place_of(x[1], pos)):
+            p_ = place_of(d, pos)
             if kn.get(s, -1) < p_:
                 waits.append((s, d))
                 kn[s] = p_
@@ -643,5 +678,5 @@ def rank_program(g, core, T, topo):
         g.sync.wait_ge(T.sem[s], 16)
 
 
-def n_ops(d, pos):
+def place_of(d, pos):
     return 0 if isinstance(d, tuple) else pos[d]

@@ -1,12 +1,21 @@
+import numpy as np
 from concourse.bass import DstId, RemoteDMATransfer
 from concourse.mybir import AluOpType as A, ActivationFunctionType as AF
 
 F32, B16, I32, U16, F16 = "float32", "bfloat16", "int32", "uint16", "float16"
-N, NSUB, TW, ZC = 8, 10, 2112, 2080
-NA = 4
-NPOOL = 7
-GA, SC, MU, PE = 1.3, 3.2, 0.83, 0.65
-RULE, SAME, CROSS, FIX = 0.5, 100, 200, 100
+N, NSUB, TW = 8, 10, 2096
+STAGES = ((6, 16, 2, 0, "dve"), (0, 6, 2, 1, "act"))
+GATHERS = (("act", 14, 16), ("dve", 12, 14), ("dve", 10, 12), ("act", 8, 10), ("dve", 6, 8), ("act", 4, 6), ("act", 2, 4), ("act", 0, 2))
+LATER = 14
+SPANS = []
+SHIFT = 1500
+CODES = ((12, 16), (0, 12))
+NPOOL = (8, 4)
+ROUND = 12582912.0
+GA, SC, CY, PE = 1.33, 3.2, 0.85, 0.43
+RULE, SAME, CROSS, FIX = 0.5, 100, 130, 50
+PASSES, ORDER = 500, {}
+LOADS, ASK, ANSWER = (2500, 4500, 11000, 12000), 3000, 3000
 
 
 def _s(shape, d):
@@ -18,27 +27,28 @@ SCRATCH = {
     "oth": _s([128, 512], B16), "otl": _s([128, 512], B16), "tab": _s([128, TW], B16), "xt": _s([128, 11 * 256], B16),
     "stp": _s([128, 256], B16), "xa": _s([128, 256], B16), "xc": _s([128, 256], B16),
     "c0s": _s([128, 16], I32), "ths": _s([128, 16], I32), "hws": _s([128, 2], B16), "hwa": _s([128, 16], B16),
-    "xe": _s([128, 4096], B16), "gg": _s([128, 4096], B16), "p2": _s([128, 4096], B16), "pp": _s([128, 16, 16, 16], B16),
-    "cod": _s([128, 256], U16), "sr": _s([128, 256], I32), "ind": _s([128, 256], B16), "mns": _s([128, 256], F32),
-    "cnt": _s([128, 256], B16), "sg": _s([128, 256], F16), "ee": _s([128, 512], B16), "lg": _s([128, 256], B16),
-    "lm": _s([128, 256], B16), "col": _s([128, 256], B16), "mm": _s([128, 256], B16), "ncl": _s([128, 256], B16),
-    "frm": _s([128, 512], F32), "od": _s([128, 256], B16), "t0": _s([128, 256], B16), "bf": _s([128, 16], F32), "be": _s([128, 16], U16),
+    "xd": _s([128, 4096], B16), "gg": _s([128, 4096], B16), "kin": _s([128, 32, 16], B16),
+    "cod": _s([128, 256], U16), "sr": _s([128, 256], I32), "ind": _s([128, 512], B16), "mns": _s([128, 512], F32),
+    "tot": _s([128, 512], B16), "sg": _s([128, 256], F16), "ee": _s([128, 384], B16), "thr": _s([128, 384], B16), "lg": _s([128, 256], B16),
+    "lm": _s([128, 512], B16), "col": _s([128, 256], B16), "mm": _s([128, 256], B16), "ncl": _s([128, 256], B16),
+    "t0": _s([128, 256], B16), "t1": _s([128, 256], B16), "t2": _s([128, 512], B16), "t3": _s([128, 512], B16), "thq": _s([128, 16], F32),
     "uu": _s([128, 512], B16), "hg": _s([128, 2048], B16), "dg": _s([128, 512], B16),
-    "ag": _s([128, 256], F32), "msk": _s([128, 256], F32), "ya": _s([128, 2048], F32), "y3": _s([128, TW], F32),
+    "ag": _s([128, 256], F32), "ya": _s([128, 2048], F32), "y3": _s([128, TW], F32),
     "yxs": _s([128, 256], F32), "anr": _s([128, 256], F32), "oh": _s([128, 256], B16), "cum": _s([128, 256], B16),
-    "le": _s([128, 256], B16), "svr": _s([128, 256], B16), "asc": _s([128, 256], F32), "dgf": _s([128, 256], F32),
-    "req0": _s([128, 128], U16), "req1": _s([128, 128], U16), "xb0": _s([128, 272], F32), "xb1": _s([128, 272], F32),
+    "le": _s([128, 256], B16), "svr": _s([128, 256], B16), "asc": _s([128, 256], F32),
+    "req0": _s([128, 128], U16), "req1": _s([128, 128], U16), "xb0": _s([128, 256], F32), "xb1": _s([128, 256], F32),
     "inh": _s([128, 176], B16), "idh": _s([128, 176], F32), "nih": _s([128, 176], F32), "csc": _s([128, 176], F32),
-    "sm": _s([128, 20, 16], F32), "si": _s([128, 6, 16], I32), "fd": _s([128, 16], F32), "nf": _s([128, 16], F32), "fc": _s([128, 16], F32),
-    "qs": _s([128, 16], F32), "hl": _s([128, 32], B16),
-    "du": _s([128, 16], U16), "fz": _s([128, 16], U16), "iu": _s([128, 16], U16), "nu": _s([128, 16], U16),
-    "ju": _s([128, 16], U16), "ou": _s([128, 16], U16), "qo": _s([128, 32], U16), "wu": _s([128, 16], U16),
-    "pu": _s([128, 16], U16), "bc": _s([128, 32], U16), "b15": _s([128, 16], U16),
-    "pi": _s([128, 8], I32), "ci": _s([128, 8], I32), "cf": _s([128, 32], F32), "ro": _s([128, 144], F32),
-    "rx": _s([128, 4, 128], F32), "ii": _s([128, 256], B16), "kp": _s([128, 256], B16), "bg": _s([128, 256], B16),
-    "one": _s([128, 256], B16), "tri": _s([128, 512], B16), "dia": _s([128, 256], B16), "fh": _s([128, 512], B16),
-    "fl": _s([128, 512], B16), "zz": _s([128, 6, 144], B16), "zh": _s([128, 144], F16), "mb": _s([128, 16, 128], B16),
-    "mf": _s([128, 2, 128], F32), "hq": _s([128, 7, 144], B16), "w2": _s([128, 32], B16), "w32": _s([128, 32], B16), "lt": _s([128, 16], B16),
+    "sm": _s([128, 8, 16], F32), "sb": _s([128, 8, 16], B16), "si": _s([128, 4, 16], I32), "mv": _s([128, 32], F16),
+    "fs": _s([128, 24], F16), "fr": _s([128, 16], F16),
+    "du": _s([128, 16], U16), "fz": _s([128, 16], U16), "iu": _s([128, 16], U16), "nj": _s([128, 32], U16),
+    "ou": _s([128, 48], U16), "qo": _s([128, 32], U16), "wu": _s([128, 16], U16), "eo": _s([128, 24], U16),
+    "pu": _s([128, 16], U16), "bc": _s([128, 16], U16),
+    "pi": _s([128, 8], I32), "ci": _s([128, 12], I32), "cf": _s([128, 48], F32), "ro": _s([128, 144], F32),
+    "rx": _s([128, 4, 128], F32), "ii": _s([128, 256], B16), "kp": _s([128, 256], B16), "j32": _s([128, 384], B16),
+    "kq": _s([128, 384], B16), "bq": _s([128, 384], B16),
+    "one": _s([128, 256], B16), "tri": _s([128, 384], B16), "dia": _s([128, 256], B16), "fh": _s([128, 512], B16),
+    "fl": _s([128, 512], B16), "zz": _s([128, 6, 144], B16), "zh": _s([128, 144], F16), "mb": _s([128, 24, 128], B16),
+    "mf": _s([128, 4, 128], F32), "mh": _s([128, 4, 128], F16), "hq": _s([128, 7, 144], B16), "w1": _s([128, 96], B16), "lt": _s([128, 16], B16),
     "st": _s([128, 16], B16), "r3": _s([128, 16], F32),
 }
 for _b in range(8):
@@ -80,7 +90,6 @@ def bits(engines):
 def schedule(ops):
     n = len(ops)
     succ = [[] for _ in range(n)]
-    left = [0] * n
     for i, o in enumerate(ops):
         pre = {}
         for d in o["deps"]:
@@ -93,44 +102,57 @@ def schedule(ops):
             pre.setdefault(d, 0)
         for d, l in pre.items():
             succ[d].append((i, l))
-        left[i] = len(pre)
     prio = [0.0] * n
     for i in range(n - 1, -1, -1):
         prio[i] = ops[i]["cost"] + max([l + prio[j] for j, l in succ[i]] + [ops[i]["lat"]])
-    ready = [0.0] * n
-    cand = {}
+    pred = [[] for _ in range(n)]
     for i in range(n):
-        if left[i] == 0:
-            cand.setdefault(ops[i]["eng"], []).append(i)
-    free, order = {}, []
-    while len(order) < n:
-        best = None
-        for e, l in cand.items():
-            if not l:
-                continue
-            t0 = max(free.get(e, 0.0), min(ready[i] for i in l))
-            pick = None
-            for p_ in sorted((i for i in l if ready[i] <= t0), key=lambda i: (-prio[i], i)):
-                soon = [i for i in l if t0 < ready[i] < t0 + RULE * ops[p_]["cost"] and prio[i] > prio[p_] + 300]
-                if not soon:
-                    pick = p_
-                    break
-                later = max(soon, key=lambda i: (prio[i], -i))
-            if pick is None:
-                pick = later
-            st = max(t0, ready[pick])
-            if best is None or st < best[0]:
-                best = (st, e, pick)
-        st, e, i = best
-        cand[e].remove(i)
-        free[e] = st + ops[i]["cost"]
-        order.append(i)
         for j, l in succ[i]:
-            ready[j] = max(ready[j], free[e] + l)
-            left[j] -= 1
-            if left[j] == 0:
-                cand.setdefault(ops[j]["eng"], []).append(j)
-    return order
+            pred[j].append((i, l))
+    tail = [o["lat"] for o in ops]
+    best, rng = None, np.random.default_rng(0)
+    kinds = {}
+    for i, o in enumerate(ops):
+        kinds.setdefault(o["kind"], []).append(i)
+    kinds = list(kinds.values())
+    for k in range(PASSES):
+        end = deal(ops, succ, prio, [0.0] * n)
+        back = deal(ops, pred, end, list(tail))
+        end = deal(ops, succ, back, [0.0] * n)
+        span = max(e + l for e, l in zip(end, tail))
+        if best is None or span <= best[0]:
+            best = (span, end, back)
+        prio = list(best[2]) if k % 2 else [o["cost"] - e for o, e in zip(ops, best[1])]
+        shift = float(rng.random()) * SHIFT
+        for i in kinds[int(rng.integers(len(kinds)))]:
+            prio[i] += shift
+        for i in range(n - 1, -1, -1):
+            for j, l in succ[i]:
+                if prio[i] <= prio[j]:
+                    prio[i] = prio[j] + 1
+        SPANS.append(span)
+    return sorted(range(n), key=lambda i: (best[1][i] - ops[i]["cost"], i))
+
+
+def deal(ops, succ, prio, ready):
+    busy, end = {}, [0.0] * len(ops)
+    for i in sorted(range(len(ops)), key=lambda i: -prio[i]):
+        l, st, cost = busy.setdefault(ops[i]["eng"], []), ready[i], ops[i]["cost"]
+        a, b = 0, len(l)
+        while a < b:
+            m = (a + b) // 2
+            if l[m][1] <= st:
+                a = m + 1
+            else:
+                b = m
+        while a < len(l) and l[a][0] < st + cost:
+            st = max(st, l[a][1])
+            a += 1
+        l.insert(a, (st, st + cost))
+        end[i] = st + cost
+        for j, lat in succ[i]:
+            ready[j] = max(ready[j], end[i] + lat)
+    return end
 
 
 def rank_program(g, core, T, topo):
@@ -138,7 +160,7 @@ def rank_program(g, core, T, topo):
     if rank is None:
         return
     Q = {"pool": g, "pe": g.tensor, "dve": g.vector, "act": g.scalar, "sync": g.sync}
-    ops, lastw, readers = [], {}, {}
+    ops, lastw, readers, later, step = [], {}, {}, [], {}
 
     def op(eng, fn, r, w, cost, dma=None, lat=0.0):
         deps, order = [], []
@@ -150,7 +172,10 @@ def rank_program(g, core, T, topo):
         for k in w:
             for x in readers.get(k, []) + ([lastw[k]] if k in lastw else []):
                 (order if k.startswith("ch") or (eng == "pe" and ops[x]["eng"] == "pe") else deps).append(x)
-        ops.append({"eng": eng, "fn": fn, "deps": deps, "ord": order, "dma": dma, "sig": False, "cost": cost, "lat": lat})
+        kind = (eng, "".join(x for x in (w or r)[0].split("_")[0] if x > "9"), (w or r)[0].split("_")[1:] if step else len(ops))
+        kind = repr(kind) + (w or r)[0] * (w or r)[0].startswith("ps")
+        step[kind] = step.get(kind, 0) + 1
+        ops.append({"kind": (kind, step[kind]), "eng": eng, "fn": fn, "deps": deps, "ord": order, "dma": dma, "sig": False, "cost": cost, "lat": lat})
         me_ = len(ops) - 1
         for k in r:
             readers.setdefault(k, []).append(me_)
@@ -162,56 +187,61 @@ def rank_program(g, core, T, topo):
     v = g.vector
 
     def vc(n, k):
-        return FIX + (max(67.0, n * k) if k < GA else n * k)
+        return FIX + (max(64 * CY, n * k) if k < GA else n * k)
 
-    def ts(out, in0, s1, o0, s2=None, o1=None, r=(), w=(), n=16, k=1.04):
+    def ts(out, in0, s1, o0, s2=None, o1=None, r=(), w=(), n=16, k=CY):
         if o1 is None:
             op("dve", lambda: v.tensor_scalar(out, in0, s1, None, o0), r, w, vc(n, k))
         else:
             op("dve", lambda: v.tensor_scalar(out, in0, s1, s2, o0, o1), r, w, vc(n, k))
 
-    def tt(out, a, b, o, r, w, n=16, k=MU):
+    def tt(out, a, b, o, r, w, n=16, k=CY):
         op("dve", lambda: v.tensor_tensor(out, a, b, o), r, w, vc(n, k))
 
-    def cp(out, a, r, w, n=16, k=1.04):
+    def cp(out, a, r, w, n=16, k=CY):
         op("dve", lambda: v.tensor_copy(out, a), r, w, vc(n, k))
 
     def ms(out, c, w, n=16):
-        op("dve", lambda: v.memset(out, c), (), w, vc(n, 0.52))
+        op("dve", lambda: v.memset(out, c), (), w, vc(n, CY / 2))
 
-    def scan(out, d0, d1, o0, o1, r, w, k=1.04):
-        op("dve", lambda: v.tensor_tensor_scan(out, d0, d1, 0.0, o0, o1), r, w, vc(256, k))
+    def scan(out, d0, d1, o0, o1, r, w, n=256, k=CY):
+        op("dve", lambda: v.tensor_tensor_scan(out, d0, d1, 0.0, o0, o1), r, w, vc(n, k))
 
-    def ac(out, a, r, w, n=256, k=1.04, bias=None, f=AF.Identity, scale=1.0):
+    def ac(out, a, r, w, n=256, k=CY, bias=None, f=AF.Identity, scale=1.0):
         if bias is None:
             op("act", lambda: g.scalar.activation(out, a, AF.Copy, scale=scale), r, w, 15 + vc(n, k))
         else:
             op("act", lambda: g.scalar.activation(out, a, f, bias=bias, scale=scale), r, w, 15 + vc(n, k))
 
     def mm(out, l, rh, st, sp, r, w, n=64):
-        op("pe", lambda: g.tensor.matmul(out, l, rh, st, sp), r, w, max(64, n) * PE)
+        op("pe", lambda: g.tensor.matmul(out, l, rh, st, sp), r, w, n * PE)
+
+    def mms(calls, r, w, n=64):
+        op("pe", lambda: [g.tensor.matmul(*c) for c in calls][-1], r, w, len(calls) * n * PE)
 
     def iota(out, pat, base, cm, w, n, flag=True):
         if flag:
-            op("pool", lambda: g.iota(out, pat, base, cm, allow_small_or_imprecise_dtypes=True), (), w, 130 + 2.1 * n)
+            op("pool", lambda: g.iota(out, pat, base, cm, allow_small_or_imprecise_dtypes=True), (), w, 130 + 2 * CY * n)
         else:
-            op("pool", lambda: g.iota(out, pat, base, cm), (), w, 130 + 2.1 * n)
+            op("pool", lambda: g.iota(out, pat, base, cm), (), w, 130 + 2 * CY * n)
 
     def dma(eng, out, in_, sem, r, w, lat):
         op(eng, lambda: Q[eng].dma_start(out, in_), r, w + ["q" + eng + sem], 60, dma=sem, lat=lat)
 
     PS = [T["ps%d" % b] for b in range(8)]
 
-    def to_l(bank, n, z, src, first, rk, lo=0, hi=None):
-        for r_ in range(16):
-            mm(PS[bank][:, 0:n], z(r_), src[:, lo + r_:hi:16], first and r_ == 0, r_ == 15, rk, ["ps%d" % bank])
+    def to_l(bank, out, z, src, first, rk, lo=0, hi=None, stop=True):
+        mms([(out, z(r_), src[:, lo + r_:hi:16], first and r_ == 0, stop and r_ == 15) for r_ in range(16)], rk, ["ps%d" % bank])
 
     def zw(k):
         return lambda r_: T.zz[:, k, 15 - r_:143 - r_]
-    Z32, Z1, Z4K, ZA, ZQ, Z37 = [zw(k) for k in range(6)]
+    Z4Q, Z1, ZA, ZQ, Z37, ZL = [zw(k) for k in range(6)]
 
     def ZH(r_):
         return T.zh[:, 15 - r_:143 - r_]
+
+    def staged(name, lo=0, hi=16):
+        return ["%s_%d" % (name, s[0]) for s in STAGES if s[0] < hi and lo < s[1]]
 
     peers = [s for s in range(N) if s != rank]
     far = [s for s in peers if topo.chip(T.cores[s]) != topo.chip(core)]
@@ -222,7 +252,7 @@ def rank_program(g, core, T, topo):
         a = topo.addr(T.cores[s])
         return DstId(rid=a[0], pnc=a[1])
 
-    def to_all(src, land, sem, r, key, cost):
+    def to_all(src, land, sem, r, key, cost, lat):
         off = off_engines(T, topo, core)
         trs = [RemoteDMATransfer(dst_ids=[dst(s) for s in far], dma_engine_mask=bits(off), remote_sem=T.sem[sem], srcs=[src], dsts=[land(s) for s in far])]
         sent[0] += len(off)
@@ -232,7 +262,7 @@ def rank_program(g, core, T, topo):
             sent[0] += len(en)
         me_ = op("pool", lambda: g.remote_dma_fused(trs, local_sem=T.sem.sent), r, (), cost)
         come = sum(len(off_engines(T, topo, T.cores[s])) for s in far) + sum(len(share(T, topo, T.cores[s], [core])[core]) for s in near)
-        lastw[key] = (sem, come, [me_], 10000)
+        lastw[key] = (sem, come, [me_], lat)
 
     def halves(h):
         sl = slots(T, topo, h)
@@ -244,121 +274,146 @@ def rank_program(g, core, T, topo):
     ans_in = sum(len(answer_engines(h, hf)[core]) for h in peers for hf in range(2) if rank in halves(h)[hf])
     myslots = slots(T, topo, rank)
 
-    dma("sync", T.c0s[:], T.c0[:], "l_c0", [], ["c0s", "chs"], 2000)
-    dma("act", T.xt[:, 0:256], T.x0[:], "l_x0", [], ["x0", "chq"], 2200)
-    dma("act", T.pws[:], T.pw[:], "l_pw", [], ["pws", "chq"], 4000)
-    dma("sync", T.sfs[:], T.sf[:], "l_sf", [], ["sfs", "chs"], 9000)
-    dma("sync", T.otq[:], T.ot[:], "l_ot", [], ["otq", "chs"], 10000)
-    dma("act", T.stp[:], T.dr[:], "l_dr", [], ["stp", "chq"], 4500)
-    dma("act", T.ths[:], T.th[:], "l_th", [], ["ths", "chq"], 4500)
-    dma("sync", T.hws[:], T.hw[:], "l_hs", [], ["hws", "chs"], 10000)
-    dma("sync", T.hwa[:, 2 * rank:2 * rank + 2], T.hw[:], "l_hw", [], ["hwown", "chs"], 10000)
+    dma("act", T.xt[:, 0:256], T.x0[:], "l_x0", [], ["x0", "chq"], LOADS[0])
+    dma("act", T.ths[:], T.th[:], "l_th", [], ["ths", "chq"], LOADS[0])
+    dma("act", T.stp[:], T.dr[:], "l_dr", [], ["stp", "chq"], LOADS[0])
+    dma("sync", T.c0s[:], T.c0[:], "l_c0", [], ["c0s", "chs"], LOADS[0])
+    dma("sync", T.hws[:], T.hw[:], "l_hs", [], ["hws", "chs"], LOADS[0])
+    dma("sync", T.pws[:], T.pw[:], "l_pw", [], ["pws", "chs"], LOADS[1])
+    dma("sync", T.sfs[:], T.sf[:], "l_sf", [], ["sfs", "chs"], LOADS[2])
+    dma("sync", T.otq[:], T.ot[:], "l_ot", [], ["otq", "chs"], LOADS[3])
+    dma("sync", T.hwa[:, 2 * rank:2 * rank + 2], T.hw[:], "l_hw", [], ["hwown", "chs"], LOADS[3])
 
+    KW = 32 * max(s[1] - s[0] for s in STAGES)
     iota(T.pi[:, 0:1], [[0, 1]], 0, 1, ["pi"], 1, False)
     iota(T.ro[:], [[1, 144]], 0, 0, ["ro"], 144)
     iota(T.ii[:], [[0, 16], [1, 16]], 0, 0, ["ii"], 256)
+    iota(T.j32[:, 0:KW], [[0, KW // 32], [1, 32]], 0, 0, ["j32"], KW)
     iota(T.fh[:], [[64, 8], [0, 64]], 0, 512, ["fh"], 512)
-    iota(T.fl[:], [[0, 8], [1, 64]], 0, 0, ["fl"], 512)
+    iota(T.fl[:], [[0, 8], [1, 64]], 1, 0, ["fl"], 512)
     iota(T.rx[:, 0], [[2, 64], [-1, 2]], 1, 0, ["rx0"], 128)
     iota(T.rx[:, 1], [[4, 32], [-1, 4]], 3, 0, ["rx1"], 128)
     iota(T.rx[:, 2], [[16, 8], [-8, 2], [1, 8]], 8, 0, ["rx2"], 128)
-    iota(T.rx[:, 3], [[16, 8], [0, 16]], 0, 0, ["rx3"], 128)
-    C = {}
+    iota(T.rx[:, 3], [[0, 16], [16, 8]], 0, 0, ["rx3"], 128)
+    C, CK = {}, {}
 
-    def colf(name, k):
-        C[name] = T.cf[:, k:k + 1]
+    def colf(name):
+        k = len(C)
+        C[name], CK[name] = T.cf[:, k:k + 1], k
         return C[name]
-    for k, (m, sh) in enumerate(((15, 0), (112, 0), (3, 0), (15, 2), (2, 0), (127, 0))):
+
+    def named(*xs):
+        return ["cf"] + ["c_" + x for x in xs if isinstance(x, str)]
+    first = (("r", 15, 0), ("g16", 112, 0), ("r3", 3, 0), ("rq", 15, 2), ("b2", 2, 0), ("p", 127, 0),
+             ("g8", 7, 0), ("q4", 96, 3), ("u2", 8, 2), ("h", 16, 4), ("b0", 1, 0))
+    for k, (n_, m, sh) in enumerate(first):
         ts(T.ci[:, k:k + 1], T.pi[:, 0:1], m, A.bitwise_and, sh, A.logical_shift_right, r=["pi"], w=["ci%d" % k])
-    cp(T.cf[:, 0:6], T.ci[:, 0:6], ["ci%d" % k for k in range(6)], ["cf"])
-    for k, n_ in enumerate(("r", "g16", "r3", "rq", "b2", "p")):
-        colf(n_, k)
-    S = {n_: T.sm[:, k] for k, n_ in enumerate(("th", "thp", "nq", "df", "jj", "jm", "e5", "fr", "j2", "cfd", "nfd", "nin", "ub", "sv", "nw", "yc", "t1"))}
-    S["fd"] = T.fd[:]
-    SI = {n_: T.si[:, k] for k, n_ in enumerate(("mk", "mk2", "fi", "q", "pr", "h"))}
+        colf(n_)
+    cp(T.cf[:, 0:11], T.ci[:, 0:11], ["ci%d" % k for k in range(11)], ["cf"])
+    S = {n_: T.sm[:, k] for k, n_ in enumerate(("df", "ub", "nw", "yc", "t1"))}
+    BK = {n_: k for k, n_ in enumerate(("jj", "nc", "e5", "t17", "pb", "sv", "th", "cb"))}
+    B = {n_: T.sb[:, k] for n_, k in BK.items()}
+    SI = {n_: T.si[:, k] for k, n_ in enumerate(("fi", "q", "pr", "h"))}
     IB, I4K, BM, BOF, IKP, SELY, IM8 = T.mb[:, 0], T.mb[:, 6], T.mb[:, 7], T.mb[:, 8], T.mb[:, 9], T.mb[:, 10, 0:32], T.mb[:, 14]
-    I2, IF, ZF = T.mb[:, 15], T.mf[:, 0], T.mf[:, 1]
-    R128 = T.ro[:, 0:128]
-    for name, k, a, s1, o0, s2, o1 in (
-            ("a", 6, "g16", 15.0, A.add, None, None), ("k", 7, "g16", "rq", A.add, 4.0, A.add), ("k8", 8, "g16", "rq", A.add, 12.0, A.add),
-            ("ge4", 9, "r", 4.0, A.is_ge, None, None), ("mid", 10, "r", 12.0, A.is_lt, "ge4", A.mult), ("r256", 11, "r", 1.0 / 256, A.mult, None, None),
-            ("dum", 12, "r", 2048.0, A.add, None, None), ("lt8", 13, "r", 8.0, A.is_lt, None, None), ("r2", 14, "r", 2.0, A.mult, None, None),
-            ("ge8", 15, "r", 8.0, A.is_ge, None, None), ("s1", 17, "b2", 2.0, A.add, "lt8", A.mult), ("rm8", 23, "r", -8.0, A.add, None, None),
-            ("p1", 24, "r", 16.0, A.mult, 128.0, A.min), ("p2", 25, "r", float(rank), A.is_equal, float(256 - 16 * rank), A.mult),
-            ("y", 26, "g16", 0.25, A.mult, "r3", A.add), ("dum16", 29, "r", 2064.0, A.add, None, None),
-            ("ndum16", 30, "r", -1.0, A.mult, -2064.0, A.add), ("ndum", 28, "r", -1.0, A.mult, -2048.0, A.add)):
-        ts(colf(name, k), C[a], C.get(s1, s1), o0, C.get(s2, s2), o1, r=["cf"] + ["c_" + x for x in (a, s1, s2) if isinstance(x, str)], w=["c_" + name])
+    M4K, NI, I16, I256, PM, PMT = [T.mb[:, k] for k in range(15, 21)]
+    IF, ZF, PF, PH, NPT, IH = T.mf[:, 0], T.mf[:, 1], (T.mf[:, 2], T.mf[:, 3]), (T.mh[:, 0], T.mh[:, 1]), T.mh[:, 2], T.mh[:, 3]
+    R128, ONE = T.ro[:, 0:128], T.one[:, 0:16]
+    JU = T.nj[:, 0:16]
+    ts(colf("rq_"), C["q4"], C["u2"], A.add, C["h"], A.add, r=["cf"], w=["c_rq_"])
+    for name, a, s, b, f in (
+            ("lp", "g8", 16.0, "rq_", AF.Identity), ("aq", "g8", 16.0, 15.0, AF.Identity), ("nh", "h", -1.0, 1.0, AF.Identity),
+            ("h16", "h", 16.0, 0.0, AF.Identity), ("nh16", "h", -16.0, 16.0, AF.Identity), ("a", "g16", 1.0, 15.0, AF.Identity),
+            ("k", "g16", 1.0, "rq", AF.Identity), ("k8", "k", 1.0, 12.0, AF.Identity), ("m0", "rq", 1.0, -2.0, AF.Relu),
+            ("mid", "m0", -1.0, 1.0, AF.Identity), ("dum", "r", 1.0, 2049.0, AF.Identity), ("dum16", "r", 1.0, 2065.0, AF.Identity),
+            ("lt8", "u2", -0.5, 1.0, AF.Identity), ("ge8", "u2", 0.5, 0.0, AF.Identity), ("rm8", "r", 16.0, -128.0, AF.Identity),
+            ("y", "g16", 0.25, "r3", AF.Identity), ("wl", "ge8", -1.0, "b0", AF.Abs)):
+        ac(colf(name), C[a], named(a, b), ["c_" + name], 1, bias=C.get(b, b), f=f, scale=s)
+    ts(colf("s1"), C["b2"], 2.0, A.add, C["lt8"], A.mult, r=named("lt8"), w=["c_s1"])
 
     def eq(out, row, rk, a, s2, w, n):
-        ts(out, row, C.get(a, a), A.is_equal, C.get(s2, s2), None if s2 is None else A.mult,
-           r=["cf", rk] + ["c_" + x for x in (a, s2) if isinstance(x, str)], w=[w], n=n)
+        ts(out, row, C.get(a, a), A.is_equal, C.get(s2, s2), None if s2 is None else A.mult, r=[rk] + named(a, s2), w=[w], n=n)
 
     def scaled(out, a, ak, s, w, n):
-        ac(out, a, [ak] + (["c_" + s] if isinstance(s, str) else []), [w], n, scale=C.get(s, s))
+        ac(out, a, [ak] + named(s), [w], n, scale=C.get(s, s))
     eq(T.r3[:], T.ro[:, 0:16], "ro", "r3", None, "r3", 16)
     eq(IB, R128, "ro", "p", None, "ib", 128)
-    eq(T.hq[:, 4], T.ro[:], "ro", "k", None, "hq4", 144)
+    eq(PM, R128, "ro", "lp", None, "pm", 128)
+    ts(T.hq[:, 4], T.ro[:], -4.0, A.add, C["k"], A.is_equal, r=["ro", "c_k"], w=["hq4"], n=144)
     eq(T.hq[:, 5], T.ro[:], "ro", "k8", "mid", "hq5", 144)
-    eq(T.zz[:, 0], T.ro[:], "ro", "a", 32.0, "z32", 144)
+    eq(T.zz[:, 0], T.ro[:], "ro", "aq", 4096.0, "z4q", 144)
     eq(T.zz[:, 1], T.ro[:], "ro", "a", None, "z1", 144)
-    eq(T.zh[:], T.ro[:], "ro", "a", None, "zh", 144)
-    eq(T.w2[:], T.ro[:, 0:32], "ro", "r2", None, "w2", 32)
-    eq(T.w32[:], T.ro[:, 0:32], "ro", "r", None, "w32", 32)
-    for out, s, w in ((I4K, 4096.0, "i4k"), (IF, 1.0, "if"), (I2, 2.0, "i2"), (IM8, -8.0, "im8")):
+    cp(T.zh[:], T.zz[:, 1], ["z1"], ["zh"], 72)
+    eq(T.w1[:], T.ro[:, 0:96], "ro", "r", None, "w1", 96)
+    for h_, a in enumerate(("nh16", "h16")):
+        scaled(PF[h_], PM, "pm", a, "pf%d" % h_, 128)
+        ts(PH[h_], PM, C[a], A.mult, -1.0, A.mult, r=["pm", "c_" + a], w=["ph%d" % h_])
+    for out, s, w in ((I4K, 4096.0, "i4k"), (IF, 1.0, "if"), (IM8, -8.0, "im8"), (M4K, -4096.0, "m4k"), (NI, -1.0, "ni"), (I16, 16.0, "i16"), (I256, 256.0, "i256")):
         scaled(out, IB, "ib", s, w, 128)
-    scaled(T.zz[:, 2], T.zz[:, 1], "z1", 4096.0, "z4k", 144)
+    cp(IH, IB, ["ib"], ["ih"])
     scaled(ZF, Z1(0), "z1", 1.0, "zf", 128)
+    mm(PS[4][:, 0:128], PM, IB, True, True, ["pm", "ib"], ["ps4"], 128)
+    ac(PMT, PS[4][:, 0:128], ["ps4"], ["pmt"], 128)
+    ts(NPT, PMT, -1.0, A.mult, r=["pmt"], w=["npt"])
     tt(T.hq[:, 6], T.hq[:, 4], T.hq[:, 5], A.add, ["hq4", "hq5"], ["hq6"], 144)
     for q in range(4):
-        ts(T.mb[:, 1 + q], T.ii[:, 0:128], 8.0, A.is_equal, T.mb[:, 0, q:q + 1], A.mult, r=["ii", "ib"], w=["s8%d" % q])
+        ts(T.mb[:, 1 + q], T.ii[:, 0:128], 11.0, A.is_equal, T.mb[:, 0, q:q + 1], A.mult, r=["ii", "ib"], w=["s8%d" % q])
         ac(T.hq[:, q], T.hq[:, 6], ["hq6", "r3"], ["hq%d" % q], 144, scale=T.r3[:, q:q + 1])
-    ts(T.mb[:, 5], T.ii[:, 0:128], 11.0, A.is_equal, T.mb[:, 0, 0:1], A.mult, r=["ii", "ib"], w=["s11"])
-    tt(colf("m12", 16), T.r3[:, 1:2], T.r3[:, 2:3], A.add, ["r3"], ["c_m12"])
-    ts(colf("s2", 18), C["m12"], 4.0, A.mult, -1.0, A.add, r=["c_m12"], w=["c_s2"])
-    ts(colf("s3", 19), C["s2"], C["ge8"], A.mult, C["s1"], A.add, r=["c_s2", "c_ge8", "c_s1"], w=["c_s3"])
+    ts(T.mb[:, 5], T.ii[:, 0:128], 15.0, A.is_equal, T.mb[:, 0, 0:1], A.mult, r=["ii", "ib"], w=["s11"])
+    ac(colf("m3"), T.r3[:, 3:4], ["r3"], ["c_m3"], 1, bias=1.0, scale=-1.0)
+    ts(colf("s0"), T.r3[:, 3:4], -9.0, A.mult, 3.0, A.add, r=["r3"], w=["c_s0"])
+    ac(colf("s2"), T.r3[:, 0:1], ["r3", "c_s0"], ["c_s2"], 1, bias=C["s0"], scale=-2.0)
+    ac(colf("s3"), C["s2"], ["c_s2", "c_ge8", "c_s1"], ["c_s3"], 1, bias=C["s1"], scale=C["ge8"])
     eq(T.mb[:, 11], T.rx[:, 0], "rx0", "p", "lt8", "m11", 128)
     eq(T.mb[:, 12], T.rx[:, 1], "rx1", "p", "ge8", "m12", 128)
-    eq(T.mb[:, 13], T.rx[:, 2], "rx2", "p", "m12", "m13", 128)
+    eq(T.mb[:, 13], T.rx[:, 2], "rx2", "p", "m3", "m13", 128)
     eq(T.st[:], T.ro[:, 0:16], "ro", "s3", None, "st", 16)
-    tt(T.mb[:, 11], T.mb[:, 11], T.mb[:, 12], A.add, ["m11", "m12"], ["m11"], 128)
-    tt(T.mb[:, 13], T.mb[:, 13], IB, A.add, ["m13", "ib"], ["m13"], 128)
-    tt(T.mb[:, 11], T.mb[:, 11], IB, A.subtract, ["m11", "ib"], ["m11"], 128)
-    for name, k, a, b in (("f2", 20, 8, 11), ("a04", 21, 0, 4), ("a37", 22, 3, 7)):
-        tt(colf(name, k), T.w32[:, a:a + 1], T.w32[:, b:b + 1], A.add, ["w32"], ["c_" + name])
-    ts(colf("n37", 27), C["a37"], 0.0, A.is_equal, r=["c_a37"], w=["c_n37"])
+    eq(T.lt[:], T.ro[:, 1:17], "ro", "s3", None, "lt", 16)
+    for name, a, b in (("f2", 11, 15), ("a04", 0, 4), ("a37", 3, 7)):
+        tt(colf(name), T.w1[:, a:a + 1], T.w1[:, b:b + 1], A.add, ["w1"], ["c_" + name])
+    ac(colf("n37"), C["a37"], ["c_a37"], ["c_n37"], 1, bias=1.0, scale=-1.0)
     eq(BOF, T.rx[:, 3], "rx3", "g16", "f2", "bof", 128)
-    for k, s, w in ((3, "a04", "za"), (4, "rm8", "zq"), (5, "a37", "z37")):
+    for k, s, w in ((2, "a04", "za"), (3, "rm8", "zq"), (4, "a37", "z37"), (5, "wl", "zl")):
         scaled(T.zz[:, k], T.zz[:, 1], "z1", s, w, 144)
     eq(SELY, T.ro[:, 0:32], "ro", "y", "lt8", "sely", 32)
     scaled(IKP, IB, "ib", "n37", "ikp", 128)
     ts(T.dia[:], T.ii[:], C["r"], A.is_equal, r=["ii", "cf"], w=["dia"], n=128)
-    iota(T.od[:], [[0, 8], [-16, 2], [0, 16]], 0, 0, ["od"], 256)
-    iota(T.bf[:], [[2, 8], [0, 2]], 0, 0, ["bf"], 16)
-    cp(T.be[:], T.bf[:], ["bf"], ["be"])
-    ts(T.t0[:], T.ii[:], C["r"], A.is_le, -8192.0, A.mult, r=["ii", "cf"], w=["t0"], n=128)
-    tt(T.tri[:, 0:256], T.t0[:], T.od[:], A.add, ["t0", "od"], ["tri"], 256)
-    ts(T.tri[:, 256:512], T.od[:], 0.0, A.is_equal, -8192.0, A.mult, r=["od"], w=["tri2"], n=128)
-    ts(T.kp[:], T.ii[:], 0.0, A.is_gt, r=["ii"], w=["kp"], n=128)
-    ts(T.bg[:], T.ii[:], 0.0, A.is_equal, 1.0e6, A.mult, r=["ii"], w=["bg"], n=128)
-    ts(T.pu[:], T.ro[:, 0:16], C["p1"], A.add, C["p2"], A.add, r=["ro", "c_p1", "c_p2"], w=["pu"])
-    ts(T.b15[:], T.ro[:, 0:16], 16.0, A.mult, 15.0, A.add, r=["ro"], w=["b15"])
-    ts(T.lt[:], T.r3[:], C["lt8"], A.mult, r=["r3", "c_lt8"], w=["lt"])
-    ts(S["nq"], T.ro[:, 0:16], 1.0 / 16, A.mult, C["r256"], A.add, r=["ro", "c_r256"], w=["nq"])
-    cp(T.bc[:], T.ro[:, 0:32], ["ro"], ["bc"])
+    ms(T.tri[:, 0:128], 0.0, ["triz"], 128)
+    ts(T.tri[:, 128:384], T.ii[:], C["rq_"], A.is_le, 8192.0, A.mult, r=["ii", "c_rq_"], w=["tri"], n=128)
+    ac(T.kp[:], T.ii[:], ["ii"], ["kp"], bias=0.0, f=AF.Sign)
+    ac(T.kq[:, 0:KW], T.j32[:, 0:KW], ["j32"], ["kq"], KW, bias=0.0, f=AF.Sign)
+    ts(T.bq[:, 0:KW], T.j32[:, 0:KW], C["h16"], A.is_equal, 1.0e6, A.mult, r=["j32", "c_h16"], w=["bq"], n=KW // 2)
+    ts(T.eo[:, 0:8], T.ro[:, 0:8], 64.0, A.mult, 31.0, A.add, r=["ro"], w=["eo0"])
+    ts(T.eo[:, 8:24], T.ro[:, 0:16], 32.0, A.mult, 31.0, A.add, r=["ro"], w=["eo1"])
+    ac(B["pb"], T.ro[:, 0:16], ["ro", "cf"], ["pb"], 16, bias=C["r"], scale=16.0)
+    ac(B["cb"], T.ro[:, 0:16], ["ro"], ["cb"], 16, bias=128.0)
+    cp(T.bc[:], T.ro[:, 0:16], ["ro"], ["bc"])
     cp(T.du[:], T.c0s[:], ["c0s"], ["du"])
-    cp(S["th"], T.ths[:], ["ths"], ["th"])
+    cp(B["th"], T.ths[:], ["ths"], ["th"])
+    ac(B["t17"], B["th"], ["th"], ["t17"], 16, bias=-16.0, f=AF.Relu)
     cp(S["df"], T.c0s[:], ["c0s"], ["df"])
-    cp(T.idh[:, 0:176:11], T.c0s[:], ["c0s"], ["id_0"])
+    ac(T.idh[:, 0:176:11], S["df"], ["df"], ["id_0"], 16)
+    ms(T.xd[:], 0.0, ["xdz"] + [x for k in range(8) for x in staged("xd%d" % k)], 4096)
     ms(T.one[:], 1.0, ["one"], 256)
-    ms(T.ju[:], 0, ["ju"])
-    ms(S["jm"], 1.0, ["jm"])
+    ms(JU, 0, ["ju"])
+    ms(B["jj"], 0.0, ["jj"])
     ms(T.inh[:, 0:176:11], 1.0, ["in_0"])
-    ms(T.tab[:, 2048:TW], 0.0, ["tabz"])
-    ms(T.y3[:, 2048:TW], 0.0, ["y3z"])
+    ms(T.tab[:, 0:1], 0.0, ["tabz"])
+    ms(T.tab[:, 2049:TW], 0.0, ["taby"])
+    ms(T.y3[:, 0:1], 0.0, ["y3z"])
+    ms(T.y3[:, 2049:TW], 0.0, ["y3y"])
     ms(T.xb1[:, 128:144], 0.0, ["dfxb1"])
-    for e in range(2):
-        ms(T["xb%d" % e][:, 16 * rank:16 * rank + 16], 0.0, ["ownxb%d" % e])
-    to_all(T.hws[:], lambda s: T.hwa[:, 2 * rank:2 * rank + 2], "hwarr", ["hws"], "hwa", 3000)
+    to_all(T.hws[:], lambda s: T.hwa[:, 2 * rank:2 * rank + 2], "hwarr", ["hws"], "hwa", 3000, 10000)
+
+    mm(PS[4][:, 0:16], PMT, B["th"], True, True, ["pmt", "th"], ["ps4"])
+    ac(T.thq[:], PS[4][:, 0:16], ["ps4"], ["thq"], 16)
+    tt(T.t0[:], T.thq[:].indirect(T.bc[:]), T.ii[:], A.add, ["thq", "bc", "ii"], ["t0"], 256, GA)
+    ac(T.t0[:], T.t0[:], ["t0"], ["t0"], bias=15.5, f=AF.Sign, scale=-1.0)
+    ts(T.t1[:], T.ii[:], -7.5, A.add, 1.0 / 16, A.mult, r=["ii"], w=["t1"], n=128)
+    for h_, (own, other) in enumerate((("nh", "h"), ("h", "nh"))):
+        cs = slice(256 * h_, 256 * h_ + 256)
+        scaled(T.t2[:, cs], T.t1[:], "t1", own, "t2%d" % h_, 256)
+        ts(T.t3[:, cs], T.t0[:], C[other], A.mult, 4096.0, A.mult, r=["t0"] + named(other), w=["t3%d" % h_], n=128)
+        tt(T.kin[:, h_:32:2, :], T.t2[:, cs], T.t3[:, cs], A.add, ["t2%d" % h_, "t3%d" % h_], ["kin%d" % h_], 256)
 
     for h_ in range(2):
         cp(T.pw2[:, 2048 * h_:2048 * h_ + 2048:2], T.pws[:, 1024 * h_:1024 * h_ + 1024], ["pws"], ["pw2a%d" % h_], 512)
@@ -367,33 +422,38 @@ def rank_program(g, core, T, topo):
     cp(T.oth[:], T.otq[:], ["otq"], ["oth"], 512)
     tt(T.otl[:], T.otq[:], T.oth[:], A.subtract, ["otq", "oth"], ["otl"], 1024)
     for q in range(4):
-        k = ["ps%d" % (3 + q)]
-        mm(PS[3 + q][:], T.mb[:, 1 + q], T.fh[:], True, False, ["s8%d" % q, "fh"], k, 512)
-        mm(PS[3 + q][:], T.mb[:, 5], T.fl[:], False, False, ["s11", "fl"], k, 512)
-        mm(PS[3 + q][:], T.hq[:, q, 4:132], T.oth[:], False, False, ["hq%d" % q, "oth"], k, 512)
-        mm(PS[3 + q][:], T.hq[:, q, 0:128], T.otl[:], False, True, ["hq%d" % q, "otl"], k, 512)
+        b = (5, 2)[q % 2]
+        k = ["ps%d" % b]
+        mm(PS[b][:], T.mb[:, 1 + q], T.fh[:], True, False, ["s8%d" % q, "fh"], k, 512)
+        mm(PS[b][:], T.mb[:, 5], T.fl[:], False, False, ["s11", "fl"], k, 512)
+        mm(PS[b][:], T.hq[:, q, 4:132], T.oth[:], False, False, ["hq%d" % q, "oth"], k, 512)
+        mm(PS[b][:], T.hq[:, q, 0:128], T.otl[:], False, True, ["hq%d" % q, "otl"], k, 512)
         if q % 2:
-            ac(T.tab[:, 512 * q:512 * q + 512], PS[3 + q][:], k, ["tab%d" % q], 512)
+            ac(T.tab[:, 512 * q + 1:512 * q + 513], PS[b][:], k, ["tab%d" % q], 512)
         else:
-            cp(T.tab[:, 512 * q:512 * q + 512], PS[3 + q][:], k, ["tab%d" % q], 512)
-    mm(PS[6][:, 0:128], T.mb[:, 11], T.mb[:, 13], True, True, ["m11", "m13"], ["ps6"], 128)
-    cp(BM, PS[6][:, 0:128], ["ps6"], ["bm"], 128)
-    TAB = ["tab%d" % q for q in range(4)] + ["tabz"]
-    XE = ["xe%d" % i for i in range(16)]
+            cp(T.tab[:, 512 * q + 1:512 * q + 513], PS[b][:], k, ["tab%d" % q], 512)
+    for k, (a, ak) in enumerate(((T.mb[:, 11], "m11"), (T.mb[:, 12], "m12"), (NI, "ni"))):
+        mm(PS[5][:, 0:128], a, T.mb[:, 13], k == 0, False, [ak, "m13"], ["ps5"], 128)
+        mm(PS[5][:, 0:128], a, IB, False, k == 2, [ak, "ib"], ["ps5"], 128)
+    ac(BM, PS[5][:, 0:128], ["ps5"], ["bm"], 128)
+    TAB = ["tab%d" % q for q in range(4)] + ["tabz", "taby"]
 
-    def expand(src, key, nd):
-        for i in range(16):
-            o = T.xe[:, i:4096:16]
-            if i < NPOOL:
-                op("pool", lambda o=o: g.affine_select(o, src, [[0, 256]], A.is_ge, 0.0, 0, 0), [key], ["xe%d" % i, "chp"], 700)
-            elif i < 16 - nd:
-                ac(o, src, [key], ["xe%d" % i, "cha"])
+    def expand(name, key, npool, lo, hi):
+        n = 16 * (hi - lo)
+        for k in range(8):
+            odd, w = k % 2, "xd%d_%d" % (k, lo)
+            ps_ = slice(0, 16 * k + 16) if k < npool else slice(16 * (k - odd), 16 * k + 16)
+            o, a = T.xd[ps_, 256 * lo + 8 + k:256 * hi:16], T[name][ps_, 16 * lo:16 * hi]
+            if k < npool:
+                op("pool", lambda o=o, a=a, k=k: g.affine_select(o, a, [[0, n]], A.is_ge, 0.0, -16 * k, 1), [key], [w, "chp"], 170 + 2 * n * CY)
+            elif odd:
+                ac(o, a, [key, "cf"], [w], n, scale=T.cf[ps_, CK["h"]:CK["h"] + 1])
             else:
-                cp(o, src, [key], ["xe%d" % i], 128)
+                ac(o, a, [key], [w], n)
 
-    def next_x(n):
+    def next_x(n, bank):
         a, b = T.xt[:, 256 * (n - 1):256 * n], T.xt[:, 256 * n:256 * n + 256]
-        o, k = PS[7][:, 0:256], ["ps7"]
+        o, k = PS[bank][:, 0:256], ["ps%d" % bank]
         mm(o, IB, a, True, False, ["ib", "x%d" % (n - 1)], k, 256)
         mm(o, IB, T.stp[:], False, True, ["ib", "stp"], k, 256)
         ac(T.xa[:], o, k, ["xa"], bias=-15.5, f=AF.Sign)
@@ -402,140 +462,205 @@ def rank_program(g, core, T, topo):
         mm(o, IM8, T.xa[:], False, True, ["im8", "xa"], k, 256)
         ac(b, o, k, ["x%d" % n], bias=-8.0)
 
-    def place(out, n, w):
-        ac(out, T.xt[:, 0:256 * n + 256].indirect(T.nu[:]), ["x%d" % k for k in range(n + 1)] + ["nu"], w, k=GA)
+    def place(out, n, lo, hi, w):
+        ac(out[:, 16 * lo:16 * hi], T.xt[:, 0:256 * n + 256].indirect(T.nj[:, 16 + lo:16 + hi]), ["x%d" % k for k in range(n + 1)] + ["nu_%d" % lo],
+           ["%s_%d" % (w, lo)], 16 * (hi - lo), GA)
 
-    def scatters(win, src, rk, wk):
-        for c in range(7, -1, -1):
-            cp(win[:].indirect(T.ou[:, 2 * c:2 * c + 2]), src[:, 32 * c:32 * c + 32], ["ou0", "ou1"] + rk, wk, 32, SC)
+    def scatters(win, src, rk, wk, lo=0, hi=16, per=2):
+        for c in range(hi - per, lo - 1, -per):
+            off = T.ou[:, c:c + 2] if per == 2 else T.ou[:, 16 + 2 * c:17 + 2 * c]
+            cp(win[:].indirect(off), src[:, 16 * c:16 * (c + per)], staged("ou0", lo, hi) + staged("ou1", lo, hi) + rk(c), wk, 16 * per, SC)
 
-    def lowest(flag, fk, base, bk):
-        tt(T.fc[:], flag, base, A.mult, [fk, bk], ["fc"])
-        mm(PS[2][:, 0:16], IF, T.fc[:], True, False, ["if", "fc"], ["ps2"], 256)
-        for h_, off in enumerate((T.bc[:, 0:16], T.be[:])):
-            cs = slice(256 * h_, 256 * h_ + 256)
-            tt(T.ee[:, cs], T.fc[:].indirect(off), T.frm[:, cs], A.is_equal, ["fc", "bc", "be", "frm"], ["ee%d" % h_], 256, GA)
-            for r_ in range(16):
-                mm(PS[2][:, 0:16], Z4K(r_), T.ee[:, 256 * h_ + r_:256 * h_ + 256:16], False, h_ == 1 and r_ == 15, ["z4k", "ee%d" % h_], ["ps2"])
+    def rivals(t):
+        k = ["ps5"]
+        bad = [] if t is None else ["nc", "t17"] + (["e5"] if t >= 5 else [])
+        p0 = 0 if t is None else min([8] + [s[0] // 2 for s in STAGES if s[2] == 2])
+        parts = [(PS[5][:, 384 + p0:392], slice(2 * p0, 16, 2))] * (p0 < 8) + [(PS[5][:, 392:408], slice(0, 16))]
+        calls = [(o, I4K, T.sb[:, BK[n_], cs]) for o, cs in parts for n_ in bad]
+        if bad:
+            mms([c + (j == 0, False) for j, c in enumerate(calls)], ["i4k"] + bad, k)
+        mms([(o, IH, T.fr[:, cs], j == 0 and not bad, j == len(parts) - 1) for j, (o, cs) in enumerate(parts)], ["ih", "fr"], k)
+        ts(T.fs[:, p0:24], PS[5][:, 384 + p0:408], 4000.0, A.min, r=k, w=["fs"])
+        mm(PS[5][:, 16 * p0:384], IB, T.tri[:, 16 * p0:384], True, False, ["ib", "tri", "triz"], k, 384 - 16 * p0)
+        mms([(PS[5][:, 16 * p0 + r_:384:16], NPT, T.fs[:, p0:24], False, False) for r_ in range(16)], ["npt", "fs"], k)
+        mm(PS[5][:, 128:384], BOF, T.col[:], False, p0 == 8, ["bof", "col"], k, 256)
+        if p0 < 8:
+            mms([(PS[5][:, 16 * c:16 * c + 16], BOF, T.col[:, 32 * c + 16:32 * c + 32], False, c == 7) for c in range(p0, 8)], ["bof", "col"], k)
+
+        def copy(w):
+            ac(T.thr[:, 16 * p0:384], PS[5][:, 16 * p0:384], k, ["thr"] + w, 384 - 16 * p0, bias=0.0, f=AF.Abs, scale=64.0)
+        if t is None:
+            copy([])
+        else:
+            later.append(copy)
+
+    def lowest(flag, fk, lo=0, hi=16, per=2):
+        n, win, tk, o = hi - lo, T.tot[:, 32 * lo:32 * hi], staged("tot", lo, hi), PS[2][:, lo:hi]
+        mm(o, IH, T.fs[:, 8 + lo:8 + hi], True, False, ["ih", "fs"], ["ps2"])
+        if per == 2:
+            cs, k = slice(8 * lo, 8 * hi), staged("ee0", lo, hi)
+            tt(T.ee[:, cs], win.indirect(T.eo[:, 0:n // 2]), T.thr[:, cs], A.is_ge, tk + ["eo0", "thr"], k, 8 * n, GA)
+            to_l(2, PS[2][:, lo + 1:hi:2], Z4Q, T.ee, False, ["z4q"] + k, 8 * lo, 8 * hi, False)
+        cs, k = slice(128 + 16 * lo, 128 + 16 * hi), staged("ee1", lo, hi)
+        tt(T.ee[:, cs], win.indirect(T.eo[:, 8:8 + n]), T.thr[:, cs], A.is_ge, tk + ["eo1", "thr"], k, 16 * n, GA)
+        mm(o, M4K, flag, False, False, ["m4k"] + fk, ["ps2"])
+        to_l(2, o, Z4Q, T.ee, False, ["z4q"] + k, 128 + 16 * lo, 128 + 16 * hi)
+        if per == 1:
+            ts(T.ou[:, 16 + 2 * lo:16 + 2 * hi:2], o, 4096.0, A.add, C["dum"], A.min, r=["ps2", "c_dum"], w=staged("ou0", lo, hi))
+            return
         for h_, n_ in enumerate(("dum", "dum16")):
-            ts(T.ou[:, h_:16:2], PS[2][:, h_:16:2], 0.0, A.min, C[n_], A.add, r=["ps2", "c_" + n_], w=["ou%d" % h_])
+            ts(T.ou[:, lo + h_:hi:2], PS[2][:, lo + h_:hi:2], 4096.0, A.add, C[n_], A.min, r=["ps2", "c_" + n_], w=staged("ou%d" % h_, lo, hi))
 
     def columns():
         ac(T.col[:], T.tab[:].indirect(T.fz[:]), TAB + ["fz"], ["col"], k=GA)
-        mm(PS[5][:], IB, T.tri[:], True, False, ["ib", "tri", "tri2"], ["ps5"], 512)
-        mm(PS[5][:, 0:256], BOF, T.col[:], False, False, ["bof", "col"], ["ps5"], 256)
-        mm(PS[5][:, 256:512], BOF, T.col[:], False, True, ["bof", "col"], ["ps5"], 256)
-        ac(T.frm[:], PS[5][:], ["ps5", "c_ndum"], ["frm"], 512, bias=C["ndum"])
 
-    def swapped():
-        tt(T.mm[:], T.st[:].indirect(T.ju[:]), T.col[:], A.mult, ["st", "ju", "col"], ["mm"], 256, GA)
+    def swapped(t):
+        if t == 5:
+            tt(T.lg[:], T.st[:].indirect(JU), T.col[:], A.mult, ["st", "ju", "col"], ["lg"], 256, GA)
         mm(PS[4][:, 0:256], IB, T.col[:], True, False, ["ib", "col"], ["ps4"], 256)
-        mm(PS[4][:, 0:256], BM, T.mm[:], False, True, ["bm", "mm"], ["ps4"], 256)
-        ac(T.ncl[:], PS[4][:, 0:256], ["ps4"], ["ncl"])
+        mm(PS[4][:, 0:256], BM, T.lg[:], False, True, ["bm", "lg"], ["ps4"], 256)
+        later.append(lambda w: ac(T.ncl[:], PS[4][:, 0:256], ["ps4"], ["ncl"] + list(w)))
+
+    def row_mask(t):
+        ac(T.lm[:, 256 * (t % 2):256 * (t % 2) + 256], T.lt[:].indirect(JU), ["lt", "ju"], ["lm%d" % (t % 2)], k=GA)
 
     def statics(t):
-        cp(T.ju[:], S["jj"], ["jj"], ["ju"])
-        ts(S["jm"], S["jj"], 1.0, A.add, 5.0, A.min, r=["jj"], w=["jm"])
-        if t < NSUB - 1:
-            ac(T.lm[:], T.lt[:].indirect(T.ju[:]), ["lt", "ju"], ["lm"], k=GA)
-            ac(T.nf[:], S["jj"], ["jj"], ["nf"], 16, bias=0.0, f=AF.Sign)
-            tt(S["nfd"], T.nf[:], S["fr"], A.mult, ["nf", "fr"], ["nfd"])
+        pj = PS[7][:, 0:16]
+        ac(B["jj"], pj, ["ps7"], ["jj"], 16, bias=0.0, f=AF.Relu)
         if t >= 2:
-            ts(S["j2"], S["jj"], 2.0, A.is_ge, r=["jj"], w=["j2"])
-            tt(S["cfd"], S["j2"], S["fd"], A.mult, ["j2", "fd"], ["cfd"])
+            ac(B["nc"], pj, ["ps7"], ["nc"], 16, bias=2.0, f=AF.Relu, scale=-1.0)
         if t >= 5:
-            ac(S["e5"], S["jj"], ["jj"], ["e5"], 16, bias=-396.0, f=AF.Relu, scale=99.0)
-            tt(S["thp"], S["e5"], S["th"], A.add, ["e5", "th"], ["thp"])
+            ac(B["e5"], pj, ["ps7"], ["e5"], 16, bias=-4.0, f=AF.Relu)
+        if t < NSUB - 1:
+            row_mask(t)
 
     def request(e):
         rq = T["req%d" % e]
         own = rq[:, 112:128]
-        cp(SI["fi"], T.fz[:], ["fz"], ["fi"])
+        ts(SI["fi"], T.fz[:], -1.0, A.add, r=["fz"], w=["fi"])
         ts(SI["q"], SI["fi"], 7, A.bitwise_and, r=["fi"], w=["q"])
         for h_ in range(2):
             ts(T.qo[:, 16 * h_:16 * h_ + 16], SI["q"], 2.0, A.mult, float(h_), A.add, r=["q"], w=["qo%d" % h_])
-            tt(T.uu[:, 256 * h_:256 * h_ + 256], T.hwa[:].indirect(T.qo[:, 16 * h_:16 * h_ + 16]), T.xc[:], A.mult, ["hwa", "hwown", "qo%d" % h_, "xc"], ["uu%d" % h_], 256, GA)
-        to_l(6, 32, Z1, T.uu, True, ["z1", "uu0", "uu1"])
-        cp(S["ub"], PS[6][:, 16:32], ["ps6"], ["ub"])
-        tt(SI["pr"], PS[6][:, 0:16], S["ub"], A.mult, ["ps6", "ub"], ["pr"])
+            tt(T.uu[:, 256 * h_:256 * h_ + 256], T.hwa[:].indirect(T.qo[:, 16 * h_:16 * h_ + 16]), T.xc[:], A.mult, ["hwa", "hwown", "qo%d" % h_] + staged("xc"), ["uu%d" % h_], 256, GA)
+        to_l(3, PS[3][:, 0:32], Z1, T.uu, True, ["z1", "uu0", "uu1"])
+        cp(S["ub"], PS[3][:, 16:32], ["ps3"], ["ub"])
+        tt(SI["pr"], PS[3][:, 0:16], S["ub"], A.mult, ["ps3", "ub"], ["pr"])
         ts(SI["h"], SI["pr"], 5, A.arith_shift_right, 2047, A.bitwise_and, r=["pr"], w=["h"])
-        cp(own, SI["h"], ["h"], ["rqown%d" % e])
+        ts(own, SI["h"], 1.0, A.add, r=["h"], w=["rqown%d" % e])
         to_all(own, lambda s: rq[:, 16 * slots(T, topo, s).index(rank):16 * slots(T, topo, s).index(rank) + 16], "rq%d" % e,
-               ["rqown%d" % e, "ownxb%d" % e], "rqarr%d" % e, 600)
+               ["rqown%d" % e], "rqarr%d" % e, 600, ASK)
 
     def codes():
-        cp(T.cod[:], T.sfs[:].indirect(T.du[:]), ["sfs", "du"], ["cod"], 256, GA)
+        for k, (a, b) in enumerate(CODES):
+            cp(T.cod[:, 16 * a:16 * b], T.sfs[:].indirect(T.du[:, a:b]), ["sfs", "du"], ["cod%d" % k], 16 * (b - a), GA)
 
-    def test():
-        mm(PS[0][:, 0:256], I2, T.ii[:], True, False, ["i2", "ii"], ["ps0"], 256)
-        for a in range(0, NA, 2):
-            b = min(a + 2, NA)
-            tt(T.p2[:, 256 * a:256 * b], T.pw2[:].indirect(T.cod[:, 16 * a:16 * b]), T.xe[:, 256 * a:256 * b], A.mult, PW2 + ["cod"] + XE, ["pp%d" % a], 256 * (b - a), GA)
-            for c in range(a, b):
-                for r_ in range(16):
-                    mm(PS[0][:, 16 * c:16 * c + 16], Z32(r_), T.p2[:, 256 * c + 16 * r_:256 * c + 16 * r_ + 16], False, False, ["z32", "pp%d" % a], ["ps0"])
-        cuts = list(range(NA, 14, 2)) + [14, 15, 16]
-        start, keys = NA, []
-        for a, b in zip(cuts[:-1], cuts[1:]):
-            ac(T.gg[:, 256 * a:256 * b], T.pw2[:].indirect(T.cod[:, 16 * a:16 * b]), PW2 + ["cod"], ["gg%d" % a, "cha"], 256 * (b - a), GA)
-            if b == 16:
-                for h_ in range(2):
-                    cs = slice(256 * a + 128 * h_, 256 * a + 128 * h_ + 128)
-                    tt(T.pp[:, a, 8 * h_:8 * h_ + 8], T.gg[:, cs], T.xe[:, cs], A.mult, ["gg%d" % a] + XE, ["pl%d" % h_], 128)
-            else:
-                tt(T.pp[:, a:b], T.gg[:, 256 * a:256 * b], T.xe[:, 256 * a:256 * b], A.mult, ["gg%d" % a] + XE, ["pp%d" % a], 256 * (b - a))
-                keys.append("pp%d" % a)
-            if (16 - b) % 4 == 0:
-                for r_ in range(16):
-                    mm(PS[0][:, 16 * start:16 * b], Z32(r_), T.pp[:, start:b, r_, :], False, b == 16 and r_ == 15,
-                       ["z32"] + keys + (["pl%d" % (r_ // 8)] if b == 16 else []), ["ps0"])
-                start, keys = b, []
+    def coded(a, b):
+        return ["cod%d" % j for j, (c0, c1) in enumerate(CODES) if c0 < b and a < c1]
 
-    expand(T.xt[:, 0:256], "x0", 0)
-    ac(T.lm[:], T.lt[:].indirect(T.ju[:]), ["lt", "ju"], ["lm"], k=GA)
+    def keys(lo, hi, bank):
+        k = ["ps%d" % bank]
+        mm(PS[bank][:, 0:32 * (hi - lo)], IB, T.kin[:, 2 * lo:2 * hi, :], True, False, ["ib", "kin0", "kin1"], k, max(64, 32 * (hi - lo)))
+        for eng, a, b in GATHERS:
+            if lo <= a < hi:
+                o, src = T.gg[:, 256 * a:256 * b], T.pw2[:].indirect(T.cod[:, 16 * a:16 * b])
+                (ac if eng == "act" else cp)(o, src, PW2 + coded(a, b), ["gg%d" % c for c in range(a, b)] + ["ch" + eng], 256 * (b - a), GA)
+                if eng == "act" and later and a <= LATER:
+                    later.pop(0)(["chact"])
+                for c in range(a, b):
+                    calls = []
+                    for r2 in range(8):
+                        p_, q, u = 16 * c + 2 * r2, r2 // 2, r2 % 2
+                        s0, c0 = 8 * (2 * p_ + 1 - u), 32 * (c - lo)
+                        calls.append((PS[bank][32 * q:32 * q + 32, c0:c0 + 32], T.xd[:, s0:s0 + 32], T.gg[:, 16 * p_:16 * p_ + 32], False, False))
+                    mms(calls, ["xd%d_%d" % (j, lo) for j in range(8)] + ["gg%d" % c], k, 32)
+        mm(PS[bank][:, 0:8], IB, T.xd[:, 0:8], False, True, ["ib", "xdz"], k)
+
+    def stage(t, lo, hi, per, bank, eng):
+        last, n, cs, k, me = t == NSUB - 1, 32 * (hi - lo), slice(32 * lo, 32 * hi), "ps%d" % bank, "_%d" % lo
+        ins, ik = T.inh[:, 11 * lo + t + 1:11 * hi:11], "in%d" % (t + 1) + me
+        keys(lo, hi, bank)
+        if eng == "act":
+            ac(T.ind[:, cs], PS[bank][:, 0:n], [k], ["ind" + me], n, bias=0.5, f=AF.Sign)
+        else:
+            ts(T.ind[:, cs], PS[bank][:, 0:n], -0.5, A.is_ge, -0.5, A.add, r=[k], w=["ind" + me], n=n)
+        scan(T.tot[:, cs], T.kq[:, 0:n], T.ind[:, cs], A.mult, A.add, ["kq", "ind" + me], ["tot" + me], n, CY / 2)
+        o = PS[3][:, lo:hi]
+        mm(o, M4K, T.sb[:, BK["t17"], lo:hi], True, False, ["m4k", "t17"], ["ps3"])
+        if t >= 5:
+            mm(o, M4K, T.sb[:, BK["e5"], lo:hi], False, False, ["m4k", "e5"], ["ps3"])
+        mm(o, PM, T.tot[:, 32 * lo + 31:32 * hi:32], False, True, ["pm", "tot" + me], ["ps3"])
+        ts(ins, o, 0.0, A.is_ge, r=["ps3"], w=[ik])
+        if not last:
+            scan(T.mns[:, cs], T.bq[:, 0:n], PS[bank][:, 0:n], A.add, A.min, ["bq", k], ["mns" + me], n)
+        k7, o, all_, ak = ["ps7"], PS[7][:, 16 + lo:16 + hi], T.inh[:, t + 1:176:11], staged("in%d" % (t + 1))
+        mm(o, IB, T.sb[:, BK["pb"], lo:hi], True, False, ["ib", "pb"], k7)
+        if t:
+            mms([(o, I256, T.inh[:, 11 * lo + n_:11 * hi:11], False, False) for n_ in range(1, t + 1)], ["i256"] + ["in%d" % n_ + me for n_ in range(1, t + 1)], k7)
+        if lo == 0:
+            mm(PS[7][:, 0:16], IB, B["jj"], False, False, ["ib", "jj"], k7)
+            mm(PS[7][:, 0:16], IB, ONE, False, False, ["ib", "one"], k7)
+            if t >= 5:
+                mm(PS[7][:, 0:16], NI, B["e5"], False, False, ["ni", "e5"], k7)
+            mm(PS[7][:, 32:48], IF, S["df"], False, False, ["if", "df"], k7, 256)
+            mm(PS[7][:, 32:48], M4K, ONE, False, False, ["m4k", "one"], k7)
+            mm(PS[7][:, 32:48], I4K, all_, False, False, ["i4k"] + ak, k7)
+            mm(PS[7][:, 0:16], IM8, all_, False, False, ["im8"] + ak, k7)
+        mm(o, I256, ins, False, True, ["i256", ik], k7)
+        first = 16 + lo if lo else 0
+        cp(T.nj[:, first:16 + hi], PS[7][:, first:16 + hi], k7, ["nu" + me] + ([] if lo else ["ju"]))
+        if last:
+            place(T.yxs, t + 1, lo, hi, "yxs")
+        else:
+            place(T.xc, t + 1, lo, hi, "xc")
+            expand("xc", "xc" + me, NPOOL[int(lo == 0)], lo, hi)
+        if lo == 0 and not last:
+            MNS, o = staged("mns"), PS[4][:, 0:16]
+            ts(T.mv[:], T.mns[:, 15:512:16], ROUND, A.add, -ROUND, A.add, r=MNS, w=["mv"])
+            mm(o, I16, B["jj"], True, False, ["i16", "jj"], ["ps4"])
+            for h_ in range(2):
+                mm(o, PF[h_], T.mns[:, 15 + 16 * h_:512:32], False, False, ["pf%d" % h_] + MNS, ["ps4"], 256)
+            for h_ in range(2):
+                mm(o, PH[h_], T.mv[:, h_:32:2], False, h_ == 1, ["ph%d" % h_, "mv"], ["ps4"])
+            ts(T.iu[:], o, 7.5, A.add, r=["ps4"], w=["iu"])
+            ts(T.sr[:], T.cod[:], 0.5, A.mult, 0.75, A.add, r=coded(0, 16), w=["sr"], n=256)
+            tt(T.sg[:], T.w1[:].indirect(T.iu[:]), T.sr[:], A.mult, ["w1", "iu", "sr"], ["sg"], 256, GA)
+            o = PS[6][:, 0:16]
+            if t > 0:
+                mm(o, IH, T.fr[:], True, False, ["ih", "fr"], ["ps6"])
+            mm(o, M4K, all_, t == 0, False, ["m4k"] + ak, ["ps6"])
+            to_l(6, o, ZH, T.sg, False, ["zh", "sg"])
+            cp(T.fz[:], o, ["ps6"], ["fz"])
+        if t >= 2:
+            lowest(ins, [ik], lo, hi, per)
+            scatters(T.tab, T.ncl, lambda c: ["ncl"], TAB, lo, hi, per)
+
+    for s in STAGES:
+        expand("xt", "x0", 4, s[0], s[1])
+    row_mask(0)
     codes()
+    for n in range(1, 6):
+        next_x(n, 6)
     for t in range(NSUB):
-        last, re_, ex, e = t == NSUB - 1, t >= 2, t % 5 == 4, t // 5
-        next_x(t + 1)
+        last, ex, e = t == NSUB - 1, t % 5 == 4, t // 5
+        step.clear()
+        step["on"] = 1
         if ex:
             request(e)
-        test()
-        if not last:
-            ts(T.sr[:], T.cod[:], 0.5, A.mult, -0.25, A.add, r=["cod"], w=["sr"], n=256)
-        if re_:
-            swapped()
-        ins, ik = T.inh[:, t + 1:176:11], "in_%d" % (t + 1)
-        thp, tk = (S["thp"], "thp") if t >= 5 else (S["th"], "th")
-        ts(T.ind[:], PS[0][:, 0:256], 0.0, A.is_ge, r=["ps0"], w=["ind"], n=256)
-        scan(T.cnt[:], T.kp[:], T.ind[:], A.mult, A.add, ["kp", "ind"], ["cnt"], 0.52)
-        tt(ins, T.cnt[:, 15:256:16], thp, A.is_ge, ["cnt", tk], [ik])
-        tt(S["nq"], S["nq"], ins, A.add, ["nq", ik], ["nq"])
-        ts(T.nu[:], S["nq"], 256.0, A.mult, r=["nq"], w=["nu"])
+        if t >= 2:
+            swapped(t)
+        k7 = ["ps7"]
+        for s in STAGES:
+            stage(t, *s)
         idd, idk = T.idh[:, t + 1:176:11], "id_%d" % (t + 1)
-        tt(idd, ins, S["df"], A.mult, [ik, "df"], [idk])
-        tt(S["nin"], T.cnt[:, 15:256:16], thp, A.is_lt, ["cnt", tk], ["nin"])
-        tt(S["jj"], S["nin"], S["jm"], A.mult, ["nin", "jm"], ["jj"])
-        if last:
-            place(T.yxs[:], t + 1, ["yxs"])
-            dma("sync", T.yx[:], T.yxs[:], "o_yx", ["yxs"], ["yx"], 2500)
+        ac(idd, PS[7][:, 32:48], k7, [idk], 16, bias=0.0, f=AF.Relu)
+        if ex:
+            ac(B["jj"], PS[7][:, 0:16], k7, ["jj"], 16, bias=0.0, f=AF.Relu)
         else:
-            place(T.xc[:], t + 1, ["xc"])
-            expand(T.xc[:], "xc", 0 if re_ else 2)
-            scan(T.mns[:], T.bg[:], PS[0][:, 0:256], A.add, A.min, ["bg", "ps0"], ["mns"])
-            if t == 0:
-                cp(SI["mk"], T.mns[:, 15:256:16], ["mns"], ["mk"])
-            else:
-                tt(SI["mk"], T.mns[:, 15:256:16], T.nf[:], A.add, ["mns", "nf"], ["mk"])
-            ts(SI["mk2"], SI["mk"], 31, A.bitwise_and, r=["mk"], w=["mk2"])
-            cp(T.iu[:], SI["mk2"], ["mk2"], ["iu"])
-            tt(T.sg[:], T.w2[:].indirect(T.iu[:]), T.sr[:], A.mult, ["w2", "iu", "sr"], ["sg"], 256, GA)
-            mm(PS[1][:, 0:16], I4K, ins, True, False, ["i4k", ik], ["ps1"])
-            if t > 0:
-                mm(PS[1][:, 0:16], IF, S["nfd"], False, False, ["if", "nfd"], ["ps1"], 256)
-            to_l(1, 16, ZH, T.sg, False, ["zh", "sg"])
-        if re_:
-            lowest(ins, ik, S["cfd"], "cfd")
-            scatters(T.tab, T.ncl, ["ncl"], TAB)
+            statics(t + 1)
+        if last:
+            dma("sync", T.yx[:], T.yxs[:], "o_yx", staged("yxs"), ["yx"], 2500)
+        else:
+            cp(T.fr[:], T.fz[:], ["fz"], ["fr"])
         if ex:
             xb, rq = T["xb%d" % e], T["req%d" % e]
             rk = TAB + ["rqarr%d" % e, "rqown%d" % e]
@@ -544,8 +669,9 @@ def rank_program(g, core, T, topo):
                 ac(T.hg[:, 1024 * hf + 512:1024 * hf + 1024], T.tab[:].indirect(rq[:, 64 * hf + 32:64 * hf + 64]), rk, ["hgb%d" % hf], 512, GA)
             sends = []
             for hf in range(2):
-                to_l(6 + hf, 64, ZA, T.hg, True, ["za", "hga%d" % hf, "hgb%d" % hf], 1024 * hf, 1024 * hf + 1024)
-                cp(xb[:, 144 + 64 * hf:208 + 64 * hf], PS[6 + hf][:, 0:64], ["ps%d" % (6 + hf)], ["ans%d%d" % (e, hf)], 64)
+                to_l(hf, PS[hf][:, 0:64], ZA, T.hg, True, ["za", "hga%d" % hf, "hgb%d" % hf], 1024 * hf, 1024 * hf + 1024)
+                n = 16 * len(halves(rank)[hf])
+                cp(xb[:, 144 + 64 * hf:144 + 64 * hf + n], PS[hf][:, 0:n], ["ps%d" % hf], ["ans%d%d" % (e, hf)], n)
                 en = answer_engines(rank, hf)
                 trs = []
                 for s in halves(rank)[hf]:
@@ -554,85 +680,92 @@ def rank_program(g, core, T, topo):
                                                  src=xb[:, k:k + 16], dst=xb[:, 16 * rank:16 * rank + 16]))
                     sent[0] += len(en[T.cores[s]])
                 sends.append(op("pool", lambda trs=trs: g.remote_dma_fused(trs, local_sem=T.sem.sent), ["ans%d%d" % (e, hf)], (), 600))
-            lastw["anarr%d" % e] = ("an%d" % e, ans_in, sends, 5000)
+            ac(xb[:, 16 * rank:16 * rank + 16], PS[1][:, 48:64], ["ps1"], ["ownxb%d" % e], 16)
+            lastw["anarr%d" % e] = ("an%d" % e, ans_in, sends, ANSWER)
         if not last:
-            ts(T.fz[:], PS[1][:, 0:16], float(ZC), A.min, r=["ps1"], w=["fz"])
-            for h_, n_ in enumerate(("ndum", "ndum16")):
-                ac(T.fd[:, h_:16:2], PS[1][:, h_:16:2], ["ps1", "c_" + n_], ["fd"], 16, bias=C[n_])
-            ac(S["fr"], PS[1][:, 0:16], ["ps1"], ["fr"], 16)
-            tt(T.lg[:], T.tab[:].indirect(T.fz[:]), T.lm[:], A.mult, TAB + ["fz", "lm"], ["lg"], 256, GA)
+            lmt = T.lm[:, 256 * (t % 2):256 * (t % 2) + 256]
+            tt(T.lg[:], T.tab[:].indirect(T.fz[:]), lmt, A.mult, TAB + ["fz", "lm%d" % (t % 2)], ["lg"], 256, GA)
             mm(PS[3][:, 0:16], IF, idd, True, False, ["if", idk], ["ps3"], 256)
-            to_l(3, 16, Z1, T.lg, False, ["z1", "lg"])
+            to_l(3, PS[3][:, 0:16], ZL, T.lg, False, ["zl", "lg"])
         if not ex:
             cp(T.du[:], PS[3][:, 0:16], ["ps3"], ["du"])
             codes()
             ac(S["df"], PS[3][:, 0:16], ["ps3"], ["df"], 16)
-            statics(t + 1)
             if t >= 1:
                 columns()
+                rivals(t + 1)
             continue
         if not last:
-            cp(xb[:, 128:144], PS[3][:, 0:16], ["ps3"], ["dfxb0"])
-        columns()
-        ts(S["nw"], S["jj"], 5.0, A.is_lt, 16.0, A.mult, r=["jj"], w=["nw"])
-        tt(S["t1"], S["nw"], SI["q"], A.add, ["nw", "q"], ["t1"])
-        cp(T.wu[:], S["t1"], ["t1"], ["wu"])
-        ac(T.oh[:], T.w32[:].indirect(T.wu[:]), ["w32", "wu"], ["oh"], k=GA)
-        scan(T.cum[:], T.one[:], T.oh[:], A.mult, A.add, ["one", "oh"], ["cum"], 0.52)
+            ac(xb[:, 128:144], PS[3][:, 0:16], ["ps3"], ["dfxb0"], 16)
+            columns()
+        rivals(None)
+        ts(S["nw"], B["jj"], 5.0, A.is_lt, 16.0, A.mult, r=["jj"], w=["nw"])
+        tt(S["t1"], S["nw"], SI["q"], A.add, ["nw", "q"], ["t1s"])
+        cp(T.wu[:], S["t1"], ["t1s"], ["wu"])
+        ac(T.oh[:], T.w1[:].indirect(T.wu[:]), ["w1", "wu"], ["oh"], k=GA)
+        scan(T.cum[:], T.one[:], T.oh[:], A.mult, A.add, ["one", "oh"], ["cum"], 256, CY / 2)
         ts(T.le[:], T.cum[:], 16.0, A.is_le, r=["cum"], w=["le"], n=128)
         tt(T.svr[:], T.le[:], T.oh[:], A.mult, ["le", "oh"], ["svr"], 256)
-        to_l(1, 16, ZQ, T.svr, True, ["zq", "svr"])
-        ts(T.qs[:], PS[1][:, 0:16], 8.0, A.add, r=["ps1"], w=["qs"])
-        ts(S["sv"], PS[1][:, 0:16], 0.0, A.is_lt, r=["ps1"], w=["sv"])
-        tt(T.msk[:], T.qs[:].indirect(T.bc[:, 0:16]), T.ii[:], A.is_equal, ["qs", "bc", "ii"], ["msk"], 256, GA)
-        lowest(S["sv"], "sv", S["fd"], "fd")
-        tt(T.ag[:], xb[:].indirect(T.pu[:]), T.msk[:], A.mult,
-           ["anarr%d" % e, "ans%d0" % e, "ans%d1" % e, "ownxb%d" % e, "dfxb%d" % e, "pu", "msk"], ["ag"], 256, GA)
-        scan(T.asc[:], T.kp[:], T.ag[:], A.mult, A.add, ["kp", "ag"], ["asc"])
-        an = T.asc[:, 15:256:16]
+        mm(PS[6][:, 0:16], IB, B["cb"], True, False, ["ib", "cb"], ["ps6"])
+        to_l(6, PS[6][:, 0:16], ZQ, T.svr, False, ["zq", "svr"])
+        ts(B["sv"], PS[6][:, 0:16], 128.0, A.is_lt, r=["ps6"], w=["sv"])
+        cp(T.pu[:], PS[6][:, 0:16], ["ps6"], ["pu"])
+        mm(PS[3][:, 0:16], PMT, B["sv"], True, True, ["pmt", "sv"], ["ps3"])
+        ts(T.tot[:, 31:512:32], PS[3][:, 0:16], -0.5, A.add, r=["ps3"], w=staged("tot"))
+        lowest(B["sv"], ["sv"])
         if not last:
+            mm(PS[7][:, 0:16], IB, B["jj"], True, False, ["ib", "jj"], k7)
+            mm(PS[7][:, 0:16], NI, B["sv"], False, True, ["ni", "sv"], k7)
+            cp(JU, PS[7][:, 0:16], k7, ["ju"])
+            statics(t + 1)
+            for n in range(6, 11):
+                next_x(n, 6)
+        tt(T.ag[:], xb[:, 0:144].indirect(T.pu[:]), T.dia[:], A.mult,
+           ["anarr%d" % e, "ownxb%d" % e, "dfxb%d" % e, "pu", "dia"], ["ag"], 256, GA)
+        if not last:
+            scan(T.asc[:], T.kp[:], T.ag[:], A.mult, A.add, ["kp", "ag"], ["asc"])
+            an = T.asc[:, 15:256:16]
             cp(T.du[:], an, ["asc"], ["du"])
             codes()
             ac(S["df"], an, ["asc"], ["df"], 16)
-            tt(S["jj"], S["jj"], S["sv"], A.subtract, ["jj", "sv"], ["jj"])
-            statics(t + 1)
-            cp(T.hl[:, 0:16], an, ["asc"], ["hl0"])
-            tt(T.hl[:, 16:32], an, T.hl[:, 0:16], A.subtract, ["asc", "hl0"], ["hl1"])
-            for hf in range(2):
-                tt(T.dg[:, 256 * hf:256 * hf + 256], T.hl[:].indirect(T.bc[:, 16 * hf:16 * hf + 16]), T.dia[:], A.mult, ["hl0", "hl1", "bc", "dia"], ["dg%d" % hf], 256, GA)
+            ac(T.dg[:, 0:256], T.ag[:], ["ag"], ["dg0"])
+            tt(T.dg[:, 256:512], T.ag[:], T.dg[:, 0:256], A.subtract, ["ag", "dg0"], ["dg1"], 512)
             mm(PS[4][:, 0:256], IKP, T.col[:], True, False, ["ikp", "col"], ["ps4"], 256)
             mm(PS[4][:, 0:256], Z1(3), T.dg[:, 0:256], False, False, ["z1", "dg0"], ["ps4"], 256)
             mm(PS[4][:, 0:256], Z1(7), T.dg[:, 256:512], False, True, ["z1", "dg1"], ["ps4"], 256)
             ac(T.ncl[:], PS[4][:, 0:256], ["ps4"], ["ncl"])
-            scatters(T.tab, T.ncl, ["ncl"], TAB)
-            ac(T.col[:], T.tab[:].indirect(T.fz[:]), TAB + ["fz"], ["col"], k=GA)
+            scatters(T.tab, T.ncl, lambda c: ["ncl"], TAB)
+            columns()
+            rivals(t + 1)
             continue
-        ts(T.nih[:], T.inh[:], -1.0, A.mult, 1.0, A.add, r=["in_%d" % k for k in range(11)], w=["nih"], n=176)
-        scan(T.csc[:], T.nih[:], T.idh[:], A.mult, A.add, ["nih"] + ["id_%d" % k for k in range(11)], ["csc"])
+        ts(T.nih[:], T.inh[:], -1.0, A.mult, 1.0, A.add, r=["in_0"] + [x for k in range(1, 11) for x in staged("in%d" % k)], w=["nih"], n=176)
+        scan(T.csc[:], T.nih[:], T.idh[:], A.mult, A.add, ["nih"] + ["id_%d" % k for k in range(11)], ["csc"], 176)
         cp(S["yc"], T.csc[:, 10:176:11], ["csc"], ["ycs"])
         dma("sync", T.yc[:], S["yc"], "o_yc", ["ycs"], ["yc"], 2500)
         for q in range(4):
-            cs = slice(512 * q, 512 * q + 512)
-            b3, ba = (0, 3)[q % 2], (5, 7)[q % 2]
-            mm(PS[ba][0:32, :], SELY, T.tab[:, cs], True, True, ["sely"] + TAB, ["ps%d" % ba], 512)
-            mm(PS[b3][:], Z37(0), T.tab[:, cs], True, True, ["z37"] + TAB, ["ps%d" % b3], 512)
-            ac(T.y3[:, cs], PS[b3][:], ["ps%d" % b3], ["y3%d" % q], 512)
+            cs, ct = slice(512 * q, 512 * q + 512), slice(512 * q + 1, 512 * q + 513)
+            b3, ba = (3, 7)[q % 2], (0, 1)[q % 2]
+            mm(PS[ba][0:32, :], SELY, T.tab[:, ct], True, True, ["sely"] + TAB, ["ps%d" % ba], 512)
+            mm(PS[b3][:], Z37(0), T.tab[:, ct], True, True, ["z37"] + TAB, ["ps%d" % b3], 512)
+            ac(T.y3[:, ct], PS[b3][:], ["ps%d" % b3], ["y3%d" % q], 512)
             if q % 2:
                 ac(T.ya[0:32, cs], PS[ba][0:32, :], ["ps%d" % ba], ["ya%d" % q], 512)
             else:
                 cp(T.ya[0:32, cs], PS[ba][0:32, :], ["ps%d" % ba], ["ya%d" % q], 512)
         dma("sync", T.yt[:], T.ya[0:32, :], "o_ya", ["ya%d" % q for q in range(4)], ["yt"], 3000)
-        tt(T.dgf[:], T.asc[:].indirect(T.b15[:]), T.dia[:], A.mult, ["asc", "b15", "dia"], ["dgf"], 256, GA)
         for hf in (1, 0):
             cs = slice(128 * hf, 128 * hf + 128)
-            mm(PS[(4, 6)[hf]][:, 0:128], ZF, T.dgf[:, cs], True, True, ["zf", "dgf"], ["ps%d" % (4, 6)[hf]], 512)
-            cp(T.anr[:, cs], PS[(4, 6)[hf]][:, 0:128], ["ps%d" % (4, 6)[hf]], ["anr%d" % hf], 128)
-        Y3 = ["y3%d" % q for q in range(4)] + ["y3z"]
-        for c in range(7, -1, -1):
-            cp(T.y3[:].indirect(T.ou[:, 2 * c:2 * c + 2]), T.anr[:, 32 * c:32 * c + 32], ["ou0", "ou1", "anr%d" % (c // 4)], Y3, 32, SC)
-        dma("sync", T.yt[3:32:4, :], T.y3[0:128:16, 0:2048], "o_y3", Y3, ["yt"], 2500)
+            mm(PS[(4, 6)[hf]][:, 0:128], ZF, T.ag[:, cs], True, True, ["zf", "ag"], ["ps%d" % (4, 6)[hf]], 512)
+            if hf:
+                cp(T.anr[:, cs], PS[6][:, 0:128], ["ps6"], ["anr1"], 128)
+            else:
+                ac(T.anr[:, cs], PS[4][:, 0:128], ["ps4"], ["anr0"], 128)
+        scatters(T.y3, T.anr, lambda c: ["anr%d" % (c // 8)], ["y3%d" % q for q in range(4)] + ["y3z", "y3y"])
+        dma("sync", T.yt[3:32:4, :], T.y3[0:128:16, 1:2049], "o_y3", ["y3%d" % q for q in range(4)], ["yt"], 2500)
 
-    order = schedule(ops)
+    if len(ops) not in ORDER:
+        ORDER[len(ops)] = schedule(ops)
+    order = ORDER[len(ops)]
     pos = {i: k for k, i in enumerate(order)}
     known, plan = {e_: {} for e_ in Q}, []
     for i in order:

@@ -4,18 +4,24 @@ from concourse.mybir import AluOpType as A, ActivationFunctionType as AF
 
 F32, B16, I32, U16, F16 = "float32", "bfloat16", "int32", "uint16", "float16"
 N, NSUB, TW = 8, 10, 2096
-STAGES = ((6, 16, 2, 0, "dve"), (0, 6, 2, 1, "act"))
-GATHERS = (("act", 14, 16), ("dve", 12, 14), ("dve", 10, 12), ("act", 8, 10), ("dve", 6, 8), ("act", 4, 6), ("act", 2, 4), ("act", 0, 2))
-LATER = 14
+BANKS = ((4, 16, 0, "act"), (0, 4, 1, "dve"))
+STAGES = ((0, 16, 2),)
+MOVES = ((0, 16),)
+FRAC, SRT, HALF, LGS = 0, 2, 0.49995, 0
+GATHERS = (("act", 14, 16), ("dve", 12, 14), ("act", 10, 12), ("dve", 8, 10), ("act", 6, 8), ("dve", 4, 6), ("act", 2, 4), ("dve", 0, 2))
+LATER = (None, None)
 SPANS = []
-SHIFT = 1500
+ASKS, XB = (2, 3, 3), 0
+SGS = ((0, 16),)
+QUEUES, FREE = {}, {}
+SHIFT, SLACK = 600, 200
 CODES = ((12, 16), (0, 12))
-NPOOL = (8, 4)
+NPOOL = (5, 5)
 ROUND = 12582912.0
-GA, SC, CY, PE = 1.33, 3.2, 0.85, 0.43
-RULE, SAME, CROSS, FIX = 0.5, 100, 130, 50
-PASSES, ORDER = 500, {}
-LOADS, ASK, ANSWER = (2500, 4500, 11000, 12000), 3000, 3000
+GA, SC, CY, PE = 1.33, 3.2, 0.85, 0.47
+RULE, SAME, CROSS, FIX = 0.5, 160, 170, 50
+PASSES, ORDER = (((6, 7, 8), 5000), ((-1, 0, 1, 2), 3000), ((3, 4, 5, 6), 3000), ((8, 9), 2000), (range(-1, 10), 2000)), {}
+LOADS, ASK, ANSWER = (2200, 3600, 7500, 8200), 4000, 3500
 
 
 def _s(shape, d):
@@ -31,14 +37,14 @@ SCRATCH = {
     "cod": _s([128, 256], U16), "sr": _s([128, 256], I32), "ind": _s([128, 512], B16), "mns": _s([128, 512], F32),
     "tot": _s([128, 512], B16), "sg": _s([128, 256], F16), "ee": _s([128, 384], B16), "thr": _s([128, 384], B16), "lg": _s([128, 256], B16),
     "lm": _s([128, 512], B16), "col": _s([128, 256], B16), "mm": _s([128, 256], B16), "ncl": _s([128, 256], B16),
-    "t0": _s([128, 256], B16), "t1": _s([128, 256], B16), "t2": _s([128, 512], B16), "t3": _s([128, 512], B16), "thq": _s([128, 16], F32),
+    "t0": _s([128, 256], B16), "t1": _s([128, 256], B16), "sh": _s([128, 256], F32), "thq": _s([128, 16], F32),
     "uu": _s([128, 512], B16), "hg": _s([128, 2048], B16), "dg": _s([128, 512], B16),
     "ag": _s([128, 256], F32), "ya": _s([128, 2048], F32), "y3": _s([128, TW], F32),
     "yxs": _s([128, 256], F32), "anr": _s([128, 256], F32), "oh": _s([128, 256], B16), "cum": _s([128, 256], B16),
     "le": _s([128, 256], B16), "svr": _s([128, 256], B16), "asc": _s([128, 256], F32),
     "req0": _s([128, 128], U16), "req1": _s([128, 128], U16), "xb0": _s([128, 256], F32), "xb1": _s([128, 256], F32),
     "inh": _s([128, 176], B16), "idh": _s([128, 176], F32), "nih": _s([128, 176], F32), "csc": _s([128, 176], F32),
-    "sm": _s([128, 8, 16], F32), "sb": _s([128, 8, 16], B16), "si": _s([128, 4, 16], I32), "mv": _s([128, 32], F16),
+    "sm": _s([128, 8, 16], F32), "sb": _s([128, 8, 16], B16), "si": _s([128, 4, 16], I32), "mv": _s([128, 32], F16), "mw": _s([128, 32], F16),
     "fs": _s([128, 24], F16), "fr": _s([128, 16], F16),
     "du": _s([128, 16], U16), "fz": _s([128, 16], U16), "iu": _s([128, 16], U16), "nj": _s([128, 32], U16),
     "ou": _s([128, 48], U16), "qo": _s([128, 32], U16), "wu": _s([128, 16], U16), "eo": _s([128, 24], U16),
@@ -48,7 +54,7 @@ SCRATCH = {
     "kq": _s([128, 384], B16), "bq": _s([128, 384], B16),
     "one": _s([128, 256], B16), "tri": _s([128, 384], B16), "dia": _s([128, 256], B16), "fh": _s([128, 512], B16),
     "fl": _s([128, 512], B16), "zz": _s([128, 6, 144], B16), "zh": _s([128, 144], F16), "mb": _s([128, 24, 128], B16),
-    "mf": _s([128, 4, 128], F32), "mh": _s([128, 4, 128], F16), "hq": _s([128, 7, 144], B16), "w1": _s([128, 96], B16), "lt": _s([128, 16], B16),
+    "mf": _s([128, 4, 128], F32), "mh": _s([128, 4, 128], F16), "hq": _s([128, 7, 144], B16), "w1": _s([128, 176], B16), "lt": _s([128, 16], B16),
     "st": _s([128, 16], B16), "r3": _s([128, 16], F32),
 }
 for _b in range(8):
@@ -102,56 +108,91 @@ def schedule(ops):
             pre.setdefault(d, 0)
         for d, l in pre.items():
             succ[d].append((i, l))
-    prio = [0.0] * n
-    for i in range(n - 1, -1, -1):
-        prio[i] = ops[i]["cost"] + max([l + prio[j] for j, l in succ[i]] + [ops[i]["lat"]])
-    pred = [[] for _ in range(n)]
+    at = {(o["step"], o["eng"], o["kind"][0][1] + str(o["kind"][1])): i for i, o in enumerate(ops)}
+    for eng, names in QUEUES.items():
+        for t in range(NSUB):
+            row = [at.get((t - x.startswith("-"), eng, x.strip("-"))) for x in names.split() if x.strip("-") not in FREE.get(t, "").split()]
+            row = [i for i in row if i is not None]
+            for a, b in zip(row, row[1:]):
+                succ[a].append((b, 0))
+    left, order = [0] * n, []
     for i in range(n):
         for j, l in succ[i]:
-            pred[j].append((i, l))
-    tail = [o["lat"] for o in ops]
-    best, rng = None, np.random.default_rng(0)
-    kinds = {}
+            left[j] += 1
+    todo = [i for i in range(n - 1, -1, -1) if not left[i]]
+    while todo:
+        order.append(todo.pop())
+        for j, l in succ[order[-1]]:
+            left[j] -= 1
+            if not left[j]:
+                todo.append(j)
+    assert len(order) == n
+    prio = [0.0] * n
+    for i in reversed(order):
+        prio[i] = ops[i]["cost"] + max([l + prio[j] for j, l in succ[i]] + [ops[i]["lat"]])
+    shift = {}
+    for steps, passes in PASSES:
+        part = [i for i in order if ops[i]["step"] in steps]
+        new = {i: k for k, i in enumerate(part)}
+        end = settle([ops[i] for i in part], [[(new[j], l) for j, l in succ[i] if j in new] for i in part], [prio[i] for i in part], shift, passes)
+    return sorted(range(n), key=lambda i: (end[new[i]] - ops[i]["cost"], new[i]))
+
+
+def settle(ops, succ, prio, shift, passes):
+    n, kinds = len(ops), {}
     for i, o in enumerate(ops):
         kinds.setdefault(o["kind"], []).append(i)
-    kinds = list(kinds.values())
-    for k in range(PASSES):
-        end = deal(ops, succ, prio, [0.0] * n)
-        back = deal(ops, pred, end, list(tail))
-        end = deal(ops, succ, back, [0.0] * n)
-        span = max(e + l for e, l in zip(end, tail))
-        if best is None or span <= best[0]:
-            best = (span, end, back)
-        prio = list(best[2]) if k % 2 else [o["cost"] - e for o, e in zip(ops, best[1])]
-        shift = float(rng.random()) * SHIFT
-        for i in kinds[int(rng.integers(len(kinds)))]:
-            prio[i] += shift
-        for i in range(n - 1, -1, -1):
-            for j, l in succ[i]:
-                if prio[i] <= prio[j]:
-                    prio[i] = prio[j] + 1
-        SPANS.append(span)
-    return sorted(range(n), key=lambda i: (best[1][i] - ops[i]["cost"], i))
+    pick = [k for k, v in kinds.items() if k not in shift] or list(kinds)
+    shift.update({k: 0.0 for k in kinds if k not in shift})
+    cost, tail, eng = [o["cost"] for o in ops], [o["lat"] for o in ops], [o["eng"] for o in ops]
+    back = [(i, [j for j, l in succ[i]]) for i in range(n - 1, -1, -1) if succ[i]]
+    now = [p + shift.get(o["kind"], 0.0) for p, o in zip(prio, ops)]
+    best, span, rng = None, 1e30, np.random.default_rng(0)
+    for k in range(passes):
+        kind, d, p = pick[int(rng.integers(len(pick)))], float(rng.normal()) * SHIFT * (k > 0), list(now)
+        for i in kinds[kind]:
+            p[i] += d
+        for i, js in back:
+            top = max([p[j] for j in js])
+            if p[i] <= top:
+                p[i] = top + 1
+        end = deal(cost, eng, succ, p)
+        time = max([e + l for e, l in zip(end, tail)])
+        if time <= span - SLACK * (1 - k / passes) * float(np.log(1 - rng.random())):
+            span = time
+            shift[kind] = shift.get(kind, 0.0) + d
+            for i in kinds[kind]:
+                now[i] += d
+            if best is None or time < best[0]:
+                best = (time, end, dict(shift))
+    shift.update(best[2])
+    SPANS.append(best[0])
+    return best[1]
 
 
-def deal(ops, succ, prio, ready):
-    busy, end = {}, [0.0] * len(ops)
-    for i in sorted(range(len(ops)), key=lambda i: -prio[i]):
-        l, st, cost = busy.setdefault(ops[i]["eng"], []), ready[i], ops[i]["cost"]
-        a, b = 0, len(l)
-        while a < b:
-            m = (a + b) // 2
-            if l[m][1] <= st:
-                a = m + 1
-            else:
-                b = m
-        while a < len(l) and l[a][0] < st + cost:
-            st = max(st, l[a][1])
-            a += 1
-        l.insert(a, (st, st + cost))
-        end[i] = st + cost
+def deal(cost, eng, succ, prio):
+    n = len(cost)
+    busy, end, ready = {e: [] for e in eng}, [0.0] * n, [0.0] * n
+    for i in sorted(range(n), key=lambda i: -prio[i]):
+        l, st, c = busy[eng[i]], ready[i], cost[i]
+        a = len(l)
+        if a and l[-1][1] > st:
+            b, a = a, 0
+            while a < b:
+                m = (a + b) // 2
+                if l[m][1] <= st:
+                    a = m + 1
+                else:
+                    b = m
+            b = len(l)
+            while a < b and l[a][0] < st + c:
+                st = l[a][1]
+                a += 1
+        e = end[i] = st + c
+        l.insert(a, (st, e))
         for j, lat in succ[i]:
-            ready[j] = max(ready[j], end[i] + lat)
+            if ready[j] < e + lat:
+                ready[j] = e + lat
     return end
 
 
@@ -172,10 +213,10 @@ def rank_program(g, core, T, topo):
         for k in w:
             for x in readers.get(k, []) + ([lastw[k]] if k in lastw else []):
                 (order if k.startswith("ch") or (eng == "pe" and ops[x]["eng"] == "pe") else deps).append(x)
-        kind = (eng, "".join(x for x in (w or r)[0].split("_")[0] if x > "9"), (w or r)[0].split("_")[1:] if step else len(ops))
-        kind = repr(kind) + (w or r)[0] * (w or r)[0].startswith("ps")
+        name = (w or r)[0]
+        kind = (eng, name if name.startswith("ps") or "t" not in step else "".join(x for x in name.split("_")[0] if x > "9"), "t" in step)
         step[kind] = step.get(kind, 0) + 1
-        ops.append({"kind": (kind, step[kind]), "eng": eng, "fn": fn, "deps": deps, "ord": order, "dma": dma, "sig": False, "cost": cost, "lat": lat})
+        ops.append({"kind": (kind, step[kind]), "step": step.get("t", -1), "eng": eng, "fn": fn, "deps": deps, "ord": order, "dma": dma, "sig": False, "cost": cost, "lat": lat})
         me_ = len(ops) - 1
         for k in r:
             readers.setdefault(k, []).append(me_)
@@ -240,8 +281,8 @@ def rank_program(g, core, T, topo):
     def ZH(r_):
         return T.zh[:, 15 - r_:143 - r_]
 
-    def staged(name, lo=0, hi=16):
-        return ["%s_%d" % (name, s[0]) for s in STAGES if s[0] < hi and lo < s[1]]
+    def staged(name, lo=0, hi=16, parts=None):
+        return ["%s_%d" % (name, s[0]) for s in parts or STAGES if s[0] < hi and lo < s[1]]
 
     peers = [s for s in range(N) if s != rank]
     far = [s for s in peers if topo.chip(T.cores[s]) != topo.chip(core)]
@@ -284,7 +325,7 @@ def rank_program(g, core, T, topo):
     dma("sync", T.otq[:], T.ot[:], "l_ot", [], ["otq", "chs"], LOADS[3])
     dma("sync", T.hwa[:, 2 * rank:2 * rank + 2], T.hw[:], "l_hw", [], ["hwown", "chs"], LOADS[3])
 
-    KW = 32 * max(s[1] - s[0] for s in STAGES)
+    KW = 32 * max(s[1] - s[0] for s in BANKS)
     iota(T.pi[:, 0:1], [[0, 1]], 0, 1, ["pi"], 1, False)
     iota(T.ro[:], [[1, 144]], 0, 0, ["ro"], 144)
     iota(T.ii[:], [[0, 16], [1, 16]], 0, 0, ["ii"], 256)
@@ -314,8 +355,8 @@ def rank_program(g, core, T, topo):
     BK = {n_: k for k, n_ in enumerate(("jj", "nc", "e5", "t17", "pb", "sv", "th", "cb"))}
     B = {n_: T.sb[:, k] for n_, k in BK.items()}
     SI = {n_: T.si[:, k] for k, n_ in enumerate(("fi", "q", "pr", "h"))}
-    IB, I4K, BM, BOF, IKP, SELY, IM8 = T.mb[:, 0], T.mb[:, 6], T.mb[:, 7], T.mb[:, 8], T.mb[:, 9], T.mb[:, 10, 0:32], T.mb[:, 14]
-    M4K, NI, I16, I256, PM, PMT = [T.mb[:, k] for k in range(15, 21)]
+    IB, BM, BOF, IKP, SELY = T.mb[:, 0], T.mb[:, 7], T.mb[:, 8], T.mb[:, 9], T.mb[:, 10, 0:32]
+    NI, PM, PMT, DH = T.mb[:, 6], T.mb[:, 14], T.mb[:, 15], (T.mb[:, 16], T.mb[:, 17])
     IF, ZF, PF, PH, NPT, IH = T.mf[:, 0], T.mf[:, 1], (T.mf[:, 2], T.mf[:, 3]), (T.mh[:, 0], T.mh[:, 1]), T.mh[:, 2], T.mh[:, 3]
     R128, ONE = T.ro[:, 0:128], T.one[:, 0:16]
     JU = T.nj[:, 0:16]
@@ -326,7 +367,7 @@ def rank_program(g, core, T, topo):
             ("k", "g16", 1.0, "rq", AF.Identity), ("k8", "k", 1.0, 12.0, AF.Identity), ("m0", "rq", 1.0, -2.0, AF.Relu),
             ("mid", "m0", -1.0, 1.0, AF.Identity), ("dum", "r", 1.0, 2049.0, AF.Identity), ("dum16", "r", 1.0, 2065.0, AF.Identity),
             ("lt8", "u2", -0.5, 1.0, AF.Identity), ("ge8", "u2", 0.5, 0.0, AF.Identity), ("rm8", "r", 16.0, -128.0, AF.Identity),
-            ("y", "g16", 0.25, "r3", AF.Identity), ("wl", "ge8", -1.0, "b0", AF.Abs)):
+            ("y", "g16", 0.25, "r3", AF.Identity), ("rm1", "r", 16.0, -16.0, AF.Identity), ("wl", "ge8", -1.0, "b0", AF.Abs)):
         ac(colf(name), C[a], named(a, b), ["c_" + name], 1, bias=C.get(b, b), f=f, scale=s)
     ts(colf("s1"), C["b2"], 2.0, A.add, C["lt8"], A.mult, r=named("lt8"), w=["c_s1"])
 
@@ -343,11 +384,12 @@ def rank_program(g, core, T, topo):
     eq(T.zz[:, 0], T.ro[:], "ro", "aq", 4096.0, "z4q", 144)
     eq(T.zz[:, 1], T.ro[:], "ro", "a", None, "z1", 144)
     cp(T.zh[:], T.zz[:, 1], ["z1"], ["zh"], 72)
-    eq(T.w1[:], T.ro[:, 0:96], "ro", "r", None, "w1", 96)
+    eq(T.w1[:, 0:16], T.ro[:, 0:16], "ro", "r", None, "w1", 16)
+    ms(T.w1[:, 16:176], 0.0, ["w1z"], 160)
     for h_, a in enumerate(("nh16", "h16")):
         scaled(PF[h_], PM, "pm", a, "pf%d" % h_, 128)
         ts(PH[h_], PM, C[a], A.mult, -1.0, A.mult, r=["pm", "c_" + a], w=["ph%d" % h_])
-    for out, s, w in ((I4K, 4096.0, "i4k"), (IF, 1.0, "if"), (IM8, -8.0, "im8"), (M4K, -4096.0, "m4k"), (NI, -1.0, "ni"), (I16, 16.0, "i16"), (I256, 256.0, "i256")):
+    for out, s, w in ((IF, 1.0, "if"), (NI, -1.0, "ni"), (DH[0], "nh", "dh0"), (DH[1], "h", "dh1")):
         scaled(out, IB, "ib", s, w, 128)
     cp(IH, IB, ["ib"], ["ih"])
     scaled(ZF, Z1(0), "z1", 1.0, "zf", 128)
@@ -384,19 +426,19 @@ def rank_program(g, core, T, topo):
     ts(T.bq[:, 0:KW], T.j32[:, 0:KW], C["h16"], A.is_equal, 1.0e6, A.mult, r=["j32", "c_h16"], w=["bq"], n=KW // 2)
     ts(T.eo[:, 0:8], T.ro[:, 0:8], 64.0, A.mult, 31.0, A.add, r=["ro"], w=["eo0"])
     ts(T.eo[:, 8:24], T.ro[:, 0:16], 32.0, A.mult, 31.0, A.add, r=["ro"], w=["eo1"])
-    ac(B["pb"], T.ro[:, 0:16], ["ro", "cf"], ["pb"], 16, bias=C["r"], scale=16.0)
+    ac(B["pb"], T.ro[:, 0:16], ["ro", "c_rm1"], ["pb"], 16, bias=C["rm1"], scale=256.0)
     ac(B["cb"], T.ro[:, 0:16], ["ro"], ["cb"], 16, bias=128.0)
     cp(T.bc[:], T.ro[:, 0:16], ["ro"], ["bc"])
-    cp(T.du[:], T.c0s[:], ["c0s"], ["du"])
+    cp(T.du[:], T.c0s[:], ["c0s"], ["du0", "du1"])
     cp(B["th"], T.ths[:], ["ths"], ["th"])
-    ac(B["t17"], B["th"], ["th"], ["t17"], 16, bias=-16.0, f=AF.Relu)
-    cp(S["df"], T.c0s[:], ["c0s"], ["df"])
-    ac(T.idh[:, 0:176:11], S["df"], ["df"], ["id_0"], 16)
-    ms(T.xd[:], 0.0, ["xdz"] + [x for k in range(8) for x in staged("xd%d" % k)], 4096)
+    ac(B["t17"], B["th"], ["th"], ["t17"], 16, bias=-65536.0, f=AF.Relu, scale=4096.0)
+    cp(S["df"], T.c0s[:], ["c0s"], ["df0", "df1"])
+    ac(T.idh[:, 0:176:11], S["df"], ["df0", "df1"], ["id_0"], 16)
+    ms(T.xd[:], 0.0, ["xdz"] + [x for k in range(8) for x in staged("xd%d" % k, 0, 16, MOVES)], 4096)
     ms(T.one[:], 1.0, ["one"], 256)
     ms(JU, 0, ["ju"])
     ms(B["jj"], 0.0, ["jj"])
-    ms(T.inh[:, 0:176:11], 1.0, ["in_0"])
+    ms(T.inh[:, 0:176:11], 4096.0, ["in_0"])
     ms(T.tab[:, 0:1], 0.0, ["tabz"])
     ms(T.tab[:, 2049:TW], 0.0, ["taby"])
     ms(T.y3[:, 0:1], 0.0, ["y3z"])
@@ -408,12 +450,12 @@ def rank_program(g, core, T, topo):
     ac(T.thq[:], PS[4][:, 0:16], ["ps4"], ["thq"], 16)
     tt(T.t0[:], T.thq[:].indirect(T.bc[:]), T.ii[:], A.add, ["thq", "bc", "ii"], ["t0"], 256, GA)
     ac(T.t0[:], T.t0[:], ["t0"], ["t0"], bias=15.5, f=AF.Sign, scale=-1.0)
-    ts(T.t1[:], T.ii[:], -7.5, A.add, 1.0 / 16, A.mult, r=["ii"], w=["t1"], n=128)
-    for h_, (own, other) in enumerate((("nh", "h"), ("h", "nh"))):
-        cs = slice(256 * h_, 256 * h_ + 256)
-        scaled(T.t2[:, cs], T.t1[:], "t1", own, "t2%d" % h_, 256)
-        ts(T.t3[:, cs], T.t0[:], C[other], A.mult, 4096.0, A.mult, r=["t0"] + named(other), w=["t3%d" % h_], n=128)
-        tt(T.kin[:, h_:32:2, :], T.t2[:, cs], T.t3[:, cs], A.add, ["t2%d" % h_, "t3%d" % h_], ["kin%d" % h_], 256)
+    ac(T.t1[:], T.ii[:], ["ii"], ["t1"], bias=-7.5 / 65536, scale=1.0 / 65536)
+    for h_ in range(2):
+        o, k = PS[h_][:, 0:256], ["ps%d" % h_]
+        mm(o, DH[h_], T.t1[:], True, False, ["dh%d" % h_, "t1"], k, 256)
+        mm(o, DH[1 - h_], T.t0[:], False, True, ["dh%d" % (1 - h_), "t0"], k, 256)
+        ac(T.kin[:, h_:32:2, :], o, k, ["kin%d" % h_], scale=4096.0)
 
     for h_ in range(2):
         cp(T.pw2[:, 2048 * h_:2048 * h_ + 2048:2], T.pws[:, 1024 * h_:1024 * h_ + 1024], ["pws"], ["pw2a%d" % h_], 512)
@@ -456,11 +498,11 @@ def rank_program(g, core, T, topo):
         o, k = PS[bank][:, 0:256], ["ps%d" % bank]
         mm(o, IB, a, True, False, ["ib", "x%d" % (n - 1)], k, 256)
         mm(o, IB, T.stp[:], False, True, ["ib", "stp"], k, 256)
-        ac(T.xa[:], o, k, ["xa"], bias=-15.5, f=AF.Sign)
+        ac(T.xa[:], o, k, ["xa"], bias=3064.5)
         mm(o, IB, a, True, False, ["ib", "x%d" % (n - 1)], k, 256)
         mm(o, IB, T.stp[:], False, False, ["ib", "stp"], k, 256)
-        mm(o, IM8, T.xa[:], False, True, ["im8", "xa"], k, 256)
-        ac(b, o, k, ["x%d" % n], bias=-8.0)
+        mm(o, NI, T.xa[:], False, True, ["ni", "xa"], k, 256)
+        ac(b, o, k, ["x%d" % n], bias=3072.0)
 
     def place(out, n, lo, hi, w):
         ac(out[:, 16 * lo:16 * hi], T.xt[:, 0:256 * n + 256].indirect(T.nj[:, 16 + lo:16 + hi]), ["x%d" % k for k in range(n + 1)] + ["nu_%d" % lo],
@@ -476,9 +518,9 @@ def rank_program(g, core, T, topo):
         bad = [] if t is None else ["nc", "t17"] + (["e5"] if t >= 5 else [])
         p0 = 0 if t is None else min([8] + [s[0] // 2 for s in STAGES if s[2] == 2])
         parts = [(PS[5][:, 384 + p0:392], slice(2 * p0, 16, 2))] * (p0 < 8) + [(PS[5][:, 392:408], slice(0, 16))]
-        calls = [(o, I4K, T.sb[:, BK[n_], cs]) for o, cs in parts for n_ in bad]
+        calls = [(o, IB, T.sb[:, BK[n_], cs]) for o, cs in parts for n_ in bad]
         if bad:
-            mms([c + (j == 0, False) for j, c in enumerate(calls)], ["i4k"] + bad, k)
+            mms([c + (j == 0, False) for j, c in enumerate(calls)], ["ib"] + bad, k)
         mms([(o, IH, T.fr[:, cs], j == 0 and not bad, j == len(parts) - 1) for j, (o, cs) in enumerate(parts)], ["ih", "fr"], k)
         ts(T.fs[:, p0:24], PS[5][:, 384 + p0:408], 4000.0, A.min, r=k, w=["fs"])
         mm(PS[5][:, 16 * p0:384], IB, T.tri[:, 16 * p0:384], True, False, ["ib", "tri", "triz"], k, 384 - 16 * p0)
@@ -486,16 +528,10 @@ def rank_program(g, core, T, topo):
         mm(PS[5][:, 128:384], BOF, T.col[:], False, p0 == 8, ["bof", "col"], k, 256)
         if p0 < 8:
             mms([(PS[5][:, 16 * c:16 * c + 16], BOF, T.col[:, 32 * c + 16:32 * c + 32], False, c == 7) for c in range(p0, 8)], ["bof", "col"], k)
+        ac(T.thr[:, 16 * p0:384], PS[5][:, 16 * p0:384], k, ["thr"], 384 - 16 * p0, bias=-64.0, f=AF.Abs, scale=64.0)
 
-        def copy(w):
-            ac(T.thr[:, 16 * p0:384], PS[5][:, 16 * p0:384], k, ["thr"] + w, 384 - 16 * p0, bias=0.0, f=AF.Abs, scale=64.0)
-        if t is None:
-            copy([])
-        else:
-            later.append(copy)
-
-    def lowest(flag, fk, lo=0, hi=16, per=2):
-        n, win, tk, o = hi - lo, T.tot[:, 32 * lo:32 * hi], staged("tot", lo, hi), PS[2][:, lo:hi]
+    def lowest(tk, flag, fk, lo=0, hi=16, per=2):
+        n, win, o = hi - lo, T.tot[:, 32 * lo:32 * hi], PS[2][:, lo:hi]
         mm(o, IH, T.fs[:, 8 + lo:8 + hi], True, False, ["ih", "fs"], ["ps2"])
         if per == 2:
             cs, k = slice(8 * lo, 8 * hi), staged("ee0", lo, hi)
@@ -503,45 +539,51 @@ def rank_program(g, core, T, topo):
             to_l(2, PS[2][:, lo + 1:hi:2], Z4Q, T.ee, False, ["z4q"] + k, 8 * lo, 8 * hi, False)
         cs, k = slice(128 + 16 * lo, 128 + 16 * hi), staged("ee1", lo, hi)
         tt(T.ee[:, cs], win.indirect(T.eo[:, 8:8 + n]), T.thr[:, cs], A.is_ge, tk + ["eo1", "thr"], k, 16 * n, GA)
-        mm(o, M4K, flag, False, False, ["m4k"] + fk, ["ps2"])
+        mm(o, NI, flag, False, False, ["ni"] + fk, ["ps2"])
         to_l(2, o, Z4Q, T.ee, False, ["z4q"] + k, 128 + 16 * lo, 128 + 16 * hi)
         if per == 1:
-            ts(T.ou[:, 16 + 2 * lo:16 + 2 * hi:2], o, 4096.0, A.add, C["dum"], A.min, r=["ps2", "c_dum"], w=staged("ou0", lo, hi))
+            ts(T.ou[:, 16 + 2 * lo:16 + 2 * hi:2], o, 4097.0, A.add, C["dum"], A.min, r=["ps2", "c_dum"], w=staged("ou0", lo, hi))
             return
         for h_, n_ in enumerate(("dum", "dum16")):
-            ts(T.ou[:, lo + h_:hi:2], PS[2][:, lo + h_:hi:2], 4096.0, A.add, C[n_], A.min, r=["ps2", "c_" + n_], w=staged("ou%d" % h_, lo, hi))
+            ts(T.ou[:, lo + h_:hi:2], PS[2][:, lo + h_:hi:2], 4097.0, A.add, C[n_], A.min, r=["ps2", "c_" + n_], w=staged("ou%d" % h_, lo, hi))
 
     def columns():
         ac(T.col[:], T.tab[:].indirect(T.fz[:]), TAB + ["fz"], ["col"], k=GA)
 
     def swapped(t):
         if t == 5:
-            tt(T.lg[:], T.st[:].indirect(JU), T.col[:], A.mult, ["st", "ju", "col"], ["lg"], 256, GA)
+            tt(T.lg[:], T.st[:].indirect(JU), T.col[:], A.mult, ["st", "ju", "col"], ["lg0", "lg1"], 256, GA)
         mm(PS[4][:, 0:256], IB, T.col[:], True, False, ["ib", "col"], ["ps4"], 256)
-        mm(PS[4][:, 0:256], BM, T.lg[:], False, True, ["bm", "lg"], ["ps4"], 256)
-        later.append(lambda w: ac(T.ncl[:], PS[4][:, 0:256], ["ps4"], ["ncl"] + list(w)))
+        mm(PS[4][:, 0:256], BM, T.lg[:], False, True, ["bm", "lg0", "lg1"], ["ps4"], 256)
+        if t == 5 or LATER[1] is None:
+            ac(T.ncl[:], PS[4][:, 0:256], ["ps4"], ["ncl"])
+        else:
+            later.append((LATER[1], lambda w: ac(T.ncl[:], PS[4][:, 0:256], ["ps4"], ["ncl"] + w)))
 
     def row_mask(t):
         ac(T.lm[:, 256 * (t % 2):256 * (t % 2) + 256], T.lt[:].indirect(JU), ["lt", "ju"], ["lm%d" % (t % 2)], k=GA)
 
     def statics(t):
         pj = PS[7][:, 0:16]
-        ac(B["jj"], pj, ["ps7"], ["jj"], 16, bias=0.0, f=AF.Relu)
+        ac(B["jj"], pj, ["ps7"], ["jj"], 16, bias=16.0, f=AF.Relu)
         if t >= 2:
-            ac(B["nc"], pj, ["ps7"], ["nc"], 16, bias=2.0, f=AF.Relu, scale=-1.0)
+            ac(B["nc"], pj, ["ps7"], ["nc"], 16, bias=4096.0, f=AF.Relu, scale=-256.0)
         if t >= 5:
-            ac(B["e5"], pj, ["ps7"], ["e5"], 16, bias=-4.0, f=AF.Relu)
+            ac(B["e5"], pj, ["ps7"], ["e5"], 16, bias=-12288.0, f=AF.Relu, scale=256.0)
         if t < NSUB - 1:
             row_mask(t)
 
-    def request(e):
+    def request(e, part):
         rq = T["req%d" % e]
         own = rq[:, 112:128]
-        ts(SI["fi"], T.fz[:], -1.0, A.add, r=["fz"], w=["fi"])
-        ts(SI["q"], SI["fi"], 7, A.bitwise_and, r=["fi"], w=["q"])
-        for h_ in range(2):
-            ts(T.qo[:, 16 * h_:16 * h_ + 16], SI["q"], 2.0, A.mult, float(h_), A.add, r=["q"], w=["qo%d" % h_])
-            tt(T.uu[:, 256 * h_:256 * h_ + 256], T.hwa[:].indirect(T.qo[:, 16 * h_:16 * h_ + 16]), T.xc[:], A.mult, ["hwa", "hwown", "qo%d" % h_] + staged("xc"), ["uu%d" % h_], 256, GA)
+        if part == 0:
+            ts(SI["fi"], T.fz[:], -1.0, A.add, r=["fz"], w=["fi"])
+            ts(SI["q"], SI["fi"], 7, A.bitwise_and, r=["fi"], w=["q"])
+        if part < 2:
+            qo = T.qo[:, 16 * part:16 * part + 16]
+            ts(qo, SI["q"], 2.0, A.mult, float(part), A.add, r=["q"], w=["qo%d" % part])
+            tt(T.uu[:, 256 * part:256 * part + 256], T.hwa[:].indirect(qo), T.xc[:], A.mult, ["hwa", "hwown", "qo%d" % part] + staged("xc", 0, 16, MOVES), ["uu%d" % part], 256, GA)
+            return
         to_l(3, PS[3][:, 0:32], Z1, T.uu, True, ["z1", "uu0", "uu1"])
         cp(S["ub"], PS[3][:, 16:32], ["ps3"], ["ub"])
         tt(SI["pr"], PS[3][:, 0:16], S["ub"], A.mult, ["ps3", "ub"], ["pr"])
@@ -552,7 +594,7 @@ def rank_program(g, core, T, topo):
 
     def codes():
         for k, (a, b) in enumerate(CODES):
-            cp(T.cod[:, 16 * a:16 * b], T.sfs[:].indirect(T.du[:, a:b]), ["sfs", "du"], ["cod%d" % k], 16 * (b - a), GA)
+            cp(T.cod[:, 16 * a:16 * b], T.sfs[:].indirect(T.du[:, a:b]), ["sfs", "du%d" % k], ["cod%d" % k], 16 * (b - a), GA)
 
     def coded(a, b):
         return ["cod%d" % j for j, (c0, c1) in enumerate(CODES) if c0 < b and a < c1]
@@ -562,105 +604,122 @@ def rank_program(g, core, T, topo):
         mm(PS[bank][:, 0:32 * (hi - lo)], IB, T.kin[:, 2 * lo:2 * hi, :], True, False, ["ib", "kin0", "kin1"], k, max(64, 32 * (hi - lo)))
         for eng, a, b in GATHERS:
             if lo <= a < hi:
+                for x in [x for x in later if x[0] == a]:
+                    later.remove(x)
+                    x[1](["chact"])
                 o, src = T.gg[:, 256 * a:256 * b], T.pw2[:].indirect(T.cod[:, 16 * a:16 * b])
                 (ac if eng == "act" else cp)(o, src, PW2 + coded(a, b), ["gg%d" % c for c in range(a, b)] + ["ch" + eng], 256 * (b - a), GA)
-                if eng == "act" and later and a <= LATER:
-                    later.pop(0)(["chact"])
                 for c in range(a, b):
                     calls = []
                     for r2 in range(8):
                         p_, q, u = 16 * c + 2 * r2, r2 // 2, r2 % 2
                         s0, c0 = 8 * (2 * p_ + 1 - u), 32 * (c - lo)
                         calls.append((PS[bank][32 * q:32 * q + 32, c0:c0 + 32], T.xd[:, s0:s0 + 32], T.gg[:, 16 * p_:16 * p_ + 32], False, False))
-                    mms(calls, ["xd%d_%d" % (j, lo) for j in range(8)] + ["gg%d" % c], k, 32)
+                    mms(calls, [x for j in range(8) for x in staged("xd%d" % j, c, c + 1, MOVES)] + ["gg%d" % c], k, 32)
         mm(PS[bank][:, 0:8], IB, T.xd[:, 0:8], False, True, ["ib", "xdz"], k)
 
-    def stage(t, lo, hi, per, bank, eng):
-        last, n, cs, k, me = t == NSUB - 1, 32 * (hi - lo), slice(32 * lo, 32 * hi), "ps%d" % bank, "_%d" % lo
-        ins, ik = T.inh[:, 11 * lo + t + 1:11 * hi:11], "in%d" % (t + 1) + me
+    def test(t, lo, hi, bank, eng):
+        n, cs, k, me = 32 * (hi - lo), slice(32 * lo, 32 * hi), "ps%d" % bank, "_%d" % lo
         keys(lo, hi, bank)
         if eng == "act":
             ac(T.ind[:, cs], PS[bank][:, 0:n], [k], ["ind" + me], n, bias=0.5, f=AF.Sign)
         else:
             ts(T.ind[:, cs], PS[bank][:, 0:n], -0.5, A.is_ge, -0.5, A.add, r=[k], w=["ind" + me], n=n)
         scan(T.tot[:, cs], T.kq[:, 0:n], T.ind[:, cs], A.mult, A.add, ["kq", "ind" + me], ["tot" + me], n, CY / 2)
-        o = PS[3][:, lo:hi]
-        mm(o, M4K, T.sb[:, BK["t17"], lo:hi], True, False, ["m4k", "t17"], ["ps3"])
-        if t >= 5:
-            mm(o, M4K, T.sb[:, BK["e5"], lo:hi], False, False, ["m4k", "e5"], ["ps3"])
-        mm(o, PM, T.tot[:, 32 * lo + 31:32 * hi:32], False, True, ["pm", "tot" + me], ["ps3"])
-        ts(ins, o, 0.0, A.is_ge, r=["ps3"], w=[ik])
-        if not last:
+        if t < NSUB - 1:
             scan(T.mns[:, cs], T.bq[:, 0:n], PS[bank][:, 0:n], A.add, A.min, ["bq", k], ["mns" + me], n)
+
+    def moved(t, lo, hi):
         k7, o, all_, ak = ["ps7"], PS[7][:, 16 + lo:16 + hi], T.inh[:, t + 1:176:11], staged("in%d" % (t + 1))
         mm(o, IB, T.sb[:, BK["pb"], lo:hi], True, False, ["ib", "pb"], k7)
         if t:
-            mms([(o, I256, T.inh[:, 11 * lo + n_:11 * hi:11], False, False) for n_ in range(1, t + 1)], ["i256"] + ["in%d" % n_ + me for n_ in range(1, t + 1)], k7)
+            mms([(o, IB, T.inh[:, 11 * lo + n_:11 * hi:11], False, False) for n_ in range(1, t + 1)],
+                ["ib"] + [x for n_ in range(1, t + 1) for x in staged("in%d" % n_, lo, hi)], k7)
         if lo == 0:
             mm(PS[7][:, 0:16], IB, B["jj"], False, False, ["ib", "jj"], k7)
-            mm(PS[7][:, 0:16], IB, ONE, False, False, ["ib", "one"], k7)
-            if t >= 5:
-                mm(PS[7][:, 0:16], NI, B["e5"], False, False, ["ni", "e5"], k7)
-            mm(PS[7][:, 32:48], IF, S["df"], False, False, ["if", "df"], k7, 256)
-            mm(PS[7][:, 32:48], M4K, ONE, False, False, ["m4k", "one"], k7)
-            mm(PS[7][:, 32:48], I4K, all_, False, False, ["i4k"] + ak, k7)
-            mm(PS[7][:, 0:16], IM8, all_, False, False, ["im8"] + ak, k7)
-        mm(o, I256, ins, False, True, ["i256", ik], k7)
+            mm(PS[7][:, 32:48], IF, S["df"], False, False, ["if", "df0", "df1"], k7, 256)
+            mm(PS[7][:, 32:48], IB, all_, False, False, ["ib"] + ak, k7)
+            mm(PS[7][:, 0:16], NI, all_, False, False, ["ni"] + ak, k7)
+        mm(o, IB, T.inh[:, 11 * lo + t + 1:11 * hi:11], False, True, ["ib"] + staged("in%d" % (t + 1), lo, hi), k7)
         first = 16 + lo if lo else 0
-        cp(T.nj[:, first:16 + hi], PS[7][:, first:16 + hi], k7, ["nu" + me] + ([] if lo else ["ju"]))
-        if last:
+        ts(T.nj[:, first:16 + hi], PS[7][:, first:16 + hi], 1.0 / 16, A.mult, 1.0, A.add, r=k7, w=["nu_%d" % lo] + ([] if lo else ["ju"]))
+        if t == NSUB - 1:
             place(T.yxs, t + 1, lo, hi, "yxs")
         else:
             place(T.xc, t + 1, lo, hi, "xc")
-            expand("xc", "xc" + me, NPOOL[int(lo == 0)], lo, hi)
+            expand("xc", "xc_%d" % lo, NPOOL[int(lo == 0)], lo, hi)
+
+    def stage(t, lo, hi, per):
+        last, all_, ak = t == NSUB - 1, T.inh[:, t + 1:176:11], staged("in%d" % (t + 1))
+        ins, ik, tk = T.inh[:, 11 * lo + t + 1:11 * hi:11], "in%d_%d" % (t + 1, lo), staged("tot", lo, hi, BANKS)
+        for b in BANKS:
+            if lo <= b[0] < hi:
+                test(t, *b)
+        o = PS[3][:, lo:hi]
+        mm(o, NI, T.sb[:, BK["t17"], lo:hi], True, False, ["ni", "t17"], ["ps3"])
+        if t >= 5:
+            mm(o, NI, T.sb[:, BK["e5"], lo:hi], False, False, ["ni", "e5"], ["ps3"])
+        mm(o, PM, T.tot[:, 32 * lo + 31:32 * hi:32], False, True, ["pm"] + tk, ["ps3"])
+        ts(ins, o, 0.0, A.is_ge, 4096.0, A.mult, r=["ps3"], w=[ik])
+        for a, b in MOVES:
+            if a == lo:
+                moved(t, a, b)
         if lo == 0 and not last:
-            MNS, o = staged("mns"), PS[4][:, 0:16]
+            MNS, o = staged("mns", 0, 16, BANKS), PS[4][:, 0:16]
             ts(T.mv[:], T.mns[:, 15:512:16], ROUND, A.add, -ROUND, A.add, r=MNS, w=["mv"])
-            mm(o, I16, B["jj"], True, False, ["i16", "jj"], ["ps4"])
-            for h_ in range(2):
+            mm(o, IB, B["jj"], True, False, ["ib", "jj"], ["ps4"])
+            if FRAC:
+                tt(T.mw[:], T.mv[:], T.mns[:, 15:512:16], A.subtract, MNS + ["mv"], ["mw"], 64)
+            for h_ in range(2 * (1 - FRAC)):
                 mm(o, PF[h_], T.mns[:, 15 + 16 * h_:512:32], False, False, ["pf%d" % h_] + MNS, ["ps4"], 256)
             for h_ in range(2):
-                mm(o, PH[h_], T.mv[:, h_:32:2], False, h_ == 1, ["ph%d" % h_, "mv"], ["ps4"])
+                mm(o, PH[h_], (T.mw if FRAC else T.mv)[:, h_:32:2], False, h_ == 1, ["ph%d" % h_, "mw" if FRAC else "mv"], ["ps4"])
             ts(T.iu[:], o, 7.5, A.add, r=["ps4"], w=["iu"])
-            ts(T.sr[:], T.cod[:], 0.5, A.mult, 0.75, A.add, r=coded(0, 16), w=["sr"], n=256)
-            tt(T.sg[:], T.w1[:].indirect(T.iu[:]), T.sr[:], A.mult, ["w1", "iu", "sr"], ["sg"], 256, GA)
+            if t < SRT:
+                ts(T.sr[:], T.cod[:], 0.5, A.mult, -0.25, A.add, r=coded(0, 16), w=["sr"], n=256)
+                tt(T.sg[:], T.w1[:].indirect(T.iu[:]), T.sr[:], A.mult, ["w1", "w1z", "iu", "sr"], ["sg%d" % a for a, b in SGS], 256, GA)
+            else:
+                ac(T.sh[:], T.w1[:].indirect(T.iu[:]), ["w1", "w1z", "iu"], ["sh"], k=GA, scale=HALF)
+                for a, b in SGS:
+                    tt(T.sg[:, 16 * a:16 * b], T.sfs[:].indirect(T.du[:, a:b]), T.sh[:, 16 * a:16 * b], A.mult, ["sfs", "du0", "du1", "sh"], ["sg%d" % a], 16 * (b - a), GA)
             o = PS[6][:, 0:16]
             if t > 0:
                 mm(o, IH, T.fr[:], True, False, ["ih", "fr"], ["ps6"])
-            mm(o, M4K, all_, t == 0, False, ["m4k"] + ak, ["ps6"])
-            to_l(6, o, ZH, T.sg, False, ["zh", "sg"])
-            cp(T.fz[:], o, ["ps6"], ["fz"])
+            mm(o, NI, all_, t == 0, False, ["ni"] + ak, ["ps6"])
+            to_l(6, o, ZH, T.sg, False, ["zh"] + ["sg%d" % a for a, b in SGS])
+            ts(T.fz[:], o, 0.75, A.add, r=["ps6"], w=["fz"])
         if t >= 2:
-            lowest(ins, [ik], lo, hi, per)
+            lowest(tk, ins, [ik], lo, hi, per)
             scatters(T.tab, T.ncl, lambda c: ["ncl"], TAB, lo, hi, per)
 
-    for s in STAGES:
+    for s in MOVES:
         expand("xt", "x0", 4, s[0], s[1])
     row_mask(0)
     codes()
-    for n in range(1, 6):
-        next_x(n, 6)
+    next_x(1, 6)
     for t in range(NSUB):
         last, ex, e = t == NSUB - 1, t % 5 == 4, t // 5
         step.clear()
-        step["on"] = 1
-        if ex:
-            request(e)
+        step["t"] = t
+        for part in range(3):
+            if ASKS[part] == t % 5:
+                request(e, part)
         if t >= 2:
             swapped(t)
         k7 = ["ps7"]
         for s in STAGES:
             stage(t, *s)
         idd, idk = T.idh[:, t + 1:176:11], "id_%d" % (t + 1)
-        ac(idd, PS[7][:, 32:48], k7, [idk], 16, bias=0.0, f=AF.Relu)
+        ac(idd, PS[7][:, 32:48], k7, [idk], 16, bias=-4096.0, f=AF.Relu)
         if ex:
-            ac(B["jj"], PS[7][:, 0:16], k7, ["jj"], 16, bias=0.0, f=AF.Relu)
+            rivals(None)
+            ac(B["jj"], PS[7][:, 0:16], k7, ["jj"], 16, bias=16.0, f=AF.Relu)
         else:
             statics(t + 1)
         if last:
-            dma("sync", T.yx[:], T.yxs[:], "o_yx", staged("yxs"), ["yx"], 2500)
+            dma("sync", T.yx[:], T.yxs[:], "o_yx", staged("yxs", 0, 16, MOVES), ["yx"], 2500)
         else:
-            cp(T.fr[:], T.fz[:], ["fz"], ["fr"])
+            ts(T.fr[:], T.fz[:], -1.0, A.add, 0.0, A.max, r=["fz"], w=["fr"])
         if ex:
             xb, rq = T["xb%d" % e], T["req%d" % e]
             rk = TAB + ["rqarr%d" % e, "rqown%d" % e]
@@ -683,14 +742,19 @@ def rank_program(g, core, T, topo):
             ac(xb[:, 16 * rank:16 * rank + 16], PS[1][:, 48:64], ["ps1"], ["ownxb%d" % e], 16)
             lastw["anarr%d" % e] = ("an%d" % e, ans_in, sends, ANSWER)
         if not last:
-            lmt = T.lm[:, 256 * (t % 2):256 * (t % 2) + 256]
-            tt(T.lg[:], T.tab[:].indirect(T.fz[:]), lmt, A.mult, TAB + ["fz", "lm%d" % (t % 2)], ["lg"], 256, GA)
-            mm(PS[3][:, 0:16], IF, idd, True, False, ["if", idk], ["ps3"], 256)
-            to_l(3, PS[3][:, 0:16], ZL, T.lg, False, ["zl", "lg"])
+            next_x(t + 2, XB)
+            for k, (a, b) in enumerate(CODES if LGS and not ex else ((0, 16),)):
+                bank, lk = (3, 4)[k], ["lg%d" % k] if LGS and not ex else ["lg0", "lg1"]
+                o, c2 = PS[bank][:, a:b], slice(16 * a, 16 * b)
+                tt(T.lg[:, c2], T.tab[:].indirect(T.fz[:, a:b]), T.lm[:, 256 * (t % 2) + 16 * a:256 * (t % 2) + 16 * b], A.mult,
+                   TAB + ["fz", "lm%d" % (t % 2)], lk, 16 * (b - a), GA)
+                mm(o, IF, T.idh[:, 11 * a + t + 1:11 * b:11], True, False, ["if", idk], ["ps%d" % bank], 256)
+                to_l(bank, o, ZL, T.lg, False, ["zl"] + lk, 16 * a, 16 * b)
+                if not ex:
+                    cp(T.du[:, a:b], o, ["ps%d" % bank], ["du%d" % k] if LGS else ["du0", "du1"])
+                    ac(T.sm[:, 0, a:b], o, ["ps%d" % bank], ["df%d" % k] if LGS else ["df0", "df1"], 16)
         if not ex:
-            cp(T.du[:], PS[3][:, 0:16], ["ps3"], ["du"])
             codes()
-            ac(S["df"], PS[3][:, 0:16], ["ps3"], ["df"], 16)
             if t >= 1:
                 columns()
                 rivals(t + 1)
@@ -698,36 +762,34 @@ def rank_program(g, core, T, topo):
         if not last:
             ac(xb[:, 128:144], PS[3][:, 0:16], ["ps3"], ["dfxb0"], 16)
             columns()
-        rivals(None)
-        ts(S["nw"], B["jj"], 5.0, A.is_lt, 16.0, A.mult, r=["jj"], w=["nw"])
+        ts(S["nw"], B["jj"], 80.0, A.is_lt, 16.0, A.mult, r=["jj"], w=["nw"])
         tt(S["t1"], S["nw"], SI["q"], A.add, ["nw", "q"], ["t1s"])
         cp(T.wu[:], S["t1"], ["t1s"], ["wu"])
-        ac(T.oh[:], T.w1[:].indirect(T.wu[:]), ["w1", "wu"], ["oh"], k=GA)
+        ac(T.oh[:], T.w1[:].indirect(T.wu[:]), ["w1", "w1z", "wu"], ["oh"], k=GA)
         scan(T.cum[:], T.one[:], T.oh[:], A.mult, A.add, ["one", "oh"], ["cum"], 256, CY / 2)
         ts(T.le[:], T.cum[:], 16.0, A.is_le, r=["cum"], w=["le"], n=128)
         tt(T.svr[:], T.le[:], T.oh[:], A.mult, ["le", "oh"], ["svr"], 256)
         mm(PS[6][:, 0:16], IB, B["cb"], True, False, ["ib", "cb"], ["ps6"])
         to_l(6, PS[6][:, 0:16], ZQ, T.svr, False, ["zq", "svr"])
-        ts(B["sv"], PS[6][:, 0:16], 128.0, A.is_lt, r=["ps6"], w=["sv"])
+        ts(B["sv"], PS[6][:, 0:16], 128.0, A.is_lt, 4096.0, A.mult, r=["ps6"], w=["sv"])
         cp(T.pu[:], PS[6][:, 0:16], ["ps6"], ["pu"])
         mm(PS[3][:, 0:16], PMT, B["sv"], True, True, ["pmt", "sv"], ["ps3"])
-        ts(T.tot[:, 31:512:32], PS[3][:, 0:16], -0.5, A.add, r=["ps3"], w=staged("tot"))
-        lowest(B["sv"], ["sv"])
+        ac(T.tot[:, 31:512:32], PS[3][:, 0:16], ["ps3"], staged("tot", 0, 16, BANKS), 16, bias=-0.5, scale=1.0 / 4096)
+        lowest(staged("tot", 0, 16, BANKS), B["sv"], ["sv"])
         if not last:
             mm(PS[7][:, 0:16], IB, B["jj"], True, False, ["ib", "jj"], k7)
-            mm(PS[7][:, 0:16], NI, B["sv"], False, True, ["ni", "sv"], k7)
-            cp(JU, PS[7][:, 0:16], k7, ["ju"])
+            ac(B["th"], B["sv"], ["sv"], ["th"], 16, bias=16.0, scale=1.0 / 256)
+            mm(PS[7][:, 0:16], NI, B["th"], False, True, ["ni", "th"], k7)
+            ts(JU, PS[7][:, 0:16], 1.0 / 16, A.mult, 1.0, A.add, r=k7, w=["ju"])
             statics(t + 1)
-            for n in range(6, 11):
-                next_x(n, 6)
         tt(T.ag[:], xb[:, 0:144].indirect(T.pu[:]), T.dia[:], A.mult,
            ["anarr%d" % e, "ownxb%d" % e, "dfxb%d" % e, "pu", "dia"], ["ag"], 256, GA)
         if not last:
             scan(T.asc[:], T.kp[:], T.ag[:], A.mult, A.add, ["kp", "ag"], ["asc"])
             an = T.asc[:, 15:256:16]
-            cp(T.du[:], an, ["asc"], ["du"])
+            cp(T.du[:], an, ["asc"], ["du0", "du1"])
             codes()
-            ac(S["df"], an, ["asc"], ["df"], 16)
+            ac(S["df"], an, ["asc"], ["df0", "df1"], 16)
             ac(T.dg[:, 0:256], T.ag[:], ["ag"], ["dg0"])
             tt(T.dg[:, 256:512], T.ag[:], T.dg[:, 0:256], A.subtract, ["ag", "dg0"], ["dg1"], 512)
             mm(PS[4][:, 0:256], IKP, T.col[:], True, False, ["ikp", "col"], ["ps4"], 256)
@@ -738,7 +800,7 @@ def rank_program(g, core, T, topo):
             columns()
             rivals(t + 1)
             continue
-        ts(T.nih[:], T.inh[:], -1.0, A.mult, 1.0, A.add, r=["in_0"] + [x for k in range(1, 11) for x in staged("in%d" % k)], w=["nih"], n=176)
+        ac(T.nih[:], T.inh[:], ["in_0"] + [x for k in range(1, 11) for x in staged("in%d" % k)], ["nih"], 176, bias=1.0, scale=-1.0 / 4096)
         scan(T.csc[:], T.nih[:], T.idh[:], A.mult, A.add, ["nih"] + ["id_%d" % k for k in range(11)], ["csc"], 176)
         cp(S["yc"], T.csc[:, 10:176:11], ["csc"], ["ycs"])
         dma("sync", T.yc[:], S["yc"], "o_yc", ["ycs"], ["yc"], 2500)

@@ -4,24 +4,41 @@ from concourse.mybir import AluOpType as A, ActivationFunctionType as AF
 
 F32, B16, I32, U16, F16 = "float32", "bfloat16", "int32", "uint16", "float16"
 N, NSUB, TW = 8, 10, 2096
-BANKS = ((4, 16, 0, "act"), (0, 4, 1, "dve"))
-STAGES = ((0, 16, 2),)
+BANKS = ((4, 16, 0, "dve"), (0, 4, 1, "act"))
+STAGES = ((4, 16, 2), (0, 4, 2))
 MOVES = ((0, 16),)
-FRAC, SRT, HALF, LGS = 0, 2, 0.49995, 0
-GATHERS = (("act", 14, 16), ("dve", 12, 14), ("act", 10, 12), ("dve", 8, 10), ("act", 6, 8), ("dve", 4, 6), ("act", 2, 4), ("dve", 0, 2))
+XDS = ((0, 16),)
+FRAC, SRT, HALF, LGS = 0, 10, 0.49995, 0
+GATHERS = (("act", 14, 16), ("dve", 12, 14), ("act", 10, 12), ("dve", 8, 10), ("dve", 5, 6), ("act", 6, 8), ("dve", 4, 5), ("act", 2, 4),
+           ("dve", 1, 2), ("act", 0, 1))
+EVEN = (("act", 14, 16), ("dve", 12, 14), ("act", 10, 12), ("dve", 8, 10), ("act", 6, 8), ("dve", 4, 6), ("act", 2, 4), ("dve", 0, 2))
 LATER = (None, None)
 SPANS = []
-ASKS, XB = (2, 3, 3), 0
-SGS = ((0, 16),)
-QUEUES, FREE = {}, {}
+ALIKE = (2, 3, 6, 7, 8)
+SWAP = (0, 1)
+OTHER = {0: EVEN, 1: EVEN,
+         5: (("act", 14, 16), ("act", 12, 14), ("dve", 10, 12), ("act", 8, 10), ("act", 6, 8), ("dve", 4, 6), ("act", 2, 4), ("act", 0, 2))}
+ASKS, XB = (1, 2, 3, 3), 1
+SGS = ((0, 8), (8, 16))
+QUEUES = {"dve": "-cod1 -cod2 gg1 gg2 gg3 gg4 gg5 ind1 tot1 ee1 ee2 in1 mns1 sr1 tot2 mns2 ee3 mv1 ou1 ou2 in2 tab1 ee4 tab2 iu1 nu1 tab3 sg1 tab4 sg2 "
+                 "tab5 ou3 ou4 tab6 tab7 fz1 tab8 lg1 +uu1 du1",
+          "act": "-xd1 -xd2 -xd3 -xd4 -x1 gg1 gg2 gg3 -thr1 gg4 gg5 ind1 ncl1 xc1",
+          "pe": "ps16 ps22 ps24 ps44 ps45 ps46 ps47 ps26 ps28"}
+LOOSE = {t: {"dve": "-cod1 -cod2 gg1 gg2 gg3 gg4 gg5 ind1 tot1 ee1 ee2 in1 tot2 ee3 ou1 ou2 in2 tab1 ee4 tab2",
+             "act": "gg1 gg2 gg3 -thr1 gg4 gg5 ind1 ncl1", "pe": "ps16 ps22 ps24"} for t in (4, 9)}
+LOOSE[5] = {"dve": "-ag1 -asc1 -du1 -cod1 -cod2 gg1 -tab9 -tab10 -tab11 -tab12 gg2 -tab13 -tab14 -tab15 -tab16 ind1 tot1 lg1 ee1 ee2",
+            "act": "-dg1 -ncl2 gg1 gg2 gg3 gg4 gg5 -col2 gg6 -thr2 ind1 ncl1"}
+SEED = 2
 SHIFT, SLACK = 600, 200
 CODES = ((12, 16), (0, 12))
-NPOOL = (5, 5)
+NPOOL = (4, 4)
 ROUND = 12582912.0
-GA, SC, CY, PE = 1.33, 3.2, 0.85, 0.47
+GA, SC, CY, PE = 1.42, 3.5, 0.88, 0.47
 RULE, SAME, CROSS, FIX = 0.5, 160, 170, 50
-PASSES, ORDER = (((6, 7, 8), 5000), ((-1, 0, 1, 2), 3000), ((3, 4, 5, 6), 3000), ((8, 9), 2000), (range(-1, 10), 2000)), {}
-LOADS, ASK, ANSWER = (2200, 3600, 7500, 8200), 4000, 3500
+ALL = range(-1, NSUB)
+PASSES = (((6, 7, 8), 2500), (ALL, 1), (ALL, 1), (ALL, 1), ((-1, 0, 1, 2), 5000), ((3, 4, 5, 6), 5000), ((8, 9), 3000), (ALL, 1), (ALL, 1), (ALL, 2000))
+ORDER = {}
+LOADS, ASK, ANSWER = (2200, 3600, 7500, 8200), 4000, 3000
 
 
 def _s(shape, d):
@@ -44,16 +61,16 @@ SCRATCH = {
     "le": _s([128, 256], B16), "svr": _s([128, 256], B16), "asc": _s([128, 256], F32),
     "req0": _s([128, 128], U16), "req1": _s([128, 128], U16), "xb0": _s([128, 256], F32), "xb1": _s([128, 256], F32),
     "inh": _s([128, 176], B16), "idh": _s([128, 176], F32), "nih": _s([128, 176], F32), "csc": _s([128, 176], F32),
-    "sm": _s([128, 8, 16], F32), "sb": _s([128, 8, 16], B16), "si": _s([128, 4, 16], I32), "mv": _s([128, 32], F16), "mw": _s([128, 32], F16),
-    "fs": _s([128, 24], F16), "fr": _s([128, 16], F16),
-    "du": _s([128, 16], U16), "fz": _s([128, 16], U16), "iu": _s([128, 16], U16), "nj": _s([128, 32], U16),
+    "sm": _s([128, 8, 16], F32), "sb": _s([128, 9, 16], B16), "w3": _s([128, 128], B16), "si": _s([128, 4, 16], I32), "mv": _s([128, 32], F16), "mw": _s([128, 32], F16),
+    "fs": _s([128, 24], F16), "fr": _s([128, 16], F32),
+    "du": _s([128, 16], U16), "fz": _s([128, 16], U16), "iu": _s([128, 16], U16), "nj": _s([128, 48], U16),
     "ou": _s([128, 48], U16), "qo": _s([128, 32], U16), "wu": _s([128, 16], U16), "eo": _s([128, 24], U16),
     "pu": _s([128, 16], U16), "bc": _s([128, 16], U16),
     "pi": _s([128, 8], I32), "ci": _s([128, 12], I32), "cf": _s([128, 48], F32), "ro": _s([128, 144], F32),
     "rx": _s([128, 4, 128], F32), "ii": _s([128, 256], B16), "kp": _s([128, 256], B16), "j32": _s([128, 384], B16),
     "kq": _s([128, 384], B16), "bq": _s([128, 384], B16),
     "one": _s([128, 256], B16), "tri": _s([128, 384], B16), "dia": _s([128, 256], B16), "fh": _s([128, 512], B16),
-    "fl": _s([128, 512], B16), "zz": _s([128, 6, 144], B16), "zh": _s([128, 144], F16), "mb": _s([128, 24, 128], B16),
+    "fl": _s([128, 512], B16), "zz": _s([128, 6, 144], B16), "zh": _s([128, 144], F16), "zf": _s([128, 144], F32), "mb": _s([128, 24, 128], B16),
     "mf": _s([128, 4, 128], F32), "mh": _s([128, 4, 128], F16), "hq": _s([128, 7, 144], B16), "w1": _s([128, 176], B16), "lt": _s([128, 16], B16),
     "st": _s([128, 16], B16), "r3": _s([128, 16], F32),
 }
@@ -111,7 +128,8 @@ def schedule(ops):
     at = {(o["step"], o["eng"], o["kind"][0][1] + str(o["kind"][1])): i for i, o in enumerate(ops)}
     for eng, names in QUEUES.items():
         for t in range(NSUB):
-            row = [at.get((t - x.startswith("-"), eng, x.strip("-"))) for x in names.split() if x.strip("-") not in FREE.get(t, "").split()]
+            names_ = names if t in ALIKE else LOOSE.get(t, {}).get(eng, "")
+            row = [at.get((t - x.startswith("-") + x.startswith("+"), eng, x.strip("-+"))) for x in names_.split()]
             row = [i for i in row if i is not None]
             for a, b in zip(row, row[1:]):
                 succ[a].append((b, 0))
@@ -134,7 +152,15 @@ def schedule(ops):
     for steps, passes in PASSES:
         part = [i for i in order if ops[i]["step"] in steps]
         new = {i: k for k, i in enumerate(part)}
-        end = settle([ops[i] for i in part], [[(new[j], l) for j, l in succ[i] if j in new] for i in part], [prio[i] for i in part], shift, passes)
+        after = [[(new[j], l) for j, l in succ[i] if j in new] for i in part]
+        end = settle([ops[i] for i in part], after, [prio[i] for i in part], shift, passes)
+        if len(part) == n and passes == 1:
+            before = [[] for _ in part]
+            for a in range(n):
+                for b, l in after[a]:
+                    before[b].append((a, l))
+            back = deal([ops[i]["cost"] for i in part], [ops[i]["eng"] for i in part], before, end, [ops[i]["lat"] for i in part])
+            prio, shift = [back[new[i]] for i in range(n)], {o["kind"]: 0.0 for o in ops if o["kind"][2] is None}
     return sorted(range(n), key=lambda i: (end[new[i]] - ops[i]["cost"], new[i]))
 
 
@@ -143,11 +169,11 @@ def settle(ops, succ, prio, shift, passes):
     for i, o in enumerate(ops):
         kinds.setdefault(o["kind"], []).append(i)
     pick = [k for k, v in kinds.items() if k not in shift] or list(kinds)
-    shift.update({k: 0.0 for k in kinds if k not in shift})
+    shift.update({k: shift.get(k[:2] + (None,), 0.0) for k in kinds if k not in shift})
     cost, tail, eng = [o["cost"] for o in ops], [o["lat"] for o in ops], [o["eng"] for o in ops]
     back = [(i, [j for j, l in succ[i]]) for i in range(n - 1, -1, -1) if succ[i]]
     now = [p + shift.get(o["kind"], 0.0) for p, o in zip(prio, ops)]
-    best, span, rng = None, 1e30, np.random.default_rng(0)
+    best, span, rng = None, 1e30, np.random.default_rng(SEED)
     for k in range(passes):
         kind, d, p = pick[int(rng.integers(len(pick)))], float(rng.normal()) * SHIFT * (k > 0), list(now)
         for i in kinds[kind]:
@@ -170,9 +196,9 @@ def settle(ops, succ, prio, shift, passes):
     return best[1]
 
 
-def deal(cost, eng, succ, prio):
+def deal(cost, eng, succ, prio, ready=None):
     n = len(cost)
-    busy, end, ready = {e: [] for e in eng}, [0.0] * n, [0.0] * n
+    busy, end, ready = {e: [] for e in eng}, [0.0] * n, ready or [0.0] * n
     for i in sorted(range(n), key=lambda i: -prio[i]):
         l, st, c = busy[eng[i]], ready[i], cost[i]
         a = len(l)
@@ -216,7 +242,7 @@ def rank_program(g, core, T, topo):
         name = (w or r)[0]
         kind = (eng, name if name.startswith("ps") or "t" not in step else "".join(x for x in name.split("_")[0] if x > "9"), "t" in step)
         step[kind] = step.get(kind, 0) + 1
-        ops.append({"kind": (kind, step[kind]), "step": step.get("t", -1), "eng": eng, "fn": fn, "deps": deps, "ord": order, "dma": dma, "sig": False, "cost": cost, "lat": lat})
+        ops.append({"kind": (kind, step[kind], None if step.get("t") in ALIKE else step.get("t", -1)), "step": step.get("t", -1), "eng": eng, "fn": fn, "deps": deps, "ord": order, "dma": dma, "sig": False, "cost": cost, "lat": lat})
         me_ = len(ops) - 1
         for k in r:
             readers.setdefault(k, []).append(me_)
@@ -245,8 +271,8 @@ def rank_program(g, core, T, topo):
     def ms(out, c, w, n=16):
         op("dve", lambda: v.memset(out, c), (), w, vc(n, CY / 2))
 
-    def scan(out, d0, d1, o0, o1, r, w, n=256, k=CY):
-        op("dve", lambda: v.tensor_tensor_scan(out, d0, d1, 0.0, o0, o1), r, w, vc(n, k))
+    def scan(out, d0, d1, o0, o1, r, w, n=256, k=CY, first=0.0):
+        op("dve", lambda: v.tensor_tensor_scan(out, d0, d1, first, o0, o1), r, w, vc(n, k))
 
     def ac(out, a, r, w, n=256, k=CY, bias=None, f=AF.Identity, scale=1.0):
         if bias is None:
@@ -352,12 +378,13 @@ def rank_program(g, core, T, topo):
         colf(n_)
     cp(T.cf[:, 0:11], T.ci[:, 0:11], ["ci%d" % k for k in range(11)], ["cf"])
     S = {n_: T.sm[:, k] for k, n_ in enumerate(("df", "ub", "nw", "yc", "t1"))}
-    BK = {n_: k for k, n_ in enumerate(("jj", "nc", "e5", "t17", "pb", "sv", "th", "cb"))}
+    BK = {n_: k for k, n_ in enumerate(("jj", "nc", "e5", "t17", "pb", "sv", "th", "cb", "qb"))}
     B = {n_: T.sb[:, k] for n_, k in BK.items()}
     SI = {n_: T.si[:, k] for k, n_ in enumerate(("fi", "q", "pr", "h"))}
     IB, BM, BOF, IKP, SELY = T.mb[:, 0], T.mb[:, 7], T.mb[:, 8], T.mb[:, 9], T.mb[:, 10, 0:32]
     NI, PM, PMT, DH = T.mb[:, 6], T.mb[:, 14], T.mb[:, 15], (T.mb[:, 16], T.mb[:, 17])
-    IF, ZF, PF, PH, NPT, IH = T.mf[:, 0], T.mf[:, 1], (T.mf[:, 2], T.mf[:, 3]), (T.mh[:, 0], T.mh[:, 1]), T.mh[:, 2], T.mh[:, 3]
+    ZD = T.mb[:, 18]
+    IF, ZF, PF, PH, NPT, IH = T.mf[:, 0], T.zf[:, 15:143], (T.mf[:, 2], T.mf[:, 3]), (T.mh[:, 0], T.mh[:, 1]), T.mh[:, 2], T.mh[:, 3]
     R128, ONE = T.ro[:, 0:128], T.one[:, 0:16]
     JU = T.nj[:, 0:16]
     ts(colf("rq_"), C["q4"], C["u2"], A.add, C["h"], A.add, r=["cf"], w=["c_rq_"])
@@ -367,7 +394,7 @@ def rank_program(g, core, T, topo):
             ("k", "g16", 1.0, "rq", AF.Identity), ("k8", "k", 1.0, 12.0, AF.Identity), ("m0", "rq", 1.0, -2.0, AF.Relu),
             ("mid", "m0", -1.0, 1.0, AF.Identity), ("dum", "r", 1.0, 2049.0, AF.Identity), ("dum16", "r", 1.0, 2065.0, AF.Identity),
             ("lt8", "u2", -0.5, 1.0, AF.Identity), ("ge8", "u2", 0.5, 0.0, AF.Identity), ("rm8", "r", 16.0, -128.0, AF.Identity),
-            ("y", "g16", 0.25, "r3", AF.Identity), ("rm1", "r", 16.0, -16.0, AF.Identity), ("wl", "ge8", -1.0, "b0", AF.Abs)):
+            ("y", "g16", 0.25, "r3", AF.Identity), ("rm1", "r", 16.0, -16.0, AF.Identity), ("r10", "r", 16.0, 10.0, AF.Identity), ("wl", "ge8", -1.0, "b0", AF.Abs)):
         ac(colf(name), C[a], named(a, b), ["c_" + name], 1, bias=C.get(b, b), f=f, scale=s)
     ts(colf("s1"), C["b2"], 2.0, A.add, C["lt8"], A.mult, r=named("lt8"), w=["c_s1"])
 
@@ -385,14 +412,16 @@ def rank_program(g, core, T, topo):
     eq(T.zz[:, 1], T.ro[:], "ro", "a", None, "z1", 144)
     cp(T.zh[:], T.zz[:, 1], ["z1"], ["zh"], 72)
     eq(T.w1[:, 0:16], T.ro[:, 0:16], "ro", "r", None, "w1", 16)
-    ms(T.w1[:, 16:176], 0.0, ["w1z"], 160)
+    ac(T.w3[:], R128, ["ro", "c_r10"], ["w3"], 128, bias=C["r10"], f=AF.Abs, scale=-1.0)
+    ts(T.w3[:], T.w3[:], 5.5, A.is_lt, r=["w3"], w=["w3"])
     for h_, a in enumerate(("nh16", "h16")):
         scaled(PF[h_], PM, "pm", a, "pf%d" % h_, 128)
         ts(PH[h_], PM, C[a], A.mult, -1.0, A.mult, r=["pm", "c_" + a], w=["ph%d" % h_])
     for out, s, w in ((IF, 1.0, "if"), (NI, -1.0, "ni"), (DH[0], "nh", "dh0"), (DH[1], "h", "dh1")):
         scaled(out, IB, "ib", s, w, 128)
     cp(IH, IB, ["ib"], ["ih"])
-    scaled(ZF, Z1(0), "z1", 1.0, "zf", 128)
+    scaled(T.zf[:], T.zz[:, 1], "z1", 1.0, "zf", 144)
+    tt(ZD, Z1(3), Z1(7), A.subtract, ["z1"], ["zd"], 128)
     mm(PS[4][:, 0:128], PM, IB, True, True, ["pm", "ib"], ["ps4"], 128)
     ac(PMT, PS[4][:, 0:128], ["ps4"], ["pmt"], 128)
     ts(NPT, PMT, -1.0, A.mult, r=["pmt"], w=["npt"])
@@ -411,7 +440,7 @@ def rank_program(g, core, T, topo):
     eq(T.st[:], T.ro[:, 0:16], "ro", "s3", None, "st", 16)
     eq(T.lt[:], T.ro[:, 1:17], "ro", "s3", None, "lt", 16)
     for name, a, b in (("f2", 11, 15), ("a04", 0, 4), ("a37", 3, 7)):
-        tt(colf(name), T.w1[:, a:a + 1], T.w1[:, b:b + 1], A.add, ["w1"], ["c_" + name])
+        ac(colf(name), T.w1[:, a:a + 1], ["w1"], ["c_" + name], 1, bias=T.w1[:, b:b + 1])
     ac(colf("n37"), C["a37"], ["c_a37"], ["c_n37"], 1, bias=1.0, scale=-1.0)
     eq(BOF, T.rx[:, 3], "rx3", "g16", "f2", "bof", 128)
     for k, s, w in ((2, "a04", "za"), (3, "rm8", "zq"), (4, "a37", "z37"), (5, "wl", "zl")):
@@ -419,7 +448,6 @@ def rank_program(g, core, T, topo):
     eq(SELY, T.ro[:, 0:32], "ro", "y", "lt8", "sely", 32)
     scaled(IKP, IB, "ib", "n37", "ikp", 128)
     ts(T.dia[:], T.ii[:], C["r"], A.is_equal, r=["ii", "cf"], w=["dia"], n=128)
-    ms(T.tri[:, 0:128], 0.0, ["triz"], 128)
     ts(T.tri[:, 128:384], T.ii[:], C["rq_"], A.is_le, 8192.0, A.mult, r=["ii", "c_rq_"], w=["tri"], n=128)
     ac(T.kp[:], T.ii[:], ["ii"], ["kp"], bias=0.0, f=AF.Sign)
     ac(T.kq[:, 0:KW], T.j32[:, 0:KW], ["j32"], ["kq"], KW, bias=0.0, f=AF.Sign)
@@ -434,16 +462,12 @@ def rank_program(g, core, T, topo):
     ac(B["t17"], B["th"], ["th"], ["t17"], 16, bias=-65536.0, f=AF.Relu, scale=4096.0)
     cp(S["df"], T.c0s[:], ["c0s"], ["df0", "df1"])
     ac(T.idh[:, 0:176:11], S["df"], ["df0", "df1"], ["id_0"], 16)
-    ms(T.xd[:], 0.0, ["xdz"] + [x for k in range(8) for x in staged("xd%d" % k, 0, 16, MOVES)], 4096)
-    ms(T.one[:], 1.0, ["one"], 256)
+    ms(T.xd[:], 0.0, ["xdz"] + [x for k in range(8) for x in staged("xd%d" % k, 0, 16, XDS)], 4096)
     ms(JU, 0, ["ju"])
-    ms(B["jj"], 0.0, ["jj"])
-    ms(T.inh[:, 0:176:11], 4096.0, ["in_0"])
-    ms(T.tab[:, 0:1], 0.0, ["tabz"])
-    ms(T.tab[:, 2049:TW], 0.0, ["taby"])
-    ms(T.y3[:, 0:1], 0.0, ["y3z"])
-    ms(T.y3[:, 2049:TW], 0.0, ["y3y"])
-    ms(T.xb1[:, 128:144], 0.0, ["dfxb1"])
+    for out, n, c, w in ((B["jj"], 16, 0.0, "jj"), (T.inh[:, 0:176:11], 16, 4096.0, "in_0"), (T.tab[:, 0:1], 1, 0.0, "tabz"),
+                         (T.tab[:, 2049:TW], TW - 2049, 0.0, "taby"), (T.xb1[:, 128:144], 16, 0.0, "dfxb1"), (T.y3[:, 0:1], 1, 0.0, "y3z"),
+                         (T.y3[:, 2049:TW], TW - 2049, 0.0, "y3y"), (T.w1[:, 16:176], 160, 0.0, "w1z"), (T.tri[:, 0:128], 128, 0.0, "triz")):
+        ac(out, T.ii[:, 0:n], ["ii"], [w], n, bias=c, scale=0.0)
     to_all(T.hws[:], lambda s: T.hwa[:, 2 * rank:2 * rank + 2], "hwarr", ["hws"], "hwa", 3000, 10000)
 
     mm(PS[4][:, 0:16], PMT, B["th"], True, True, ["pmt", "th"], ["ps4"])
@@ -521,7 +545,7 @@ def rank_program(g, core, T, topo):
         calls = [(o, IB, T.sb[:, BK[n_], cs]) for o, cs in parts for n_ in bad]
         if bad:
             mms([c + (j == 0, False) for j, c in enumerate(calls)], ["ib"] + bad, k)
-        mms([(o, IH, T.fr[:, cs], j == 0 and not bad, j == len(parts) - 1) for j, (o, cs) in enumerate(parts)], ["ih", "fr"], k)
+        mms([(o, IF, T.fr[:, cs], j == 0 and not bad, j == len(parts) - 1) for j, (o, cs) in enumerate(parts)], ["if", "fr"], k, 256)
         ts(T.fs[:, p0:24], PS[5][:, 384 + p0:408], 4000.0, A.min, r=k, w=["fs"])
         mm(PS[5][:, 16 * p0:384], IB, T.tri[:, 16 * p0:384], True, False, ["ib", "tri", "triz"], k, 384 - 16 * p0)
         mms([(PS[5][:, 16 * p0 + r_:384:16], NPT, T.fs[:, p0:24], False, False) for r_ in range(16)], ["npt", "fs"], k)
@@ -579,10 +603,14 @@ def rank_program(g, core, T, topo):
         if part == 0:
             ts(SI["fi"], T.fz[:], -1.0, A.add, r=["fz"], w=["fi"])
             ts(SI["q"], SI["fi"], 7, A.bitwise_and, r=["fi"], w=["q"])
-        if part < 2:
-            qo = T.qo[:, 16 * part:16 * part + 16]
-            ts(qo, SI["q"], 2.0, A.mult, float(part), A.add, r=["q"], w=["qo%d" % part])
-            tt(T.uu[:, 256 * part:256 * part + 256], T.hwa[:].indirect(qo), T.xc[:], A.mult, ["hwa", "hwown", "qo%d" % part] + staged("xc", 0, 16, MOVES), ["uu%d" % part], 256, GA)
+            ts(B["qb"], SI["q"], 256.0, A.mult, r=["q"], w=["qb"])
+            for h_ in range(2):
+                ts(T.qo[:, 16 * h_:16 * h_ + 16], SI["q"], 2.0, A.mult, float(h_), A.add, r=["q"], w=["qo%d" % h_])
+            return
+        if part < 3:
+            h_ = part - 1
+            tt(T.uu[:, 256 * h_:256 * h_ + 256], T.hwa[:].indirect(T.qo[:, 16 * h_:16 * h_ + 16]), T.xc[:], A.mult,
+               ["hwa", "hwown", "qo%d" % h_] + staged("xc", 0, 16, MOVES), ["uu%d" % h_], 256, GA)
             return
         to_l(3, PS[3][:, 0:32], Z1, T.uu, True, ["z1", "uu0", "uu1"])
         cp(S["ub"], PS[3][:, 16:32], ["ps3"], ["ub"])
@@ -602,7 +630,7 @@ def rank_program(g, core, T, topo):
     def keys(lo, hi, bank):
         k = ["ps%d" % bank]
         mm(PS[bank][:, 0:32 * (hi - lo)], IB, T.kin[:, 2 * lo:2 * hi, :], True, False, ["ib", "kin0", "kin1"], k, max(64, 32 * (hi - lo)))
-        for eng, a, b in GATHERS:
+        for eng, a, b in OTHER.get(step["t"], GATHERS):
             if lo <= a < hi:
                 for x in [x for x in later if x[0] == a]:
                     later.remove(x)
@@ -615,13 +643,13 @@ def rank_program(g, core, T, topo):
                         p_, q, u = 16 * c + 2 * r2, r2 // 2, r2 % 2
                         s0, c0 = 8 * (2 * p_ + 1 - u), 32 * (c - lo)
                         calls.append((PS[bank][32 * q:32 * q + 32, c0:c0 + 32], T.xd[:, s0:s0 + 32], T.gg[:, 16 * p_:16 * p_ + 32], False, False))
-                    mms(calls, [x for j in range(8) for x in staged("xd%d" % j, c, c + 1, MOVES)] + ["gg%d" % c], k, 32)
+                    mms(calls, [x for j in range(8) for x in staged("xd%d" % j, c, c + 1, XDS)] + ["gg%d" % c], k, 32)
         mm(PS[bank][:, 0:8], IB, T.xd[:, 0:8], False, True, ["ib", "xdz"], k)
 
     def test(t, lo, hi, bank, eng):
         n, cs, k, me = 32 * (hi - lo), slice(32 * lo, 32 * hi), "ps%d" % bank, "_%d" % lo
         keys(lo, hi, bank)
-        if eng == "act":
+        if (eng == "act") != (t in SWAP):
             ac(T.ind[:, cs], PS[bank][:, 0:n], [k], ["ind" + me], n, bias=0.5, f=AF.Sign)
         else:
             ts(T.ind[:, cs], PS[bank][:, 0:n], -0.5, A.is_ge, -0.5, A.add, r=[k], w=["ind" + me], n=n)
@@ -637,17 +665,22 @@ def rank_program(g, core, T, topo):
                 ["ib"] + [x for n_ in range(1, t + 1) for x in staged("in%d" % n_, lo, hi)], k7)
         if lo == 0:
             mm(PS[7][:, 0:16], IB, B["jj"], False, False, ["ib", "jj"], k7)
-            mm(PS[7][:, 32:48], IF, S["df"], False, False, ["if", "df0", "df1"], k7, 256)
-            mm(PS[7][:, 32:48], IB, all_, False, False, ["ib"] + ak, k7)
+            mm(PS[7][:, 48:64], IF, S["df"], False, False, ["if", "df0", "df1"], k7, 256)
+            if t % 5 == 4:
+                mms([(PS[7][:, 32:48], IB, B[n_], False, False) for n_ in ("jj", "qb")], ["ib", "jj", "qb"], k7)
+                mm(PS[7][:, 32:48], NI, all_, False, False, ["ni"] + ak, k7)
+            mm(PS[7][:, 48:64], IB, all_, False, False, ["ib"] + ak, k7)
             mm(PS[7][:, 0:16], NI, all_, False, False, ["ni"] + ak, k7)
         mm(o, IB, T.inh[:, 11 * lo + t + 1:11 * hi:11], False, True, ["ib"] + staged("in%d" % (t + 1), lo, hi), k7)
         first = 16 + lo if lo else 0
-        ts(T.nj[:, first:16 + hi], PS[7][:, first:16 + hi], 1.0 / 16, A.mult, 1.0, A.add, r=k7, w=["nu_%d" % lo] + ([] if lo else ["ju"]))
+        cs = slice(first, 48 if t % 5 == 4 else 16 + hi)
+        ts(T.nj[:, cs], PS[7][:, cs], 1.0 / 16, A.mult, 1.0, A.add, r=k7, w=["nu_%d" % lo, "ju", "wu"])
         if t == NSUB - 1:
             place(T.yxs, t + 1, lo, hi, "yxs")
         else:
             place(T.xc, t + 1, lo, hi, "xc")
-            expand("xc", "xc_%d" % lo, NPOOL[int(lo == 0)], lo, hi)
+            for k, (a, b) in enumerate(XDS):
+                expand("xc", "xc_%d" % lo, NPOOL[k], a, b)
 
     def stage(t, lo, hi, per):
         last, all_, ak = t == NSUB - 1, T.inh[:, t + 1:176:11], staged("in%d" % (t + 1))
@@ -677,14 +710,16 @@ def rank_program(g, core, T, topo):
             ts(T.iu[:], o, 7.5, A.add, r=["ps4"], w=["iu"])
             if t < SRT:
                 ts(T.sr[:], T.cod[:], 0.5, A.mult, -0.25, A.add, r=coded(0, 16), w=["sr"], n=256)
-                tt(T.sg[:], T.w1[:].indirect(T.iu[:]), T.sr[:], A.mult, ["w1", "w1z", "iu", "sr"], ["sg%d" % a for a, b in SGS], 256, GA)
+                for a, b in SGS if t >= 2 else ((0, 16),):
+                    tt(T.sg[:, 16 * a:16 * b], T.w1[:].indirect(T.iu[:, a:b]), T.sr[:, 16 * a:16 * b], A.mult, ["w1", "w1z", "iu", "sr"],
+                       ["sg%d" % x for x, y in SGS if a <= x < b], 16 * (b - a), GA)
             else:
                 ac(T.sh[:], T.w1[:].indirect(T.iu[:]), ["w1", "w1z", "iu"], ["sh"], k=GA, scale=HALF)
                 for a, b in SGS:
                     tt(T.sg[:, 16 * a:16 * b], T.sfs[:].indirect(T.du[:, a:b]), T.sh[:, 16 * a:16 * b], A.mult, ["sfs", "du0", "du1", "sh"], ["sg%d" % a], 16 * (b - a), GA)
             o = PS[6][:, 0:16]
             if t > 0:
-                mm(o, IH, T.fr[:], True, False, ["ih", "fr"], ["ps6"])
+                mm(o, IF, T.fr[:], True, False, ["if", "fr"], ["ps6"], 256)
             mm(o, NI, all_, t == 0, False, ["ni"] + ak, ["ps6"])
             to_l(6, o, ZH, T.sg, False, ["zh"] + ["sg%d" % a for a, b in SGS])
             ts(T.fz[:], o, 0.75, A.add, r=["ps6"], w=["fz"])
@@ -692,7 +727,7 @@ def rank_program(g, core, T, topo):
             lowest(tk, ins, [ik], lo, hi, per)
             scatters(T.tab, T.ncl, lambda c: ["ncl"], TAB, lo, hi, per)
 
-    for s in MOVES:
+    for s in XDS:
         expand("xt", "x0", 4, s[0], s[1])
     row_mask(0)
     codes()
@@ -701,7 +736,7 @@ def rank_program(g, core, T, topo):
         last, ex, e = t == NSUB - 1, t % 5 == 4, t // 5
         step.clear()
         step["t"] = t
-        for part in range(3):
+        for part in range(4):
             if ASKS[part] == t % 5:
                 request(e, part)
         if t >= 2:
@@ -710,7 +745,7 @@ def rank_program(g, core, T, topo):
         for s in STAGES:
             stage(t, *s)
         idd, idk = T.idh[:, t + 1:176:11], "id_%d" % (t + 1)
-        ac(idd, PS[7][:, 32:48], k7, [idk], 16, bias=-4096.0, f=AF.Relu)
+        ac(idd, PS[7][:, 48:64], k7, [idk], 16, bias=-4096.0, f=AF.Relu)
         if ex:
             rivals(None)
             ac(B["jj"], PS[7][:, 0:16], k7, ["jj"], 16, bias=16.0, f=AF.Relu)
@@ -719,7 +754,7 @@ def rank_program(g, core, T, topo):
         if last:
             dma("sync", T.yx[:], T.yxs[:], "o_yx", staged("yxs", 0, 16, MOVES), ["yx"], 2500)
         else:
-            ts(T.fr[:], T.fz[:], -1.0, A.add, 0.0, A.max, r=["fz"], w=["fr"])
+            ac(T.fr[:], PS[6][:, 0:16], ["ps6"], ["fr"], 16, bias=0.0, f=AF.Relu)
         if ex:
             xb, rq = T["xb%d" % e], T["req%d" % e]
             rk = TAB + ["rqarr%d" % e, "rqown%d" % e]
@@ -762,19 +797,16 @@ def rank_program(g, core, T, topo):
         if not last:
             ac(xb[:, 128:144], PS[3][:, 0:16], ["ps3"], ["dfxb0"], 16)
             columns()
-        ts(S["nw"], B["jj"], 80.0, A.is_lt, 16.0, A.mult, r=["jj"], w=["nw"])
-        tt(S["t1"], S["nw"], SI["q"], A.add, ["nw", "q"], ["t1s"])
-        cp(T.wu[:], S["t1"], ["t1s"], ["wu"])
-        ac(T.oh[:], T.w1[:].indirect(T.wu[:]), ["w1", "w1z", "wu"], ["oh"], k=GA)
-        scan(T.cum[:], T.one[:], T.oh[:], A.mult, A.add, ["one", "oh"], ["cum"], 256, CY / 2)
-        ts(T.le[:], T.cum[:], 16.0, A.is_le, r=["cum"], w=["le"], n=128)
-        tt(T.svr[:], T.le[:], T.oh[:], A.mult, ["le", "oh"], ["svr"], 256)
-        mm(PS[6][:, 0:16], IB, B["cb"], True, False, ["ib", "cb"], ["ps6"])
-        to_l(6, PS[6][:, 0:16], ZQ, T.svr, False, ["zq", "svr"])
-        ts(B["sv"], PS[6][:, 0:16], 128.0, A.is_lt, 4096.0, A.mult, r=["ps6"], w=["sv"])
-        cp(T.pu[:], PS[6][:, 0:16], ["ps6"], ["pu"])
-        mm(PS[3][:, 0:16], PMT, B["sv"], True, True, ["pmt", "sv"], ["ps3"])
-        ac(T.tot[:, 31:512:32], PS[3][:, 0:16], ["ps3"], staged("tot", 0, 16, BANKS), 16, bias=-0.5, scale=1.0 / 4096)
+        ac(T.oh[:], T.w3[:].indirect(T.nj[:, 32:48]), ["w3", "wu"], ["oh"], k=GA)
+        ac(T.le[:], T.oh[:], ["oh"], ["le"], scale=16.5)
+        scan(T.cum[:], T.oh[:], T.oh[:], A.add, A.max, ["oh"], ["cum"], 256, CY / 2, 0.5)
+        tt(T.svr[:], T.le[:], T.cum[:], A.is_ge, ["le", "cum"], ["svr"], 256)
+        mm(PS[2][:, 0:16], IB, B["cb"], True, False, ["ib", "cb"], ["ps2"])
+        to_l(2, PS[2][:, 0:16], ZQ, T.svr, False, ["zq", "svr"])
+        ts(B["sv"], PS[2][:, 0:16], 128.0, A.is_lt, 4096.0, A.mult, r=["ps2"], w=["sv"])
+        cp(T.pu[:], PS[2][:, 0:16], ["ps2"], ["pu"])
+        mm(PS[5][:, 0:16], PMT, B["sv"], True, True, ["pmt", "sv"], ["ps5"])
+        ac(T.tot[:, 31:512:32], PS[5][:, 0:16], ["ps5"], staged("tot", 0, 16, BANKS), 16, bias=-0.5, scale=1.0 / 4096)
         lowest(staged("tot", 0, 16, BANKS), B["sv"], ["sv"])
         if not last:
             mm(PS[7][:, 0:16], IB, B["jj"], True, False, ["ib", "jj"], k7)
@@ -791,10 +823,9 @@ def rank_program(g, core, T, topo):
             codes()
             ac(S["df"], an, ["asc"], ["df0", "df1"], 16)
             ac(T.dg[:, 0:256], T.ag[:], ["ag"], ["dg0"])
-            tt(T.dg[:, 256:512], T.ag[:], T.dg[:, 0:256], A.subtract, ["ag", "dg0"], ["dg1"], 512)
             mm(PS[4][:, 0:256], IKP, T.col[:], True, False, ["ikp", "col"], ["ps4"], 256)
-            mm(PS[4][:, 0:256], Z1(3), T.dg[:, 0:256], False, False, ["z1", "dg0"], ["ps4"], 256)
-            mm(PS[4][:, 0:256], Z1(7), T.dg[:, 256:512], False, True, ["z1", "dg1"], ["ps4"], 256)
+            mm(PS[4][:, 0:256], T.zf[:, 8:136], T.ag[:], False, False, ["zf", "ag"], ["ps4"], 1024)
+            mm(PS[4][:, 0:256], ZD, T.dg[:, 0:256], False, True, ["zd", "dg0"], ["ps4"], 256)
             ac(T.ncl[:], PS[4][:, 0:256], ["ps4"], ["ncl"])
             scatters(T.tab, T.ncl, lambda c: ["ncl"], TAB)
             columns()

import numpy as np
from concourse.bass import DstId, RemoteDMATransfer
from concourse.mybir import AluOpType as A, ActivationFunctionType as AF

F32, B16, I32, U16, F16 = "float32", "bfloat16", "int32", "uint16", "float16"
N, NSUB, TW = 8, 10, 2096
BANKS = ((4, 16, 0, "dve"), (0, 4, 1, "act"))
STAGES = ((4, 16, 2), (0, 4, 2))
MOVES = ((0, 16),)
XDS = ((0, 16),)
FRAC, SRT, HALF, LGS = 0, 10, 0.49995, 0
GATHERS = (("act", 14, 16), ("dve", 12, 14), ("act", 10, 12), ("dve", 8, 10), ("dve", 5, 6), ("act", 6, 8), ("dve", 4, 5), ("act", 2, 4),
           ("dve", 1, 2), ("act", 0, 1))
EVEN = (("act", 14, 16), ("dve", 12, 14), ("act", 10, 12), ("dve", 8, 10), ("act", 6, 8), ("dve", 4, 6), ("act", 2, 4), ("dve", 0, 2))
LATER = (None, None)
SPANS = []
ALIKE = (2, 3, 6, 7, 8)
SWAP = (0, 1)
OTHER = {0: EVEN, 1: EVEN,
         5: (("act", 14, 16), ("act", 12, 14), ("dve", 10, 12), ("act", 8, 10), ("act", 6, 8), ("dve", 4, 6), ("act", 2, 4), ("act", 0, 2))}
ASKS, XB = (1, 2, 3, 3), 1
SGS = ((0, 8), (8, 16))
QUEUES = {"dve": "-cod1 -cod2 gg1 gg2 gg3 gg4 gg5 ind1 tot1 ee1 ee2 in1 mns1 sr1 tot2 mns2 ee3 mv1 ou1 ou2 in2 tab1 ee4 tab2 iu1 nu1 tab3 sg1 tab4 sg2 "
                 "tab5 ou3 ou4 tab6 tab7 fz1 tab8 lg1 +uu1 du1",
          "act": "-xd1 -xd2 -xd3 -xd4 -x1 gg1 gg2 gg3 -thr1 gg4 gg5 ind1 ncl1 xc1",
          "pe": "ps16 ps22 ps24 ps44 ps45 ps46 ps47 ps26 ps28"}
LOOSE = {t: {"dve": "-cod1 -cod2 gg1 gg2 gg3 gg4 gg5 ind1 tot1 ee1 ee2 in1 tot2 ee3 ou1 ou2 in2 tab1 ee4 tab2",
             "act": "gg1 gg2 gg3 -thr1 gg4 gg5 ind1 ncl1", "pe": "ps16 ps22 ps24"} for t in (4, 9)}
LOOSE[5] = {"dve": "-ag1 -asc1 -du1 -cod1 -cod2 gg1 -tab9 -tab10 -tab11 -tab12 gg2 -tab13 -tab14 -tab15 -tab16 ind1 tot1 lg1 ee1 ee2",
            "act": "-dg1 -ncl2 gg1 gg2 gg3 gg4 gg5 -col2 gg6 -thr2 ind1 ncl1"}
SEED = 2
SHIFT, SLACK = 600, 200
CODES = ((12, 16), (0, 12))
NPOOL = (4, 4)
ROUND = 12582912.0
GA, SC, CY, PE = 1.42, 3.5, 0.88, 0.47
RULE, SAME, CROSS, FIX = 0.5, 160, 170, 50
ALL = range(-1, NSUB)
PASSES = (((6, 7, 8), 2500), (ALL, 1), (ALL, 1), (ALL, 1), ((-1, 0, 1, 2), 5000), ((3, 4, 5, 6), 5000), ((8, 9), 3000), (ALL, 1), (ALL, 1), (ALL, 2000))
ORDER = {}
LOADS, ASK, ANSWER = (2200, 3600, 7500, 8200), 4000, 3000


def _s(shape, d):
    return ("sbuf", shape, d)


SCRATCH = {
    "sfs": _s([128, 3072], I32), "pws": _s([128, 2048], B16), "pw2": _s([128, 4096], B16), "otq": _s([128, 512], I32),
    "oth": _s([128, 512], B16), "otl": _s([128, 512], B16), "tab": _s([128, TW], B16), "xt": _s([128, 11 * 256], B16),
    "stp": _s([128, 256], B16), "xa": _s([128, 256], B16), "xc": _s([128, 256], B16),
    "c0s": _s([128, 16], I32), "ths": _s([128, 16], I32), "hws": _s([128, 2], B16), "hwa": _s([128, 16], B16),
    "xd": _s([128, 4096], B16), "gg": _s([128, 4096], B16), "kin": _s([128, 32, 16], B16),
    "cod": _s([128, 256], U16), "sr": _s([128, 256], I32), "ind": _s([128, 512], B16), "mns": _s([128, 512], F32),
    "tot": _s([128, 512], B16), "sg": _s([128, 256], F16), "ee": _s([128, 384], B16), "thr": _s([128, 384], B16), "lg": _s([128, 256], B16),
    "lm": _s([128, 512], B16), "col": _s([128, 256], B16), "mm": _s([128, 256], B16), "ncl": _s([128, 256], B16),
    "t0": _s([128, 256], B16), "t1": _s([128, 256], B16), "sh": _s([128, 256], F32), "thq": _s([128, 16], F32),
    "uu": _s([128, 512], B16), "hg": _s([128, 2048], B16), "dg": _s([128, 512], B16),
    "ag": _s([128, 256], F32), "ya": _s([128, 2048], F32), "y3": _s([128, TW], F32),
    "yxs": _s([128, 256], F32), "anr": _s([128, 256], F32), "oh": _s([128, 256], B16), "cum": _s([128, 256], B16),
    "le": _s([128, 256], B16), "svr": _s([128, 256], B16), "asc": _s([128, 256], F32),
    "req0": _s([128, 128], U16), "req1": _s([128, 128], U16), "xb0": _s([128, 256], F32), "xb1": _s([128, 256], F32),
    "inh": _s([128, 176], B16), "idh": _s([128, 176], F32), "nih": _s([128, 176], F32), "csc": _s([128, 176], F32),
    "sm": _s([128, 8, 16], F32), "sb": _s([128, 9, 16], B16), "w3": _s([128, 128], B16), "si": _s([128, 4, 16], I32), "mv": _s([128, 32], F16), "mw": _s([128, 32], F16),
    "fs": _s([128, 24], F16), "fr": _s([128, 16], F32),
    "du": _s([128, 16], U16), "fz": _s([128, 16], U16), "iu": _s([128, 16], U16), "nj": _s([128, 48], U16),
    "ou": _s([128, 48], U16), "qo": _s([128, 32], U16), "wu": _s([128, 16], U16), "eo": _s([128, 24], U16),
    "pu": _s([128, 16], U16), "bc": _s([128, 16], U16),
    "pi": _s([128, 8], I32), "ci": _s([128, 12], I32), "cf": _s([128, 48], F32), "ro": _s([128, 144], F32),
    "rx": _s([128, 4, 128], F32), "ii": _s([128, 256], B16), "kp": _s([128, 256], B16), "j32": _s([128, 384], B16),
    "kq": _s([128, 384], B16), "bq": _s([128, 384], B16),
    "one": _s([128, 256], B16), "tri": _s([128, 384], B16), "dia": _s([128, 256], B16), "fh": _s([128, 512], B16),
    "fl": _s([128, 512], B16), "zz": _s([128, 6, 144], B16), "zh": _s([128, 144], F16), "zf": _s([128, 144], F32), "mb": _s([128, 24, 128], B16),
    "mf": _s([128, 4, 128], F32), "mh": _s([128, 4, 128], F16), "hq": _s([128, 7, 144], B16), "w1": _s([128, 176], B16), "lt": _s([128, 16], B16),
    "st": _s([128, 16], B16), "r3": _s([128, 16], F32),
}
for _b in range(8):
    SCRATCH["ps%d" % _b] = ("psum", [128, 512], F32)
SEMAPHORES = ["pool", "pe", "dve", "act", "l_c0", "l_sf", "l_ot", "l_x0", "l_pw", "l_dr", "l_th", "l_hw", "l_hs", "hwarr",
              "rq0", "rq1", "an0", "an1", "sent", "o_ya", "o_y3", "o_yc", "o_yx"]


def slots(T, topo, h):
    ch = topo.chip(T.cores[h])

    def far(s):
        cs = topo.chip(T.cores[s])
        return (3 if s == h else 2 if cs == ch else 1 if topo.same_plane(cs, ch) else 0, s)
    return sorted(range(N), key=far)


def off_engines(T, topo, src):
    return topo.engines(src, [c for c in T.cores if topo.chip(c) != topo.chip(src)][0])


def share(T, topo, src, dsts):
    off = off_engines(T, topo, src)
    far = [d for d in dsts if topo.chip(d) != topo.chip(src)]
    per = 1
    while far and 2 * per * len(far) <= len(off):
        per *= 2
    out = {d: off[k * per:(k + 1) * per] for k, d in enumerate(far)}
    for d in dsts:
        if d not in out:
            out[d] = [e for e in topo.engines(src, d) if e not in off]
    return out


def bits(engines):
    return sum(1 << e for e in engines)


def schedule(ops):
    n = len(ops)
    succ = [[] for _ in range(n)]
    for i, o in enumerate(ops):
        pre = {}
        for d in o["deps"]:
            if isinstance(d, tuple):
                for a in d[2]:
                    pre[a] = max(pre.get(a, 0), d[3])
            else:
                pre[d] = max(pre.get(d, 0), ops[d]["lat"] + (SAME if ops[d]["eng"] == o["eng"] else CROSS))
        for d in o["ord"]:
            pre.setdefault(d, 0)
        for d, l in pre.items():
            succ[d].append((i, l))
    at = {(o["step"], o["eng"], o["kind"][0][1] + str(o["kind"][1])): i for i, o in enumerate(ops)}
    for eng, names in QUEUES.items():
        for t in range(NSUB):
            names_ = names if t in ALIKE else LOOSE.get(t, {}).get(eng, "")
            row = [at.get((t - x.startswith("-") + x.startswith("+"), eng, x.strip("-+"))) for x in names_.split()]
            row = [i for i in row if i is not None]
            for a, b in zip(row, row[1:]):
                succ[a].append((b, 0))
    left, order = [0] * n, []
    for i in range(n):
        for j, l in succ[i]:
            left[j] += 1
    todo = [i for i in range(n - 1, -1, -1) if not left[i]]
    while todo:
        order.append(todo.pop())
        for j, l in succ[order[-1]]:
            left[j] -= 1
            if not left[j]:
                todo.append(j)
    assert len(order) == n
    prio = [0.0] * n
    for i in reversed(order):
        prio[i] = ops[i]["cost"] + max([l + prio[j] for j, l in succ[i]] + [ops[i]["lat"]])
    shift = {}
    for steps, passes in PASSES:
        part = [i for i in order if ops[i]["step"] in steps]
        new = {i: k for k, i in enumerate(part)}
        after = [[(new[j], l) for j, l in succ[i] if j in new] for i in part]
        end = settle([ops[i] for i in part], after, [prio[i] for i in part], shift, passes)
        if len(part) == n and passes == 1:
            before = [[] for _ in part]
            for a in range(n):
                for b, l in after[a]:
                    before[b].append((a, l))
            back = deal([ops[i]["cost"] for i in part], [ops[i]["eng"] for i in part], before, end, [ops[i]["lat"] for i in part])
            prio, shift = [back[new[i]] for i in range(n)], {o["kind"]: 0.0 for o in ops if o["kind"][2] is None}
    return sorted(range(n), key=lambda i: (end[new[i]] - ops[i]["cost"], new[i]))


def settle(ops, succ, prio, shift, passes):
    n, kinds = len(ops), {}
    for i, o in enumerate(ops):
        kinds.setdefault(o["kind"], []).append(i)
    pick = [k for k, v in kinds.items() if k not in shift] or list(kinds)
    shift.update({k: shift.get(k[:2] + (None,), 0.0) for k in kinds if k not in shift})
    cost, tail, eng = [o["cost"] for o in ops], [o["lat"] for o in ops], [o["eng"] for o in ops]
    back = [(i, [j for j, l in succ[i]]) for i in range(n - 1, -1, -1) if succ[i]]
    now = [p + shift.get(o["kind"], 0.0) for p, o in zip(prio, ops)]
    best, span, rng = None, 1e30, np.random.default_rng(SEED)
    for k in range(passes):
        kind, d, p = pick[int(rng.integers(len(pick)))], float(rng.normal()) * SHIFT * (k > 0), list(now)
        for i in kinds[kind]:
            p[i] += d
        for i, js in back:
            top = max([p[j] for j in js])
            if p[i] <= top:
                p[i] = top + 1
        end = deal(cost, eng, succ, p)
        time = max([e + l for e, l in zip(end, tail)])
        if time <= span - SLACK * (1 - k / passes) * float(np.log(1 - rng.random())):
            span = time
            shift[kind] = shift.get(kind, 0.0) + d
            for i in kinds[kind]:
                now[i] += d
            if best is None or time < best[0]:
                best = (time, end, dict(shift))
    shift.update(best[2])
    SPANS.append(best[0])
    return best[1]


def deal(cost, eng, succ, prio, ready=None):
    n = len(cost)
    busy, end, ready = {e: [] for e in eng}, [0.0] * n, ready or [0.0] * n
    for i in sorted(range(n), key=lambda i: -prio[i]):
        l, st, c = busy[eng[i]], ready[i], cost[i]
        a = len(l)
        if a and l[-1][1] > st:
            b, a = a, 0
            while a < b:
                m = (a + b) // 2
                if l[m][1] <= st:
                    a = m + 1
                else:
                    b = m
            b = len(l)
            while a < b and l[a][0] < st + c:
                st = l[a][1]
                a += 1
        e = end[i] = st + c
        l.insert(a, (st, e))
        for j, lat in succ[i]:
            if ready[j] < e + lat:
                ready[j] = e + lat
    return end


def rank_program(g, core, T, topo):
    rank = T.rank_of(core)
    if rank is None:
        return
    Q = {"pool": g, "pe": g.tensor, "dve": g.vector, "act": g.scalar, "sync": g.sync}
    ops, lastw, readers, later, step = [], {}, {}, [], {}

    def op(eng, fn, r, w, cost, dma=None, lat=0.0):
        deps, order = [], []
        for k in r:
            if k in lastw:
                deps.append(lastw[k])
            if k.startswith("ps"):
                deps += [x for x in readers.get(k, []) if ops[x]["eng"] != eng]
        for k in w:
            for x in readers.get(k, []) + ([lastw[k]] if k in lastw else []):
                (order if k.startswith("ch") or (eng == "pe" and ops[x]["eng"] == "pe") else deps).append(x)
        name = (w or r)[0]
        kind = (eng, name if name.startswith("ps") or "t" not in step else "".join(x for x in name.split("_")[0] if x > "9"), "t" in step)
        step[kind] = step.get(kind, 0) + 1
        ops.append({"kind": (kind, step[kind], None if step.get("t") in ALIKE else step.get("t", -1)), "step": step.get("t", -1), "eng": eng, "fn": fn, "deps": deps, "ord": order, "dma": dma, "sig": False, "cost": cost, "lat": lat})
        me_ = len(ops) - 1
        for k in r:
            readers.setdefault(k, []).append(me_)
        for k in w:
            lastw[k] = me_
            readers[k] = []
        return me_

    v = g.vector

    def vc(n, k):
        return FIX + (max(64 * CY, n * k) if k < GA else n * k)

    def ts(out, in0, s1, o0, s2=None, o1=None, r=(), w=(), n=16, k=CY):
        if o1 is None:
            op("dve", lambda: v.tensor_scalar(out, in0, s1, None, o0), r, w, vc(n, k))
        else:
            op("dve", lambda: v.tensor_scalar(out, in0, s1, s2, o0, o1), r, w, vc(n, k))

    def tt(out, a, b, o, r, w, n=16, k=CY):
        op("dve", lambda: v.tensor_tensor(out, a, b, o), r, w, vc(n, k))

    def cp(out, a, r, w, n=16, k=CY):
        op("dve", lambda: v.tensor_copy(out, a), r, w, vc(n, k))

    def ms(out, c, w, n=16):
        op("dve", lambda: v.memset(out, c), (), w, vc(n, CY / 2))

    def scan(out, d0, d1, o0, o1, r, w, n=256, k=CY, first=0.0):
        op("dve", lambda: v.tensor_tensor_scan(out, d0, d1, first, o0, o1), r, w, vc(n, k))

    def ac(out, a, r, w, n=256, k=CY, bias=None, f=AF.Identity, scale=1.0):
        if bias is None:
            op("act", lambda: g.scalar.activation(out, a, AF.Copy, scale=scale), r, w, 15 + vc(n, k))
        else:
            op("act", lambda: g.scalar.activation(out, a, f, bias=bias, scale=scale), r, w, 15 + vc(n, k))

    def mm(out, l, rh, st, sp, r, w, n=64):
        op("pe", lambda: g.tensor.matmul(out, l, rh, st, sp), r, w, n * PE)

    def mms(calls, r, w, n=64):
        op("pe", lambda: [g.tensor.matmul(*c) for c in calls][-1], r, w, len(calls) * n * PE)

    def iota(out, pat, base, cm, w, n, flag=True):
        if flag:
            op("pool", lambda: g.iota(out, pat, base, cm, allow_small_or_imprecise_dtypes=True), (), w, 130 + 2 * CY * n)
        else:
            op("pool", lambda: g.iota(out, pat, base, cm), (), w, 130 + 2 * CY * n)

    def dma(eng, out, in_, sem, r, w, lat):
        op(eng, lambda: Q[eng].dma_start(out, in_), r, w + ["q" + eng + sem], 60, dma=sem, lat=lat)

    PS = [T["ps%d" % b] for b in range(8)]

    def to_l(bank, out, z, src, first, rk, lo=0, hi=None, stop=True):
        mms([(out, z(r_), src[:, lo + r_:hi:16], first and r_ == 0, stop and r_ == 15) for r_ in range(16)], rk, ["ps%d" % bank])

    def zw(k):
        return lambda r_: T.zz[:, k, 15 - r_:143 - r_]
    Z4Q, Z1, ZA, ZQ, Z37, ZL = [zw(k) for k in range(6)]

    def ZH(r_):
        return T.zh[:, 15 - r_:143 - r_]

    def staged(name, lo=0, hi=16, parts=None):
        return ["%s_%d" % (name, s[0]) for s in parts or STAGES if s[0] < hi and lo < s[1]]

    peers = [s for s in range(N) if s != rank]
    far = [s for s in peers if topo.chip(T.cores[s]) != topo.chip(core)]
    near = [s for s in peers if s not in far]
    sent = [0]

    def dst(s):
        a = topo.addr(T.cores[s])
        return DstId(rid=a[0], pnc=a[1])

    def to_all(src, land, sem, r, key, cost, lat):
        off = off_engines(T, topo, core)
        trs = [RemoteDMATransfer(dst_ids=[dst(s) for s in far], dma_engine_mask=bits(off), remote_sem=T.sem[sem], srcs=[src], dsts=[land(s) for s in far])]
        sent[0] += len(off)
        for s in near:
            en = share(T, topo, core, [T.cores[s]])[T.cores[s]]
            trs.append(RemoteDMATransfer(dst_ids=[dst(s)], dma_engine_mask=bits(en), remote_sem=T.sem[sem], src=src, dst=land(s)))
            sent[0] += len(en)
        me_ = op("pool", lambda: g.remote_dma_fused(trs, local_sem=T.sem.sent), r, (), cost)
        come = sum(len(off_engines(T, topo, T.cores[s])) for s in far) + sum(len(share(T, topo, T.cores[s], [core])[core]) for s in near)
        lastw[key] = (sem, come, [me_], lat)

    def halves(h):
        sl = slots(T, topo, h)
        return [sl[0:4], [s for s in sl[4:8] if s != h]]

    def answer_engines(h, half):
        return share(T, topo, T.cores[h], [T.cores[s] for s in halves(h)[half]])

    ans_in = sum(len(answer_engines(h, hf)[core]) for h in peers for hf in range(2) if rank in halves(h)[hf])
    myslots = slots(T, topo, rank)

    dma("act", T.xt[:, 0:256], T.x0[:], "l_x0", [], ["x0", "chq"], LOADS[0])
    dma("act", T.ths[:], T.th[:], "l_th", [], ["ths", "chq"], LOADS[0])
    dma("act", T.stp[:], T.dr[:], "l_dr", [], ["stp", "chq"], LOADS[0])
    dma("sync", T.c0s[:], T.c0[:], "l_c0", [], ["c0s", "chs"], LOADS[0])
    dma("sync", T.hws[:], T.hw[:], "l_hs", [], ["hws", "chs"], LOADS[0])
    dma("sync", T.pws[:], T.pw[:], "l_pw", [], ["pws", "chs"], LOADS[1])
    dma("sync", T.sfs[:], T.sf[:], "l_sf", [], ["sfs", "chs"], LOADS[2])
    dma("sync", T.otq[:], T.ot[:], "l_ot", [], ["otq", "chs"], LOADS[3])
    dma("sync", T.hwa[:, 2 * rank:2 * rank + 2], T.hw[:], "l_hw", [], ["hwown", "chs"], LOADS[3])

    KW = 32 * max(s[1] - s[0] for s in BANKS)
    iota(T.pi[:, 0:1], [[0, 1]], 0, 1, ["pi"], 1, False)
    iota(T.ro[:], [[1, 144]], 0, 0, ["ro"], 144)
    iota(T.ii[:], [[0, 16], [1, 16]], 0, 0, ["ii"], 256)
    iota(T.j32[:, 0:KW], [[0, KW // 32], [1, 32]], 0, 0, ["j32"], KW)
    iota(T.fh[:], [[64, 8], [0, 64]], 0, 512, ["fh"], 512)
    iota(T.fl[:], [[0, 8], [1, 64]], 1, 0, ["fl"], 512)
    iota(T.rx[:, 0], [[2, 64], [-1, 2]], 1, 0, ["rx0"], 128)
    iota(T.rx[:, 1], [[4, 32], [-1, 4]], 3, 0, ["rx1"], 128)
    iota(T.rx[:, 2], [[16, 8], [-8, 2], [1, 8]], 8, 0, ["rx2"], 128)
    iota(T.rx[:, 3], [[0, 16], [16, 8]], 0, 0, ["rx3"], 128)
    C, CK = {}, {}

    def colf(name):
        k = len(C)
        C[name], CK[name] = T.cf[:, k:k + 1], k
        return C[name]

    def named(*xs):
        return ["cf"] + ["c_" + x for x in xs if isinstance(x, str)]
    first = (("r", 15, 0), ("g16", 112, 0), ("r3", 3, 0), ("rq", 15, 2), ("b2", 2, 0), ("p", 127, 0),
             ("g8", 7, 0), ("q4", 96, 3), ("u2", 8, 2), ("h", 16, 4), ("b0", 1, 0))
    for k, (n_, m, sh) in enumerate(first):
        ts(T.ci[:, k:k + 1], T.pi[:, 0:1], m, A.bitwise_and, sh, A.logical_shift_right, r=["pi"], w=["ci%d" % k])
        colf(n_)
    cp(T.cf[:, 0:11], T.ci[:, 0:11], ["ci%d" % k for k in range(11)], ["cf"])
    S = {n_: T.sm[:, k] for k, n_ in enumerate(("df", "ub", "nw", "yc", "t1"))}
    BK = {n_: k for k, n_ in enumerate(("jj", "nc", "e5", "t17", "pb", "sv", "th", "cb", "qb"))}
    B = {n_: T.sb[:, k] for n_, k in BK.items()}
    SI = {n_: T.si[:, k] for k, n_ in enumerate(("fi", "q", "pr", "h"))}
    IB, BM, BOF, IKP, SELY = T.mb[:, 0], T.mb[:, 7], T.mb[:, 8], T.mb[:, 9], T.mb[:, 10, 0:32]
    NI, PM, PMT, DH = T.mb[:, 6], T.mb[:, 14], T.mb[:, 15], (T.mb[:, 16], T.mb[:, 17])
    ZD = T.mb[:, 18]
    IF, ZF, PF, PH, NPT, IH = T.mf[:, 0], T.zf[:, 15:143], (T.mf[:, 2], T.mf[:, 3]), (T.mh[:, 0], T.mh[:, 1]), T.mh[:, 2], T.mh[:, 3]
    R128, ONE = T.ro[:, 0:128], T.one[:, 0:16]
    JU = T.nj[:, 0:16]
    ts(colf("rq_"), C["q4"], C["u2"], A.add, C["h"], A.add, r=["cf"], w=["c_rq_"])
    for name, a, s, b, f in (
            ("lp", "g8", 16.0, "rq_", AF.Identity), ("aq", "g8", 16.0, 15.0, AF.Identity), ("nh", "h", -1.0, 1.0, AF.Identity),
            ("h16", "h", 16.0, 0.0, AF.Identity), ("nh16", "h", -16.0, 16.0, AF.Identity), ("a", "g16", 1.0, 15.0, AF.Identity),
            ("k", "g16", 1.0, "rq", AF.Identity), ("k8", "k", 1.0, 12.0, AF.Identity), ("m0", "rq", 1.0, -2.0, AF.Relu),
            ("mid", "m0", -1.0, 1.0, AF.Identity), ("dum", "r", 1.0, 2049.0, AF.Identity), ("dum16", "r", 1.0, 2065.0, AF.Identity),
            ("lt8", "u2", -0.5, 1.0, AF.Identity), ("ge8", "u2", 0.5, 0.0, AF.Identity), ("rm8", "r", 16.0, -128.0, AF.Identity),
            ("y", "g16", 0.25, "r3", AF.Identity), ("rm1", "r", 16.0, -16.0, AF.Identity), ("r10", "r", 16.0, 10.0, AF.Identity), ("wl", "ge8", -1.0, "b0", AF.Abs)):
        ac(colf(name), C[a], named(a, b), ["c_" + name], 1, bias=C.get(b, b), f=f, scale=s)
    ts(colf("s1"), C["b2"], 2.0, A.add, C["lt8"], A.mult, r=named("lt8"), w=["c_s1"])

    def eq(out, row, rk, a, s2, w, n):
        ts(out, row, C.get(a, a), A.is_equal, C.get(s2, s2), None if s2 is None else A.mult, r=[rk] + named(a, s2), w=[w], n=n)

    def scaled(out, a, ak, s, w, n):
        ac(out, a, [ak] + named(s), [w], n, scale=C.get(s, s))
    eq(T.r3[:], T.ro[:, 0:16], "ro", "r3", None, "r3", 16)
    eq(IB, R128, "ro", "p", None, "ib", 128)
    eq(PM, R128, "ro", "lp", None, "pm", 128)
    ts(T.hq[:, 4], T.ro[:], -4.0, A.add, C["k"], A.is_equal, r=["ro", "c_k"], w=["hq4"], n=144)
    eq(T.hq[:, 5], T.ro[:], "ro", "k8", "mid", "hq5", 144)
    eq(T.zz[:, 0], T.ro[:], "ro", "aq", 4096.0, "z4q", 144)
    eq(T.zz[:, 1], T.ro[:], "ro", "a", None, "z1", 144)
    cp(T.zh[:], T.zz[:, 1], ["z1"], ["zh"], 72)
    eq(T.w1[:, 0:16], T.ro[:, 0:16], "ro", "r", None, "w1", 16)
    ac(T.w3[:], R128, ["ro", "c_r10"], ["w3"], 128, bias=C["r10"], f=AF.Abs, scale=-1.0)
    ts(T.w3[:], T.w3[:], 5.5, A.is_lt, r=["w3"], w=["w3"])
    for h_, a in enumerate(("nh16", "h16")):
        scaled(PF[h_], PM, "pm", a, "pf%d" % h_, 128)
        ts(PH[h_], PM, C[a], A.mult, -1.0, A.mult, r=["pm", "c_" + a], w=["ph%d" % h_])
    for out, s, w in ((IF, 1.0, "if"), (NI, -1.0, "ni"), (DH[0], "nh", "dh0"), (DH[1], "h", "dh1")):
        scaled(out, IB, "ib", s, w, 128)
    cp(IH, IB, ["ib"], ["ih"])
    scaled(T.zf[:], T.zz[:, 1], "z1", 1.0, "zf", 144)
    tt(ZD, Z1(3), Z1(7), A.subtract, ["z1"], ["zd"], 128)
    mm(PS[4][:, 0:128], PM, IB, True, True, ["pm", "ib"], ["ps4"], 128)
    ac(PMT, PS[4][:, 0:128], ["ps4"], ["pmt"], 128)
    ts(NPT, PMT, -1.0, A.mult, r=["pmt"], w=["npt"])
    tt(T.hq[:, 6], T.hq[:, 4], T.hq[:, 5], A.add, ["hq4", "hq5"], ["hq6"], 144)
    for q in range(4):
        ts(T.mb[:, 1 + q], T.ii[:, 0:128], 11.0, A.is_equal, T.mb[:, 0, q:q + 1], A.mult, r=["ii", "ib"], w=["s8%d" % q])
        ac(T.hq[:, q], T.hq[:, 6], ["hq6", "r3"], ["hq%d" % q], 144, scale=T.r3[:, q:q + 1])
    ts(T.mb[:, 5], T.ii[:, 0:128], 15.0, A.is_equal, T.mb[:, 0, 0:1], A.mult, r=["ii", "ib"], w=["s11"])
    ac(colf("m3"), T.r3[:, 3:4], ["r3"], ["c_m3"], 1, bias=1.0, scale=-1.0)
    ts(colf("s0"), T.r3[:, 3:4], -9.0, A.mult, 3.0, A.add, r=["r3"], w=["c_s0"])
    ac(colf("s2"), T.r3[:, 0:1], ["r3", "c_s0"], ["c_s2"], 1, bias=C["s0"], scale=-2.0)
    ac(colf("s3"), C["s2"], ["c_s2", "c_ge8", "c_s1"], ["c_s3"], 1, bias=C["s1"], scale=C["ge8"])
    eq(T.mb[:, 11], T.rx[:, 0], "rx0", "p", "lt8", "m11", 128)
    eq(T.mb[:, 12], T.rx[:, 1], "rx1", "p", "ge8", "m12", 128)
    eq(T.mb[:, 13], T.rx[:, 2], "rx2", "p", "m3", "m13", 128)
    eq(T.st[:], T.ro[:, 0:16], "ro", "s3", None, "st", 16)
    eq(T.lt[:], T.ro[:, 1:17], "ro", "s3", None, "lt", 16)
    for name, a, b in (("f2", 11, 15), ("a04", 0, 4), ("a37", 3, 7)):
        ac(colf(name), T.w1[:, a:a + 1], ["w1"], ["c_" + name], 1, bias=T.w1[:, b:b + 1])
    ac(colf("n37"), C["a37"], ["c_a37"], ["c_n37"], 1, bias=1.0, scale=-1.0)
    eq(BOF, T.rx[:, 3], "rx3", "g16", "f2", "bof", 128)
    for k, s, w in ((2, "a04", "za"), (3, "rm8", "zq"), (4, "a37", "z37"), (5, "wl", "zl")):
        scaled(T.zz[:, k], T.zz[:, 1], "z1", s, w, 144)
    eq(SELY, T.ro[:, 0:32], "ro", "y", "lt8", "sely", 32)
    scaled(IKP, IB, "ib", "n37", "ikp", 128)
    ts(T.dia[:], T.ii[:], C["r"], A.is_equal, r=["ii", "cf"], w=["dia"], n=128)
    ts(T.tri[:, 128:384], T.ii[:], C["rq_"], A.is_le, 8192.0, A.mult, r=["ii", "c_rq_"], w=["tri"], n=128)
    ac(T.kp[:], T.ii[:], ["ii"], ["kp"], bias=0.0, f=AF.Sign)
    ac(T.kq[:, 0:KW], T.j32[:, 0:KW], ["j32"], ["kq"], KW, bias=0.0, f=AF.Sign)
    ts(T.bq[:, 0:KW], T.j32[:, 0:KW], C["h16"], A.is_equal, 1.0e6, A.mult, r=["j32", "c_h16"], w=["bq"], n=KW // 2)
    ts(T.eo[:, 0:8], T.ro[:, 0:8], 64.0, A.mult, 31.0, A.add, r=["ro"], w=["eo0"])
    ts(T.eo[:, 8:24], T.ro[:, 0:16], 32.0, A.mult, 31.0, A.add, r=["ro"], w=["eo1"])
    ac(B["pb"], T.ro[:, 0:16], ["ro", "c_rm1"], ["pb"], 16, bias=C["rm1"], scale=256.0)
    ac(B["cb"], T.ro[:, 0:16], ["ro"], ["cb"], 16, bias=128.0)
    cp(T.bc[:], T.ro[:, 0:16], ["ro"], ["bc"])
    cp(T.du[:], T.c0s[:], ["c0s"], ["du0", "du1"])
    cp(B["th"], T.ths[:], ["ths"], ["th"])
    ac(B["t17"], B["th"], ["th"], ["t17"], 16, bias=-65536.0, f=AF.Relu, scale=4096.0)
    cp(S["df"], T.c0s[:], ["c0s"], ["df0", "df1"])
    ac(T.idh[:, 0:176:11], S["df"], ["df0", "df1"], ["id_0"], 16)
    ms(T.xd[:], 0.0, ["xdz"] + [x for k in range(8) for x in staged("xd%d" % k, 0, 16, XDS)], 4096)
    ms(JU, 0, ["ju"])
    for out, n, c, w in ((B["jj"], 16, 0.0, "jj"), (T.inh[:, 0:176:11], 16, 4096.0, "in_0"), (T.tab[:, 0:1], 1, 0.0, "tabz"),
                         (T.tab[:, 2049:TW], TW - 2049, 0.0, "taby"), (T.xb1[:, 128:144], 16, 0.0, "dfxb1"), (T.y3[:, 0:1], 1, 0.0, "y3z"),
                         (T.y3[:, 2049:TW], TW - 2049, 0.0, "y3y"), (T.w1[:, 16:176], 160, 0.0, "w1z"), (T.tri[:, 0:128], 128, 0.0, "triz")):
        ac(out, T.ii[:, 0:n], ["ii"], [w], n, bias=c, scale=0.0)
    to_all(T.hws[:], lambda s: T.hwa[:, 2 * rank:2 * rank + 2], "hwarr", ["hws"], "hwa", 3000, 10000)

    mm(PS[4][:, 0:16], PMT, B["th"], True, True, ["pmt", "th"], ["ps4"])
    ac(T.thq[:], PS[4][:, 0:16], ["ps4"], ["thq"], 16)
    tt(T.t0[:], T.thq[:].indirect(T.bc[:]), T.ii[:], A.add, ["thq", "bc", "ii"], ["t0"], 256, GA)
    ac(T.t0[:], T.t0[:], ["t0"], ["t0"], bias=15.5, f=AF.Sign, scale=-1.0)
    ac(T.t1[:], T.ii[:], ["ii"], ["t1"], bias=-7.5 / 65536, scale=1.0 / 65536)
    for h_ in range(2):
        o, k = PS[h_][:, 0:256], ["ps%d" % h_]
        mm(o, DH[h_], T.t1[:], True, False, ["dh%d" % h_, "t1"], k, 256)
        mm(o, DH[1 - h_], T.t0[:], False, True, ["dh%d" % (1 - h_), "t0"], k, 256)
        ac(T.kin[:, h_:32:2, :], o, k, ["kin%d" % h_], scale=4096.0)

    for h_ in range(2):
        cp(T.pw2[:, 2048 * h_:2048 * h_ + 2048:2], T.pws[:, 1024 * h_:1024 * h_ + 1024], ["pws"], ["pw2a%d" % h_], 512)
        ts(T.pw2[:, 2048 * h_ + 1:2048 * h_ + 2048:2], T.pws[:, 1024 * h_:1024 * h_ + 1024], -1.0, A.mult, r=["pws"], w=["pw2b%d" % h_], n=512)
    PW2 = ["pw2a0", "pw2a1", "pw2b0", "pw2b1"]
    cp(T.oth[:], T.otq[:], ["otq"], ["oth"], 512)
    tt(T.otl[:], T.otq[:], T.oth[:], A.subtract, ["otq", "oth"], ["otl"], 1024)
    for q in range(4):
        b = (5, 2)[q % 2]
        k = ["ps%d" % b]
        mm(PS[b][:], T.mb[:, 1 + q], T.fh[:], True, False, ["s8%d" % q, "fh"], k, 512)
        mm(PS[b][:], T.mb[:, 5], T.fl[:], False, False, ["s11", "fl"], k, 512)
        mm(PS[b][:], T.hq[:, q, 4:132], T.oth[:], False, False, ["hq%d" % q, "oth"], k, 512)
        mm(PS[b][:], T.hq[:, q, 0:128], T.otl[:], False, True, ["hq%d" % q, "otl"], k, 512)
        if q % 2:
            ac(T.tab[:, 512 * q + 1:512 * q + 513], PS[b][:], k, ["tab%d" % q], 512)
        else:
            cp(T.tab[:, 512 * q + 1:512 * q + 513], PS[b][:], k, ["tab%d" % q], 512)
    for k, (a, ak) in enumerate(((T.mb[:, 11], "m11"), (T.mb[:, 12], "m12"), (NI, "ni"))):
        mm(PS[5][:, 0:128], a, T.mb[:, 13], k == 0, False, [ak, "m13"], ["ps5"], 128)
        mm(PS[5][:, 0:128], a, IB, False, k == 2, [ak, "ib"], ["ps5"], 128)
    ac(BM, PS[5][:, 0:128], ["ps5"], ["bm"], 128)
    TAB = ["tab%d" % q for q in range(4)] + ["tabz", "taby"]

    def expand(name, key, npool, lo, hi):
        n = 16 * (hi - lo)
        for k in range(8):
            odd, w = k % 2, "xd%d_%d" % (k, lo)
            ps_ = slice(0, 16 * k + 16) if k < npool else slice(16 * (k - odd), 16 * k + 16)
            o, a = T.xd[ps_, 256 * lo + 8 + k:256 * hi:16], T[name][ps_, 16 * lo:16 * hi]
            if k < npool:
                op("pool", lambda o=o, a=a, k=k: g.affine_select(o, a, [[0, n]], A.is_ge, 0.0, -16 * k, 1), [key], [w, "chp"], 170 + 2 * n * CY)
            elif odd:
                ac(o, a, [key, "cf"], [w], n, scale=T.cf[ps_, CK["h"]:CK["h"] + 1])
            else:
                ac(o, a, [key], [w], n)

    def next_x(n, bank):
        a, b = T.xt[:, 256 * (n - 1):256 * n], T.xt[:, 256 * n:256 * n + 256]
        o, k = PS[bank][:, 0:256], ["ps%d" % bank]
        mm(o, IB, a, True, False, ["ib", "x%d" % (n - 1)], k, 256)
        mm(o, IB, T.stp[:], False, True, ["ib", "stp"], k, 256)
        ac(T.xa[:], o, k, ["xa"], bias=3064.5)
        mm(o, IB, a, True, False, ["ib", "x%d" % (n - 1)], k, 256)
        mm(o, IB, T.stp[:], False, False, ["ib", "stp"], k, 256)
        mm(o, NI, T.xa[:], False, True, ["ni", "xa"], k, 256)
        ac(b, o, k, ["x%d" % n], bias=3072.0)

    def place(out, n, lo, hi, w):
        ac(out[:, 16 * lo:16 * hi], T.xt[:, 0:256 * n + 256].indirect(T.nj[:, 16 + lo:16 + hi]), ["x%d" % k for k in range(n + 1)] + ["nu_%d" % lo],
           ["%s_%d" % (w, lo)], 16 * (hi - lo), GA)

    def scatters(win, src, rk, wk, lo=0, hi=16, per=2):
        for c in range(hi - per, lo - 1, -per):
            off = T.ou[:, c:c + 2] if per == 2 else T.ou[:, 16 + 2 * c:17 + 2 * c]
            cp(win[:].indirect(off), src[:, 16 * c:16 * (c + per)], staged("ou0", lo, hi) + staged("ou1", lo, hi) + rk(c), wk, 16 * per, SC)

    def rivals(t):
        k = ["ps5"]
        bad = [] if t is None else ["nc", "t17"] + (["e5"] if t >= 5 else [])
        p0 = 0 if t is None else min([8] + [s[0] // 2 for s in STAGES if s[2] == 2])
        parts = [(PS[5][:, 384 + p0:392], slice(2 * p0, 16, 2))] * (p0 < 8) + [(PS[5][:, 392:408], slice(0, 16))]
        calls = [(o, IB, T.sb[:, BK[n_], cs]) for o, cs in parts for n_ in bad]
        if bad:
            mms([c + (j == 0, False) for j, c in enumerate(calls)], ["ib"] + bad, k)
        mms([(o, IF, T.fr[:, cs], j == 0 and not bad, j == len(parts) - 1) for j, (o, cs) in enumerate(parts)], ["if", "fr"], k, 256)
        ts(T.fs[:, p0:24], PS[5][:, 384 + p0:408], 4000.0, A.min, r=k, w=["fs"])
        mm(PS[5][:, 16 * p0:384], IB, T.tri[:, 16 * p0:384], True, False, ["ib", "tri", "triz"], k, 384 - 16 * p0)
        mms([(PS[5][:, 16 * p0 + r_:384:16], NPT, T.fs[:, p0:24], False, False) for r_ in range(16)], ["npt", "fs"], k)
        mm(PS[5][:, 128:384], BOF, T.col[:], False, p0 == 8, ["bof", "col"], k, 256)
        if p0 < 8:
            mms([(PS[5][:, 16 * c:16 * c + 16], BOF, T.col[:, 32 * c + 16:32 * c + 32], False, c == 7) for c in range(p0, 8)], ["bof", "col"], k)
        ac(T.thr[:, 16 * p0:384], PS[5][:, 16 * p0:384], k, ["thr"], 384 - 16 * p0, bias=-64.0, f=AF.Abs, scale=64.0)

    def lowest(tk, flag, fk, lo=0, hi=16, per=2):
        n, win, o = hi - lo, T.tot[:, 32 * lo:32 * hi], PS[2][:, lo:hi]
        mm(o, IH, T.fs[:, 8 + lo:8 + hi], True, False, ["ih", "fs"], ["ps2"])
        if per == 2:
            cs, k = slice(8 * lo, 8 * hi), staged("ee0", lo, hi)
            tt(T.ee[:, cs], win.indirect(T.eo[:, 0:n // 2]), T.thr[:, cs], A.is_ge, tk + ["eo0", "thr"], k, 8 * n, GA)
            to_l(2, PS[2][:, lo + 1:hi:2], Z4Q, T.ee, False, ["z4q"] + k, 8 * lo, 8 * hi, False)
        cs, k = slice(128 + 16 * lo, 128 + 16 * hi), staged("ee1", lo, hi)
        tt(T.ee[:, cs], win.indirect(T.eo[:, 8:8 + n]), T.thr[:, cs], A.is_ge, tk + ["eo1", "thr"], k, 16 * n, GA)
        mm(o, NI, flag, False, False, ["ni"] + fk, ["ps2"])
        to_l(2, o, Z4Q, T.ee, False, ["z4q"] + k, 128 + 16 * lo, 128 + 16 * hi)
        if per == 1:
            ts(T.ou[:, 16 + 2 * lo:16 + 2 * hi:2], o, 4097.0, A.add, C["dum"], A.min, r=["ps2", "c_dum"], w=staged("ou0", lo, hi))
            return
        for h_, n_ in enumerate(("dum", "dum16")):
            ts(T.ou[:, lo + h_:hi:2], PS[2][:, lo + h_:hi:2], 4097.0, A.add, C[n_], A.min, r=["ps2", "c_" + n_], w=staged("ou%d" % h_, lo, hi))

    def columns():
        ac(T.col[:], T.tab[:].indirect(T.fz[:]), TAB + ["fz"], ["col"], k=GA)

    def swapped(t):
        if t == 5:
            tt(T.lg[:], T.st[:].indirect(JU), T.col[:], A.mult, ["st", "ju", "col"], ["lg0", "lg1"], 256, GA)
        mm(PS[4][:, 0:256], IB, T.col[:], True, False, ["ib", "col"], ["ps4"], 256)
        mm(PS[4][:, 0:256], BM, T.lg[:], False, True, ["bm", "lg0", "lg1"], ["ps4"], 256)
        if t == 5 or LATER[1] is None:
            ac(T.ncl[:], PS[4][:, 0:256], ["ps4"], ["ncl"])
        else:
            later.append((LATER[1], lambda w: ac(T.ncl[:], PS[4][:, 0:256], ["ps4"], ["ncl"] + w)))

    def row_mask(t):
        ac(T.lm[:, 256 * (t % 2):256 * (t % 2) + 256], T.lt[:].indirect(JU), ["lt", "ju"], ["lm%d" % (t % 2)], k=GA)

    def statics(t):
        pj = PS[7][:, 0:16]
        ac(B["jj"], pj, ["ps7"], ["jj"], 16, bias=16.0, f=AF.Relu)
        if t >= 2:
            ac(B["nc"], pj, ["ps7"], ["nc"], 16, bias=4096.0, f=AF.Relu, scale=-256.0)
        if t >= 5:
            ac(B["e5"], pj, ["ps7"], ["e5"], 16, bias=-12288.0, f=AF.Relu, scale=256.0)
        if t < NSUB - 1:
            row_mask(t)

    def request(e, part):
        rq = T["req%d" % e]
        own = rq[:, 112:128]
        if part == 0:
            ts(SI["fi"], T.fz[:], -1.0, A.add, r=["fz"], w=["fi"])
            ts(SI["q"], SI["fi"], 7, A.bitwise_and, r=["fi"], w=["q"])
            ts(B["qb"], SI["q"], 256.0, A.mult, r=["q"], w=["qb"])
            for h_ in range(2):
                ts(T.qo[:, 16 * h_:16 * h_ + 16], SI["q"], 2.0, A.mult, float(h_), A.add, r=["q"], w=["qo%d" % h_])
            return
        if part < 3:
            h_ = part - 1
            tt(T.uu[:, 256 * h_:256 * h_ + 256], T.hwa[:].indirect(T.qo[:, 16 * h_:16 * h_ + 16]), T.xc[:], A.mult,
               ["hwa", "hwown", "qo%d" % h_] + staged("xc", 0, 16, MOVES), ["uu%d" % h_], 256, GA)
            return
        to_l(3, PS[3][:, 0:32], Z1, T.uu, True, ["z1", "uu0", "uu1"])
        cp(S["ub"], PS[3][:, 16:32], ["ps3"], ["ub"])
        tt(SI["pr"], PS[3][:, 0:16], S["ub"], A.mult, ["ps3", "ub"], ["pr"])
        ts(SI["h"], SI["pr"], 5, A.arith_shift_right, 2047, A.bitwise_and, r=["pr"], w=["h"])
        ts(own, SI["h"], 1.0, A.add, r=["h"], w=["rqown%d" % e])
        to_all(own, lambda s: rq[:, 16 * slots(T, topo, s).index(rank):16 * slots(T, topo, s).index(rank) + 16], "rq%d" % e,
               ["rqown%d" % e], "rqarr%d" % e, 600, ASK)

    def codes():
        for k, (a, b) in enumerate(CODES):
            cp(T.cod[:, 16 * a:16 * b], T.sfs[:].indirect(T.du[:, a:b]), ["sfs", "du%d" % k], ["cod%d" % k], 16 * (b - a), GA)

    def coded(a, b):
        return ["cod%d" % j for j, (c0, c1) in enumerate(CODES) if c0 < b and a < c1]

    def keys(lo, hi, bank):
        k = ["ps%d" % bank]
        mm(PS[bank][:, 0:32 * (hi - lo)], IB, T.kin[:, 2 * lo:2 * hi, :], True, False, ["ib", "kin0", "kin1"], k, max(64, 32 * (hi - lo)))
        for eng, a, b in OTHER.get(step["t"], GATHERS):
            if lo <= a < hi:
                for x in [x for x in later if x[0] == a]:
                    later.remove(x)
                    x[1](["chact"])
                o, src = T.gg[:, 256 * a:256 * b], T.pw2[:].indirect(T.cod[:, 16 * a:16 * b])
                (ac if eng == "act" else cp)(o, src, PW2 + coded(a, b), ["gg%d" % c for c in range(a, b)] + ["ch" + eng], 256 * (b - a), GA)
                for c in range(a, b):
                    calls = []
                    for r2 in range(8):
                        p_, q, u = 16 * c + 2 * r2, r2 // 2, r2 % 2
                        s0, c0 = 8 * (2 * p_ + 1 - u), 32 * (c - lo)
                        calls.append((PS[bank][32 * q:32 * q + 32, c0:c0 + 32], T.xd[:, s0:s0 + 32], T.gg[:, 16 * p_:16 * p_ + 32], False, False))
                    mms(calls, [x for j in range(8) for x in staged("xd%d" % j, c, c + 1, XDS)] + ["gg%d" % c], k, 32)
        mm(PS[bank][:, 0:8], IB, T.xd[:, 0:8], False, True, ["ib", "xdz"], k)

    def test(t, lo, hi, bank, eng):
        n, cs, k, me = 32 * (hi - lo), slice(32 * lo, 32 * hi), "ps%d" % bank, "_%d" % lo
        keys(lo, hi, bank)
        if (eng == "act") != (t in SWAP):
            ac(T.ind[:, cs], PS[bank][:, 0:n], [k], ["ind" + me], n, bias=0.5, f=AF.Sign)
        else:
            ts(T.ind[:, cs], PS[bank][:, 0:n], -0.5, A.is_ge, -0.5, A.add, r=[k], w=["ind" + me], n=n)
        scan(T.tot[:, cs], T.kq[:, 0:n], T.ind[:, cs], A.mult, A.add, ["kq", "ind" + me], ["tot" + me], n, CY / 2)
        if t < NSUB - 1:
            scan(T.mns[:, cs], T.bq[:, 0:n], PS[bank][:, 0:n], A.add, A.min, ["bq", k], ["mns" + me], n)

    def moved(t, lo, hi):
        k7, o, all_, ak = ["ps7"], PS[7][:, 16 + lo:16 + hi], T.inh[:, t + 1:176:11], staged("in%d" % (t + 1))
        mm(o, IB, T.sb[:, BK["pb"], lo:hi], True, False, ["ib", "pb"], k7)
        if t:
            mms([(o, IB, T.inh[:, 11 * lo + n_:11 * hi:11], False, False) for n_ in range(1, t + 1)],
                ["ib"] + [x for n_ in range(1, t + 1) for x in staged("in%d" % n_, lo, hi)], k7)
        if lo == 0:
            mm(PS[7][:, 0:16], IB, B["jj"], False, False, ["ib", "jj"], k7)
            mm(PS[7][:, 48:64], IF, S["df"], False, False, ["if", "df0", "df1"], k7, 256)
            if t % 5 == 4:
                mms([(PS[7][:, 32:48], IB, B[n_], False, False) for n_ in ("jj", "qb")], ["ib", "jj", "qb"], k7)
                mm(PS[7][:, 32:48], NI, all_, False, False, ["ni"] + ak, k7)
            mm(PS[7][:, 48:64], IB, all_, False, False, ["ib"] + ak, k7)
            mm(PS[7][:, 0:16], NI, all_, False, False, ["ni"] + ak, k7)
        mm(o, IB, T.inh[:, 11 * lo + t + 1:11 * hi:11], False, True, ["ib"] + staged("in%d" % (t + 1), lo, hi), k7)
        first = 16 + lo if lo else 0
        cs = slice(first, 48 if t % 5 == 4 else 16 + hi)
        ts(T.nj[:, cs], PS[7][:, cs], 1.0 / 16, A.mult, 1.0, A.add, r=k7, w=["nu_%d" % lo, "ju", "wu"])
        if t == NSUB - 1:
            place(T.yxs, t + 1, lo, hi, "yxs")
        else:
            place(T.xc, t + 1, lo, hi, "xc")
            for k, (a, b) in enumerate(XDS):
                expand("xc", "xc_%d" % lo, NPOOL[k], a, b)

    def stage(t, lo, hi, per):
        last, all_, ak = t == NSUB - 1, T.inh[:, t + 1:176:11], staged("in%d" % (t + 1))
        ins, ik, tk = T.inh[:, 11 * lo + t + 1:11 * hi:11], "in%d_%d" % (t + 1, lo), staged("tot", lo, hi, BANKS)
        for b in BANKS:
            if lo <= b[0] < hi:
                test(t, *b)
        o = PS[3][:, lo:hi]
        mm(o, NI, T.sb[:, BK["t17"], lo:hi], True, False, ["ni", "t17"], ["ps3"])
        if t >= 5:
            mm(o, NI, T.sb[:, BK["e5"], lo:hi], False, False, ["ni", "e5"], ["ps3"])
        mm(o, PM, T.tot[:, 32 * lo + 31:32 * hi:32], False, True, ["pm"] + tk, ["ps3"])
        ts(ins, o, 0.0, A.is_ge, 4096.0, A.mult, r=["ps3"], w=[ik])
        for a, b in MOVES:
            if a == lo:
                moved(t, a, b)
        if lo == 0 and not last:
            MNS, o = staged("mns", 0, 16, BANKS), PS[4][:, 0:16]
            ts(T.mv[:], T.mns[:, 15:512:16], ROUND, A.add, -ROUND, A.add, r=MNS, w=["mv"])
            mm(o, IB, B["jj"], True, False, ["ib", "jj"], ["ps4"])
            if FRAC:
                tt(T.mw[:], T.mv[:], T.mns[:, 15:512:16], A.subtract, MNS + ["mv"], ["mw"], 64)
            for h_ in range(2 * (1 - FRAC)):
                mm(o, PF[h_], T.mns[:, 15 + 16 * h_:512:32], False, False, ["pf%d" % h_] + MNS, ["ps4"], 256)
            for h_ in range(2):
                mm(o, PH[h_], (T.mw if FRAC else T.mv)[:, h_:32:2], False, h_ == 1, ["ph%d" % h_, "mw" if FRAC else "mv"], ["ps4"])
            ts(T.iu[:], o, 7.5, A.add, r=["ps4"], w=["iu"])
            if t < SRT:
                ts(T.sr[:], T.cod[:], 0.5, A.mult, -0.25, A.add, r=coded(0, 16), w=["sr"], n=256)
                for a, b in SGS if t >= 2 else ((0, 16),):
                    tt(T.sg[:, 16 * a:16 * b], T.w1[:].indirect(T.iu[:, a:b]), T.sr[:, 16 * a:16 * b], A.mult, ["w1", "w1z", "iu", "sr"],
                       ["sg%d" % x for x, y in SGS if a <= x < b], 16 * (b - a), GA)
            else:
                ac(T.sh[:], T.w1[:].indirect(T.iu[:]), ["w1", "w1z", "iu"], ["sh"], k=GA, scale=HALF)
                for a, b in SGS:
                    tt(T.sg[:, 16 * a:16 * b], T.sfs[:].indirect(T.du[:, a:b]), T.sh[:, 16 * a:16 * b], A.mult, ["sfs", "du0", "du1", "sh"], ["sg%d" % a], 16 * (b - a), GA)
            o = PS[6][:, 0:16]
            if t > 0:
                mm(o, IF, T.fr[:], True, False, ["if", "fr"], ["ps6"], 256)
            mm(o, NI, all_, t == 0, False, ["ni"] + ak, ["ps6"])
            to_l(6, o, ZH, T.sg, False, ["zh"] + ["sg%d" % a for a, b in SGS])
            ts(T.fz[:], o, 0.75, A.add, r=["ps6"], w=["fz"])
        if t >= 2:
            lowest(tk, ins, [ik], lo, hi, per)
            scatters(T.tab, T.ncl, lambda c: ["ncl"], TAB, lo, hi, per)

    for s in XDS:
        expand("xt", "x0", 4, s[0], s[1])
    row_mask(0)
    codes()
    next_x(1, 6)
    for t in range(NSUB):
        last, ex, e = t == NSUB - 1, t % 5 == 4, t // 5
        step.clear()
        step["t"] = t
        for part in range(4):
            if ASKS[part] == t % 5:
                request(e, part)
        if t >= 2:
            swapped(t)
        k7 = ["ps7"]
        for s in STAGES:
            stage(t, *s)
        idd, idk = T.idh[:, t + 1:176:11], "id_%d" % (t + 1)
        ac(idd, PS[7][:, 48:64], k7, [idk], 16, bias=-4096.0, f=AF.Relu)
        if ex:
            rivals(None)
            ac(B["jj"], PS[7][:, 0:16], k7, ["jj"], 16, bias=16.0, f=AF.Relu)
        else:
            statics(t + 1)
        if last:
            dma("sync", T.yx[:], T.yxs[:], "o_yx", staged("yxs", 0, 16, MOVES), ["yx"], 2500)
        else:
            ac(T.fr[:], PS[6][:, 0:16], ["ps6"], ["fr"], 16, bias=0.0, f=AF.Relu)
        if ex:
            xb, rq = T["xb%d" % e], T["req%d" % e]
            rk = TAB + ["rqarr%d" % e, "rqown%d" % e]
            for hf in range(2):
                cp(T.hg[:, 1024 * hf:1024 * hf + 512], T.tab[:].indirect(rq[:, 64 * hf:64 * hf + 32]), rk, ["hga%d" % hf], 512, GA)
                ac(T.hg[:, 1024 * hf + 512:1024 * hf + 1024], T.tab[:].indirect(rq[:, 64 * hf + 32:64 * hf + 64]), rk, ["hgb%d" % hf], 512, GA)
            sends = []
            for hf in range(2):
                to_l(hf, PS[hf][:, 0:64], ZA, T.hg, True, ["za", "hga%d" % hf, "hgb%d" % hf], 1024 * hf, 1024 * hf + 1024)
                n = 16 * len(halves(rank)[hf])
                cp(xb[:, 144 + 64 * hf:144 + 64 * hf + n], PS[hf][:, 0:n], ["ps%d" % hf], ["ans%d%d" % (e, hf)], n)
                en = answer_engines(rank, hf)
                trs = []
                for s in halves(rank)[hf]:
                    k = 144 + 16 * myslots.index(s)
                    trs.append(RemoteDMATransfer(dst_ids=[dst(s)], dma_engine_mask=bits(en[T.cores[s]]), remote_sem=T.sem["an%d" % e],
                                                 src=xb[:, k:k + 16], dst=xb[:, 16 * rank:16 * rank + 16]))
                    sent[0] += len(en[T.cores[s]])
                sends.append(op("pool", lambda trs=trs: g.remote_dma_fused(trs, local_sem=T.sem.sent), ["ans%d%d" % (e, hf)], (), 600))
            ac(xb[:, 16 * rank:16 * rank + 16], PS[1][:, 48:64], ["ps1"], ["ownxb%d" % e], 16)
            lastw["anarr%d" % e] = ("an%d" % e, ans_in, sends, ANSWER)
        if not last:
            next_x(t + 2, XB)
            for k, (a, b) in enumerate(CODES if LGS and not ex else ((0, 16),)):
                bank, lk = (3, 4)[k], ["lg%d" % k] if LGS and not ex else ["lg0", "lg1"]
                o, c2 = PS[bank][:, a:b], slice(16 * a, 16 * b)
                tt(T.lg[:, c2], T.tab[:].indirect(T.fz[:, a:b]), T.lm[:, 256 * (t % 2) + 16 * a:256 * (t % 2) + 16 * b], A.mult,
                   TAB + ["fz", "lm%d" % (t % 2)], lk, 16 * (b - a), GA)
                mm(o, IF, T.idh[:, 11 * a + t + 1:11 * b:11], True, False, ["if", idk], ["ps%d" % bank], 256)
                to_l(bank, o, ZL, T.lg, False, ["zl"] + lk, 16 * a, 16 * b)
                if not ex:
                    cp(T.du[:, a:b], o, ["ps%d" % bank], ["du%d" % k] if LGS else ["du0", "du1"])
                    ac(T.sm[:, 0, a:b], o, ["ps%d" % bank], ["df%d" % k] if LGS else ["df0", "df1"], 16)
        if not ex:
            codes()
            if t >= 1:
                columns()
                rivals(t + 1)
            continue
        if not last:
            ac(xb[:, 128:144], PS[3][:, 0:16], ["ps3"], ["dfxb0"], 16)
            columns()
        ac(T.oh[:], T.w3[:].indirect(T.nj[:, 32:48]), ["w3", "wu"], ["oh"], k=GA)
        ac(T.le[:], T.oh[:], ["oh"], ["le"], scale=16.5)
        scan(T.cum[:], T.oh[:], T.oh[:], A.add, A.max, ["oh"], ["cum"], 256, CY / 2, 0.5)
        tt(T.svr[:], T.le[:], T.cum[:], A.is_ge, ["le", "cum"], ["svr"], 256)
        mm(PS[2][:, 0:16], IB, B["cb"], True, False, ["ib", "cb"], ["ps2"])
        to_l(2, PS[2][:, 0:16], ZQ, T.svr, False, ["zq", "svr"])
        ts(B["sv"], PS[2][:, 0:16], 128.0, A.is_lt, 4096.0, A.mult, r=["ps2"], w=["sv"])
        cp(T.pu[:], PS[2][:, 0:16], ["ps2"], ["pu"])
        mm(PS[5][:, 0:16], PMT, B["sv"], True, True, ["pmt", "sv"], ["ps5"])
        ac(T.tot[:, 31:512:32], PS[5][:, 0:16], ["ps5"], staged("tot", 0, 16, BANKS), 16, bias=-0.5, scale=1.0 / 4096)
        lowest(staged("tot", 0, 16, BANKS), B["sv"], ["sv"])
        if not last:
            mm(PS[7][:, 0:16], IB, B["jj"], True, False, ["ib", "jj"], k7)
            ac(B["th"], B["sv"], ["sv"], ["th"], 16, bias=16.0, scale=1.0 / 256)
            mm(PS[7][:, 0:16], NI, B["th"], False, True, ["ni", "th"], k7)
            ts(JU, PS[7][:, 0:16], 1.0 / 16, A.mult, 1.0, A.add, r=k7, w=["ju"])
            statics(t + 1)
        tt(T.ag[:], xb[:, 0:144].indirect(T.pu[:]), T.dia[:], A.mult,
           ["anarr%d" % e, "ownxb%d" % e, "dfxb%d" % e, "pu", "dia"], ["ag"], 256, GA)
        if not last:
            scan(T.asc[:], T.kp[:], T.ag[:], A.mult, A.add, ["kp", "ag"], ["asc"])
            an = T.asc[:, 15:256:16]
            cp(T.du[:], an, ["asc"], ["du0", "du1"])
            codes()
            ac(S["df"], an, ["asc"], ["df0", "df1"], 16)
            ac(T.dg[:, 0:256], T.ag[:], ["ag"], ["dg0"])
            mm(PS[4][:, 0:256], IKP, T.col[:], True, False, ["ikp", "col"], ["ps4"], 256)
            mm(PS[4][:, 0:256], T.zf[:, 8:136], T.ag[:], False, False, ["zf", "ag"], ["ps4"], 1024)
            mm(PS[4][:, 0:256], ZD, T.dg[:, 0:256], False, True, ["zd", "dg0"], ["ps4"], 256)
            ac(T.ncl[:], PS[4][:, 0:256], ["ps4"], ["ncl"])
            scatters(T.tab, T.ncl, lambda c: ["ncl"], TAB)
            columns()
            rivals(t + 1)
            continue
        ac(T.nih[:], T.inh[:], ["in_0"] + [x for k in range(1, 11) for x in staged("in%d" % k)], ["nih"], 176, bias=1.0, scale=-1.0 / 4096)
        scan(T.csc[:], T.nih[:], T.idh[:], A.mult, A.add, ["nih"] + ["id_%d" % k for k in range(11)], ["csc"], 176)
        cp(S["yc"], T.csc[:, 10:176:11], ["csc"], ["ycs"])
        dma("sync", T.yc[:], S["yc"], "o_yc", ["ycs"], ["yc"], 2500)
        for q in range(4):
            cs, ct = slice(512 * q, 512 * q + 512), slice(512 * q + 1, 512 * q + 513)
            b3, ba = (3, 7)[q % 2], (0, 1)[q % 2]
            mm(PS[ba][0:32, :], SELY, T.tab[:, ct], True, True, ["sely"] + TAB, ["ps%d" % ba], 512)
            mm(PS[b3][:], Z37(0), T.tab[:, ct], True, True, ["z37"] + TAB, ["ps%d" % b3], 512)
            ac(T.y3[:, ct], PS[b3][:], ["ps%d" % b3], ["y3%d" % q], 512)
            if q % 2:
                ac(T.ya[0:32, cs], PS[ba][0:32, :], ["ps%d" % ba], ["ya%d" % q], 512)
            else:
                cp(T.ya[0:32, cs], PS[ba][0:32, :], ["ps%d" % ba], ["ya%d" % q], 512)
        dma("sync", T.yt[:], T.ya[0:32, :], "o_ya", ["ya%d" % q for q in range(4)], ["yt"], 3000)
        for hf in (1, 0):
            cs = slice(128 * hf, 128 * hf + 128)
            mm(PS[(4, 6)[hf]][:, 0:128], ZF, T.ag[:, cs], True, True, ["zf", "ag"], ["ps%d" % (4, 6)[hf]], 512)
            if hf:
                cp(T.anr[:, cs], PS[6][:, 0:128], ["ps6"], ["anr1"], 128)
            else:
                ac(T.anr[:, cs], PS[4][:, 0:128], ["ps4"], ["anr0"], 128)
        scatters(T.y3, T.anr, lambda c: ["anr%d" % (c // 8)], ["y3%d" % q for q in range(4)] + ["y3z", "y3y"])
        dma("sync", T.yt[3:32:4, :], T.y3[0:128:16, 1:2049], "o_y3", ["y3%d" % q for q in range(4)], ["yt"], 2500)

    if len(ops) not in ORDER:
        ORDER[len(ops)] = schedule(ops)
    order = ORDER[len(ops)]
    pos = {i: k for k, i in enumerate(order)}
    known, plan = {e_: {} for e_ in Q}, []
    for i in order:
        o = ops[i]
        kn = known[o["eng"]]
        need = {}
        for d in o["deps"]:
            if isinstance(d, tuple):
                need[d[0]] = d
            else:
                s = ops[d]["dma"] or ops[d]["eng"]
                if s not in need or pos[d] > pos[need[s]]:
                    need[s] = d
        waits = []
        for s, d in sorted(need.items(), key=lambda x: -place_of(x[1], pos)):
            p_ = place_of(d, pos)
            if kn.get(s, -1) < p_:
                waits.append((s, d))
                kn[s] = p_
                if not isinstance(d, tuple):
                    ops[d]["sig"] = True
                    for s2, p2 in ops[d]["clock"].items():
                        kn[s2] = max(kn.get(s2, -1), p2)
        o["clock"] = dict(kn)
        plan.append(waits)
    cnt = {}
    for i in order:
        o = ops[i]
        if o["sig"] and not o["dma"]:
            cnt[o["eng"]] = cnt.get(o["eng"], 0) + 1
            o["n"] = cnt[o["eng"]]
    for i, waits in zip(order, plan):
        o = ops[i]
        for s, d in waits:
            Q[o["eng"]].wait_ge(T.sem[s], d[1] if isinstance(d, tuple) else 16 if ops[d]["dma"] else ops[d]["n"])
        call = o["fn"]()
        if o["dma"]:
            call.then_inc(T.sem[o["dma"]], 16)
        elif o["sig"]:
            call.then_inc(T.sem[o["eng"]], 1)
    g.wait_ge(T.sem.sent, sent[0])
    for s in ("o_y3", "o_yc", "o_yx"):
        g.sync.wait_ge(T.sem[s], 16)


def place_of(d, pos):
    return 0 if isinstance(d, tuple) else pos[d]
